import numpy as np
import ml_dtypes


def mxq(x, axis, fmt="e4m3"):
    dtype, down = {"e4m3": (ml_dtypes.float8_e4m3fn, 7), "e5m2": (ml_dtypes.float8_e5m2, 14)}[fmt]
    v = np.moveaxis(np.asarray(x, np.float32).astype(ml_dtypes.bfloat16).astype(np.float64), axis, -1)
    blocks = v.reshape(v.shape[:-1] + (-1, 32))
    amax = np.abs(blocks).max(-1, keepdims=True)
    byte = np.maximum(np.where(amax > 0, np.frexp(amax)[1] - 1 + 127, 0) - down, 1)
    scale = np.exp2(byte - 127.0)
    codes = (blocks / scale).astype(np.float32).astype(dtype).astype(np.float64)
    return np.moveaxis((codes * scale).reshape(v.shape), -1, axis)


WIDE = False


def mx_kscale(k):
    if not WIDE:
        return np.ones(k)
    levels = np.array([10, -10, 5, -5, 0])
    if k % 512:
        return np.exp2(np.random.permutation(np.resize(levels, k // 32))).repeat(32)
    a = np.empty((k // 512, 16))
    for p in range(k // 512):
        a[p, :8] = np.random.permutation(np.resize(levels, 8))
        for g in range(8):
            far = levels[np.abs(levels - a[p, g]) >= 10]
            a[p, g + 8] = far[np.random.randint(len(far))]
    return np.exp2(a.ravel()).repeat(32)


def f64(x):
    return np.asarray(x).astype(np.float64)


def striped(idx):
    return np.tile(np.asarray(idx).reshape(-1, 16).T, (8, 1)).astype(np.uint16)


def unstriped(offs):
    return offs[:16].T.reshape(-1).astype(np.int64)


B, N, T, D, NQ = 1, 1024, 4096, 512, 128
SEG = 32


def setup_inputs():
    n = np.random.standard_normal
    pages = np.random.permutation(T // 32)[:B * N // 32]
    idx = (pages[:, None] * 32 + np.arange(32)[None, :]).reshape(-1)
    s = mx_kscale(D)[:, None]
    return {
        "qT": (n((B, D, NQ)) * s * (1.00 / np.sqrt(D))).astype(np.float32),
        "kT": (n((D, T)) / s).astype(np.float32),
        "kb": np.tile(n(4096), (128, 1)).astype(np.float32),
        "im": (np.random.uniform(0.5, 2.5, (B, NQ, 1))).astype(np.float32),
        "offs": striped(idx),
    }


def reference(qT, kT, kb, im, offs):
    idx = unstriped(offs)
    pick = lambda x, which: x[:, which].reshape(x.shape[0], B, -1).transpose(1, 0, 2)
    kg = mxq(pick(f64(kT), idx), 1, "e4m3")
    qq = mxq(f64(qT), 1, "e4m3")
    a = qq.transpose(0, 2, 1) @ kg
    y = np.maximum((a + pick(f64(kb), idx)[:, :1, :]).reshape(B, NQ, N // SEG, SEG).max(-1), f64(im))
    return y

@@ -1,0 +1,124 @@
+from contextlib import ExitStack
+
+import concourse.mybir as mybir
+from concourse.masks import make_identity
+
+F32 = mybir.dt.float32
+BF16 = mybir.dt.bfloat16
+U32 = mybir.dt.uint32
+U16 = mybir.dt.uint16
+U8 = mybir.dt.uint8
+FP8X4 = mybir.dt.float8_e4m3fn_x4
+ALU = mybir.AluOpType
+ACT = mybir.ActivationFunctionType
+AXES = mybir.AxisListType
+
+P = 128
+PACK = 4
+D, NQ, T, N, SEG = 512, 128, 4096, 1024, 32
+HALF = N // 2
+SEGS = HALF // SEG
+BLOCKS = HALF // P
+RUN = SEG // BLOCKS
+BANK = 512
+
+FLOPS = 2 * D * NQ * N
+BYTES = 4 * (D * NQ + D * T + T + NQ + NQ * N // SEG) + 2 * P * N // 16
+
+
+def tile_attend_xtr_f_kernel(tc, qT, kT, kb, im, offs, out):
+    nc = tc.nc
+    with ExitStack() as ctx:
+        keep = ctx.enter_context(tc.tile_pool(name="keep", bufs=1))
+        psum = ctx.enter_context(tc.psum_pool(name="psum", bufs=1))
+
+        offsets = keep.tile([P, N // 16], U16, name="offsets")
+        nc.sync.dma_start(offsets[:], offs)
+        q_raw = keep.tile([P, PACK, NQ], F32, name="q_raw")
+        nc.sync.dma_start(out=q_raw[:], in_=qT[0].rearrange("(p t) q -> p t q", t=PACK))
+        k_rows = kT.rearrange("(p t) w -> p t w", t=PACK)
+        planes = [keep.tile([P, T], F32, name="plane%d" % t) for t in range(PACK)]
+        for t in range(PACK):
+            nc.sync.dma_start(out=planes[t][:], in_=k_rows[:, t, :])
+
+        im_col = keep.tile([P, 1], F32, name="im_col")
+        nc.scalar.dma_start(out=im_col[:], in_=im[0])
+        bias_pool = keep.tile([P, T], F32, name="bias_pool")
+        nc.vector.memset(bias_pool[:], 0.0)
+        nc.scalar.dma_start(out=bias_pool[0:1, :], in_=kb[0:1, :])
+
+        ident = keep.tile([P, P], F32, name="ident")
+        make_identity(nc, ident[:])
+        banks = [psum.tile([P, BANK], F32, name="bank%d" % b) for b in range(8)]
+
+        q_bf = keep.tile([P, NQ, PACK], BF16, name="q_bf", align_bytes=64)
+        nc.vector.tensor_copy(out=q_bf[:], in_=q_raw[:].rearrange("p t q -> p q t"))
+        q_codes = keep.tile([P, NQ], U32, name="q_codes", align_bytes=64)
+        q_scales = keep.tile([P, NQ], U8, name="q_scales", align_bytes=64)
+        nc.vector.quantize_mx(out=q_codes[:].bitcast(FP8X4), scales=q_scales[:],
+                              in_=q_bf[:].rearrange("p q t -> p (q t)"))
+
+        im_wide = keep.tile([P, P], F32, name="im_wide")
+        nc.vector.tensor_copy(out=im_wide[:], in_=im_col[:].to_broadcast([P, P]))
+        nc.tensor.transpose(banks[2][:, 0:P], im_wide[:], ident[:])
+        im_rows = keep.tile([P, NQ], F32, name="im_rows")
+        nc.scalar.activation(out=im_rows[:], in_=banks[2][:, 0:P], func=ACT.Identity)
+
+        bias_listed = keep.tile([P, N], F32, name="bias_listed")
+        nc.vector.tensor_copy(out=bias_listed[:], in_=bias_pool[:].indirect(offsets[:]))
+        bias_blocked = keep.tile([P, N], F32, name="bias_blocked")
+        bias_cols = keep.tile([P, 2 * BLOCKS], F32, name="bias_cols")
+        for h in range(2):
+            cols = slice(h * HALF, (h + 1) * HALF)
+            nc.scalar.copy(
+                out=bias_blocked[:, cols].rearrange("p (j s r) -> p j s r", j=BLOCKS, r=RUN),
+                in_=bias_listed[:, cols].rearrange("p (s j r) -> p j s r", j=BLOCKS, r=RUN))
+            for j in range(BLOCKS):
+                c0 = h * HALF + j * P
+                nc.tensor.transpose(banks[6 + h][:, j * P:(j + 1) * P], bias_blocked[:, c0:c0 + P], ident[:])
+            nc.scalar.copy(out=bias_cols[:, h * BLOCKS:(h + 1) * BLOCKS], in_=banks[6 + h][:, 0:BANK:P])
+
+        k_bf = [keep.tile([P, HALF, PACK], BF16, name="k_bf%d" % h, align_bytes=64) for h in range(2)]
+        k_codes = [keep.tile([P, HALF], U32, name="k_codes%d" % h, align_bytes=64) for h in range(2)]
+        k_scales = [keep.tile([P, HALF], U8, name="k_scales%d" % h, align_bytes=64) for h in range(2)]
+        for t in range(PACK):
+            for h in range(2):
+                nc.vector.tensor_copy(
+                    out=k_bf[h][:, :, t].rearrange("p (j s r) -> p s j r", j=BLOCKS, r=RUN),
+                    in_=planes[t][:].indirect(offsets[:, h * HALF // 16:(h + 1) * HALF // 16]))
+        for h in range(2):
+            nc.vector.quantize_mx(out=k_codes[h][:].bitcast(FP8X4), scales=k_scales[h][:],
+                                  in_=k_bf[h][:].rearrange("p c t -> p (c t)"))
+
+        score = {(0, 0): banks[0][:, 0:P], (0, 1): banks[1][:, 0:P], (0, 2): banks[2][:, 0:P], (0, 3): banks[2][:, P:2 * P],
+                 (1, 0): banks[3][:, 0:P], (1, 1): banks[4][:, 0:P], (1, 2): banks[5][:, 0:P], (1, 3): banks[6][:, 0:P]}
+        turned = [banks[7], banks[1]]
+        for h in range(2):
+            for j in range(BLOCKS):
+                cols = slice(j * P, (j + 1) * P)
+                nc.tensor.matmul_mx(out=score[h, j], lhsT=k_codes[h][:, cols].bitcast(FP8X4),
+                                    lhsT_scale=k_scales[h][:, cols], rhs=q_codes[:].bitcast(FP8X4),
+                                    rhs_scale=q_scales[:], start=True, stop=True)
+
+        best = []
+        for h in range(2):
+            bias = lambda j: bias_cols[:, h * BLOCKS + j:h * BLOCKS + j + 1]
+            first0 = keep.tile([P, NQ], F32, name="first0_%d" % h)
+            first1 = keep.tile([P, NQ], F32, name="first1_%d" % h)
+            best0 = keep.tile([P, NQ], F32, name="best0_%d" % h)
+            best1 = keep.tile([P, NQ], F32, name="best1_%d" % h)
+            nc.scalar.activation(out=first0[:], in_=score[h, 0], func=ACT.Identity, bias=bias(0))
+            for dst, j, other in ((first1, 1, im_rows), (best0, 2, first0), (best1, 3, first1)):
+                nc.vector.scalar_tensor_tensor(out=dst[:], in0=score[h, j], scalar=bias(j), in1=other[:],
+                                               op0=ALU.add, op1=ALU.max)
+            best.append((best0, best1))
+
+        result = keep.tile([P, N // SEG], F32, name="result")
+        for h in range(2):
+            for u in range(2):
+                nc.tensor.transpose(turned[h][:, u * P:(u + 1) * P], best[h][u][:], ident[:])
+            nc.vector.tensor_reduce(
+                out=result[:, h * SEGS:(h + 1) * SEGS],
+                in_=turned[h][:, 0:2 * P].rearrange("p (u s r) -> p s u r", u=2, r=RUN),
+                axis=AXES.XY, op=ALU.max)
+        nc.sync.dma_start(out=out[0], in_=result[:])

@@ -32,20 +32,19 @@ def tile_attend_xtr_f_kernel(tc, qT, kT, kb, im, offs, out):
         keep = ctx.enter_context(tc.tile_pool(name="keep", bufs=1))
         psum = ctx.enter_context(tc.psum_pool(name="psum", bufs=1))
 
-        offsets = keep.tile([P, N // 16], U16, name="offsets")
-        nc.sync.dma_start(offsets[:], offs)
         q_raw = keep.tile([P, PACK, NQ], F32, name="q_raw")
         nc.sync.dma_start(out=q_raw[:], in_=qT[0].rearrange("(p t) q -> p t q", t=PACK))
+        offsets = keep.tile([P, N // 16], U16, name="offsets")
+        nc.sync.dma_start(offsets[:], offs)
         k_rows = kT.rearrange("(p t) w -> p t w", t=PACK)
         planes = [keep.tile([P, T], F32, name="plane%d" % t) for t in range(PACK)]
         for t in range(PACK):
             nc.sync.dma_start(out=planes[t][:], in_=k_rows[:, t, :])
-
+        bias_pool = keep.tile([P, T], F32, name="bias_pool")
+        nc.scalar.dma_start(out=bias_pool[P - 1:P, :], in_=kb[0:1, :])
+        nc.vector.memset(bias_pool[0:P - 1, :], 0.0)
         im_col = keep.tile([P, 1], F32, name="im_col")
         nc.scalar.dma_start(out=im_col[:], in_=im[0])
-        bias_pool = keep.tile([P, T], F32, name="bias_pool")
-        nc.vector.memset(bias_pool[:], 0.0)
-        nc.scalar.dma_start(out=bias_pool[0:1, :], in_=kb[0:1, :])
 
         ident = keep.tile([P, P], F32, name="ident")
         make_identity(nc, ident[:])
@@ -76,28 +75,33 @@ def tile_attend_xtr_f_kernel(tc, qT, kT, kb, im, offs, out):
             for j in range(BLOCKS):
                 c0 = h * HALF + j * P
                 nc.tensor.transpose(banks[6 + h][:, j * P:(j + 1) * P], bias_blocked[:, c0:c0 + P], ident[:])
-            nc.scalar.copy(out=bias_cols[:, h * BLOCKS:(h + 1) * BLOCKS], in_=banks[6 + h][:, 0:BANK:P])
+            nc.scalar.copy(out=bias_cols[:, h * BLOCKS:(h + 1) * BLOCKS], in_=banks[6 + h][:, P - 1:BANK:P])
 
-        k_bf = [keep.tile([P, HALF, PACK], BF16, name="k_bf%d" % h, align_bytes=64) for h in range(2)]
-        k_codes = [keep.tile([P, HALF], U32, name="k_codes%d" % h, align_bytes=64) for h in range(2)]
-        k_scales = [keep.tile([P, HALF], U8, name="k_scales%d" % h, align_bytes=64) for h in range(2)]
+        quarters = [(h, u) for h in range(2) for u in range(2)]
+        k_bf = {q: keep.tile([P, 2 * P, PACK], BF16, name="k_bf%d%d" % q, align_bytes=64) for q in quarters}
+        k_codes = {q: keep.tile([P, 2 * P], U32, name="k_codes%d%d" % q, align_bytes=64) for q in quarters}
+        k_scales = {q: keep.tile([P, 2 * P], U8, name="k_scales%d%d" % q, align_bytes=64) for q in quarters}
         for t in range(PACK):
-            for h in range(2):
+            listed = [keep.tile([P, HALF], F32, name="listed%d%d" % (t, h)) for h in range(2)]
+            for h in (1, 0):
                 nc.vector.tensor_copy(
-                    out=k_bf[h][:, :, t].rearrange("p (j s r) -> p s j r", j=BLOCKS, r=RUN),
-                    in_=planes[t][:].indirect(offsets[:, h * HALF // 16:(h + 1) * HALF // 16]))
-        for h in range(2):
-            nc.vector.quantize_mx(out=k_codes[h][:].bitcast(FP8X4), scales=k_scales[h][:],
-                                  in_=k_bf[h][:].rearrange("p c t -> p (c t)"))
+                    out=listed[h][:], in_=planes[t][:].indirect(offsets[:, h * HALF // 16:(h + 1) * HALF // 16]))
+            for h, u in quarters:
+                copy = nc.scalar.copy if h == 1 else nc.vector.tensor_copy
+                copy(out=k_bf[h, u][:, :, t].rearrange("p (j s r) -> p j s r", j=2, r=RUN),
+                     in_=listed[h][:].rearrange("p (s j r) -> p j s r", j=BLOCKS, r=RUN)[:, 2 * u:2 * u + 2])
+        for q in quarters:
+            nc.vector.quantize_mx(out=k_codes[q][:].bitcast(FP8X4), scales=k_scales[q][:],
+                                  in_=k_bf[q][:].rearrange("p c t -> p (c t)"))
 
         score = {(0, 0): banks[0][:, 0:P], (0, 1): banks[1][:, 0:P], (0, 2): banks[2][:, 0:P], (0, 3): banks[2][:, P:2 * P],
                  (1, 0): banks[3][:, 0:P], (1, 1): banks[4][:, 0:P], (1, 2): banks[5][:, 0:P], (1, 3): banks[6][:, 0:P]}
         turned = [banks[7], banks[1]]
         for h in range(2):
             for j in range(BLOCKS):
-                cols = slice(j * P, (j + 1) * P)
-                nc.tensor.matmul_mx(out=score[h, j], lhsT=k_codes[h][:, cols].bitcast(FP8X4),
-                                    lhsT_scale=k_scales[h][:, cols], rhs=q_codes[:].bitcast(FP8X4),
+                cols = slice(j % 2 * P, (j % 2 + 1) * P)
+                nc.tensor.matmul_mx(out=score[h, j], lhsT=k_codes[h, j // 2][:, cols].bitcast(FP8X4),
+                                    lhsT_scale=k_scales[h, j // 2][:, cols], rhs=q_codes[:].bitcast(FP8X4),
                                     rhs_scale=q_scales[:], start=True, stop=True)
 
         best = []

@@ -21,6 +21,8 @@ SEGS = HALF // SEG
 BLOCKS = HALF // P
 RUN = SEG // BLOCKS
 BANK = 512
+CHUNKS = 4
+ROW_STEP = 4
 
 FLOPS = 2 * D * NQ * N
 BYTES = 4 * (D * NQ + D * T + T + NQ + NQ * N // SEG) + 2 * P * N // 16
@@ -41,10 +43,12 @@ def tile_attend_xtr_f_kernel(tc, qT, kT, kb, im, offs, out):
         for t in range(PACK):
             nc.sync.dma_start(out=planes[t][:], in_=k_rows[:, t, :])
         bias_pool = keep.tile([P, T], F32, name="bias_pool")
-        nc.scalar.dma_start(out=bias_pool[P - 1:P, :], in_=kb[0:1, :])
-        nc.vector.memset(bias_pool[0:P - 1, :], 0.0)
         im_col = keep.tile([P, 1], F32, name="im_col")
         nc.scalar.dma_start(out=im_col[:], in_=im[0])
+        nc.vector.memset(bias_pool[:], 0.0)
+        for c in range(CHUNKS):
+            cols = slice(c * T // CHUNKS, (c + 1) * T // CHUNKS)
+            nc.scalar.dma_start(out=bias_pool[c * ROW_STEP:c * ROW_STEP + 1, cols], in_=kb[0:1, cols])
 
         ident = keep.tile([P, P], F32, name="ident")
         make_identity(nc, ident[:])
@@ -75,7 +79,10 @@ def tile_attend_xtr_f_kernel(tc, qT, kT, kb, im, offs, out):
             for j in range(BLOCKS):
                 c0 = h * HALF + j * P
                 nc.tensor.transpose(banks[6 + h][:, j * P:(j + 1) * P], bias_blocked[:, c0:c0 + P], ident[:])
-            nc.scalar.copy(out=bias_cols[:, h * BLOCKS:(h + 1) * BLOCKS], in_=banks[6 + h][:, P - 1:BANK:P])
+            nc.vector.tensor_reduce(
+                out=bias_cols[:, h * BLOCKS:(h + 1) * BLOCKS],
+                in_=banks[6 + h][:].rearrange("p (j n) -> p j n", n=P)[:, :, 0:CHUNKS * ROW_STEP:ROW_STEP],
+                axis=AXES.X, op=ALU.add)
 
         quarters = [(h, u) for h in range(2) for u in range(2)]
         k_bf = {q: keep.tile([P, 2 * P, PACK], BF16, name="k_bf%d%d" % q, align_bytes=64) for q in quarters}
@@ -83,11 +90,11 @@ def tile_attend_xtr_f_kernel(tc, qT, kT, kb, im, offs, out):
         k_scales = {q: keep.tile([P, 2 * P], U8, name="k_scales%d%d" % q, align_bytes=64) for q in quarters}
         for t in range(PACK):
             listed = [keep.tile([P, HALF], F32, name="listed%d%d" % (t, h)) for h in range(2)]
-            for h in (1, 0):
+            for h in range(2):
                 nc.vector.tensor_copy(
                     out=listed[h][:], in_=planes[t][:].indirect(offsets[:, h * HALF // 16:(h + 1) * HALF // 16]))
             for h, u in quarters:
-                copy = nc.scalar.copy if h == 1 else nc.vector.tensor_copy
+                copy = nc.scalar.copy if h == u else nc.vector.tensor_copy
                 copy(out=k_bf[h, u][:, :, t].rearrange("p (j s r) -> p j s r", j=2, r=RUN),
                      in_=listed[h][:].rearrange("p (s j r) -> p j s r", j=BLOCKS, r=RUN)[:, 2 * u:2 * u + 2])
         for q in quarters:

@@ -21,8 +21,7 @@ SEGS = HALF // SEG
 BLOCKS = HALF // P
 RUN = SEG // BLOCKS
 BANK = 512
-CHUNKS = 4
-ROW_STEP = 4
+VECTOR_PAGES = 80
 
 FLOPS = 2 * D * NQ * N
 BYTES = 4 * (D * NQ + D * T + T + NQ + NQ * N // SEG) + 2 * P * N // 16
@@ -34,25 +33,49 @@ def tile_attend_xtr_f_kernel(tc, qT, kT, kb, im, offs, out):
         keep = ctx.enter_context(tc.tile_pool(name="keep", bufs=1))
         psum = ctx.enter_context(tc.psum_pool(name="psum", bufs=1))
 
+        bias_pages = keep.tile([P, SEG], F32, name="bias_pages")
+        nc.sync.dma_start(out=bias_pages[:], in_=kb[0].rearrange("(g i) -> g i", i=SEG))
         q_raw = keep.tile([P, PACK, NQ], F32, name="q_raw")
         nc.sync.dma_start(out=q_raw[:], in_=qT[0].rearrange("(p t) q -> p t q", t=PACK))
         offsets = keep.tile([P, N // 16], U16, name="offsets")
         nc.sync.dma_start(offsets[:], offs)
         k_rows = kT.rearrange("(p t) w -> p t w", t=PACK)
         planes = [keep.tile([P, T], F32, name="plane%d" % t) for t in range(PACK)]
-        for t in range(PACK):
-            nc.sync.dma_start(out=planes[t][:], in_=k_rows[:, t, :])
         bias_pool = keep.tile([P, T], F32, name="bias_pool")
         im_col = keep.tile([P, 1], F32, name="im_col")
-        nc.scalar.dma_start(out=im_col[:], in_=im[0])
-        nc.vector.memset(bias_pool[:], 0.0)
-        for c in range(CHUNKS):
-            cols = slice(c * T // CHUNKS, (c + 1) * T // CHUNKS)
-            nc.scalar.dma_start(out=bias_pool[c * ROW_STEP:c * ROW_STEP + 1, cols], in_=kb[0:1, cols])
+        nc.sync.dma_start(out=im_col[:], in_=im[0])
+        bias_paged = bias_pool[:].rearrange("p (g i) -> p g i", i=SEG)
+        for t in range(PACK):
+            nc.sync.dma_start(out=planes[t][:], in_=k_rows[:, t, :])
 
         ident = keep.tile([P, P], F32, name="ident")
         make_identity(nc, ident[:])
-        banks = [psum.tile([P, BANK], F32, name="bank%d" % b) for b in range(8)]
+        nc.gpsimd.memset(bias_paged[:, VECTOR_PAGES:, RUN:], 0.0)
+        nc.vector.memset(bias_paged[:, 0:VECTOR_PAGES, RUN:], 0.0)
+        turned_bias = [psum.tile([P, BANK], F32, name="turned_bias%d" % b, tag="bank%d" % (4 + b)) for b in range(2)]
+        banks = {b: psum.tile([P, BANK], F32, name="bank%d" % b, tag="bank%d" % b) for b in (0, 1, 2, 3, 6, 7)}
+
+        bias_dealt = keep.tile([P, P + SEG], F32, name="bias_dealt")
+        for c in range(0, P + SEG, SEG):
+            nc.vector.tensor_copy(out=bias_dealt[:, c:c + SEG].rearrange("p (r j) -> p r j", j=BLOCKS),
+                                  in_=bias_pages[:].rearrange("p (j r) -> p r j", j=BLOCKS))
+        for b in range(2):
+            for r in range(RUN // 2):
+                first = (b * RUN // 2 + r) * BLOCKS
+                nc.tensor.transpose(turned_bias[b][:, r * P:(r + 1) * P], bias_dealt[:, first:first + P], ident[:])
+            nc.scalar.activation(
+                out=bias_paged[:, :, b * RUN // 2:(b + 1) * RUN // 2],
+                in_=turned_bias[b][:].rearrange("p (r g) -> p g r", g=P), func=ACT.Copy)
+        bias_listed = keep.tile([P, N], F32, name="bias_listed", tag="listed")
+        nc.vector.tensor_copy(out=bias_listed[:], in_=bias_pool[:].indirect(offsets[:]))
+        bias_blocked = keep.tile([P, 2 * P], F32, name="bias_blocked")
+        nc.scalar.copy(out=bias_blocked[:].rearrange("p (s r) -> p s r", r=RUN),
+                       in_=bias_listed[:].rearrange("p (s i) -> p s i", i=SEG)[:, :, 0:RUN])
+        bias_cols = keep.tile([P, 2 * BLOCKS], F32, name="bias_cols")
+        for h in range(2):
+            nc.tensor.transpose(banks[6][:, h * P:(h + 1) * P], bias_blocked[:, h * P:(h + 1) * P], ident[:])
+        nc.scalar.copy(out=bias_cols[:].rearrange("p (h j) -> p h j", h=2),
+                       in_=banks[6][:, 0:2 * P].rearrange("p (h n) -> p h n", h=2)[:, :, 0:BLOCKS])
 
         q_bf = keep.tile([P, NQ, PACK], BF16, name="q_bf", align_bytes=64)
         nc.vector.tensor_copy(out=q_bf[:], in_=q_raw[:].rearrange("p t q -> p q t"))
@@ -67,40 +90,26 @@ def tile_attend_xtr_f_kernel(tc, qT, kT, kb, im, offs, out):
         im_rows = keep.tile([P, NQ], F32, name="im_rows")
         nc.scalar.activation(out=im_rows[:], in_=banks[2][:, 0:P], func=ACT.Identity)
 
-        bias_listed = keep.tile([P, N], F32, name="bias_listed")
-        nc.vector.tensor_copy(out=bias_listed[:], in_=bias_pool[:].indirect(offsets[:]))
-        bias_blocked = keep.tile([P, N], F32, name="bias_blocked")
-        bias_cols = keep.tile([P, 2 * BLOCKS], F32, name="bias_cols")
-        for h in range(2):
-            cols = slice(h * HALF, (h + 1) * HALF)
-            nc.scalar.copy(
-                out=bias_blocked[:, cols].rearrange("p (j s r) -> p j s r", j=BLOCKS, r=RUN),
-                in_=bias_listed[:, cols].rearrange("p (s j r) -> p j s r", j=BLOCKS, r=RUN))
-            for j in range(BLOCKS):
-                c0 = h * HALF + j * P
-                nc.tensor.transpose(banks[6 + h][:, j * P:(j + 1) * P], bias_blocked[:, c0:c0 + P], ident[:])
-            nc.vector.tensor_reduce(
-                out=bias_cols[:, h * BLOCKS:(h + 1) * BLOCKS],
-                in_=banks[6 + h][:].rearrange("p (j n) -> p j n", n=P)[:, :, 0:CHUNKS * ROW_STEP:ROW_STEP],
-                axis=AXES.X, op=ALU.add)
-
+        k_bf = [keep.tile([P, HALF, PACK], BF16, name="k_bf%d" % h, align_bytes=64) for h in range(2)]
         quarters = [(h, u) for h in range(2) for u in range(2)]
-        k_bf = {q: keep.tile([P, 2 * P, PACK], BF16, name="k_bf%d%d" % q, align_bytes=64) for q in quarters}
         k_codes = {q: keep.tile([P, 2 * P], U32, name="k_codes%d%d" % q, align_bytes=64) for q in quarters}
         k_scales = {q: keep.tile([P, 2 * P], U8, name="k_scales%d%d" % q, align_bytes=64) for q in quarters}
+        half_list = [offsets[:, h * HALF // 16:(h + 1) * HALF // 16] for h in range(2)]
         for t in range(PACK):
-            listed = [keep.tile([P, HALF], F32, name="listed%d%d" % (t, h)) for h in range(2)]
+            both = keep.tile([P, N], F32, name="listed%d" % t, tag="listed")
+            listed = [both[:, h * HALF:(h + 1) * HALF] for h in range(2)]
             for h in range(2):
-                nc.vector.tensor_copy(
-                    out=listed[h][:], in_=planes[t][:].indirect(offsets[:, h * HALF // 16:(h + 1) * HALF // 16]))
+                nc.vector.tensor_copy(out=listed[h], in_=planes[t][:].indirect(half_list[h]))
             for h, u in quarters:
                 copy = nc.scalar.copy if h == u else nc.vector.tensor_copy
-                copy(out=k_bf[h, u][:, :, t].rearrange("p (j s r) -> p j s r", j=2, r=RUN),
-                     in_=listed[h][:].rearrange("p (s j r) -> p j s r", j=BLOCKS, r=RUN)[:, 2 * u:2 * u + 2])
-        for q in quarters:
-            nc.vector.quantize_mx(out=k_codes[q][:].bitcast(FP8X4), scales=k_scales[q][:],
-                                  in_=k_bf[q][:].rearrange("p c t -> p (c t)"))
+                copy(out=k_bf[h][:, u * 2 * P:(u + 1) * 2 * P, t].rearrange("p (j s r) -> p j s r", j=2, r=RUN),
+                     in_=listed[h].rearrange("p (s j r) -> p j s r", j=BLOCKS, r=RUN)[:, 2 * u:2 * u + 2])
+        for h, u in quarters:
+            nc.vector.quantize_mx(out=k_codes[h, u][:].bitcast(FP8X4), scales=k_scales[h, u][:],
+                                  in_=k_bf[h][:, u * 2 * P:(u + 1) * 2 * P].rearrange("p c t -> p (c t)"))
 
+        for b in (4, 5):
+            banks[b] = psum.tile([P, BANK], F32, name="bank%d" % b, tag="bank%d" % b)
         score = {(0, 0): banks[0][:, 0:P], (0, 1): banks[1][:, 0:P], (0, 2): banks[2][:, 0:P], (0, 3): banks[2][:, P:2 * P],
                  (1, 0): banks[3][:, 0:P], (1, 1): banks[4][:, 0:P], (1, 2): banks[5][:, 0:P], (1, 3): banks[6][:, 0:P]}
         turned = [banks[7], banks[1]]

@@ -17,11 +17,13 @@ P = 128
 PACK = 4
 D, NQ, T, N, SEG = 512, 128, 4096, 1024, 32
 HALF = N // 2
-SEGS = HALF // SEG
-BLOCKS = HALF // P
-RUN = SEG // BLOCKS
 BANK = 512
-VECTOR_PAGES = 80
+LOADS = ((0, 2), (2, 3))
+RUN = 16
+FIRST, PAIR_A, PAIR_B, PAIR_V, LAST = range(5)
+PIECES = ((0, 128), (128, 384), (384, 640), (640, 896), (896, 1024))
+PAIRS = (PAIR_A, PAIR_B, PAIR_V)
+LAST_GATHERS = ((0, 128), (128, 384), (384, 640), (640, 1024))
 
 FLOPS = 2 * D * NQ * N
 BYTES = 4 * (D * NQ + D * T + T + NQ + NQ * N // SEG) + 2 * P * N // 16
@@ -32,50 +34,68 @@ def tile_attend_xtr_f_kernel(tc, qT, kT, kb, im, offs, out):
     with ExitStack() as ctx:
         keep = ctx.enter_context(tc.tile_pool(name="keep", bufs=1))
         psum = ctx.enter_context(tc.psum_pool(name="psum", bufs=1))
+        bank = lambda b, name: psum.tile([P, BANK], F32, name=name, tag="bank%d" % b)
 
-        bias_pages = keep.tile([P, SEG], F32, name="bias_pages")
-        nc.sync.dma_start(out=bias_pages[:], in_=kb[0].rearrange("(g i) -> g i", i=SEG))
-        q_raw = keep.tile([P, PACK, NQ], F32, name="q_raw")
-        nc.sync.dma_start(out=q_raw[:], in_=qT[0].rearrange("(p t) q -> p t q", t=PACK))
         offsets = keep.tile([P, N // 16], U16, name="offsets")
-        nc.sync.dma_start(offsets[:], offs)
-        k_rows = kT.rearrange("(p t) w -> p t w", t=PACK)
-        planes = [keep.tile([P, T], F32, name="plane%d" % t) for t in range(PACK)]
-        bias_pool = keep.tile([P, T], F32, name="bias_pool")
+        bias_pages = keep.tile([P, SEG], F32, name="bias_pages")
+        q_raw = keep.tile([P, PACK, NQ], F32, name="q_raw")
         im_col = keep.tile([P, 1], F32, name="im_col")
-        nc.sync.dma_start(out=im_col[:], in_=im[0])
-        bias_paged = bias_pool[:].rearrange("p (g i) -> p g i", i=SEG)
-        for t in range(PACK):
-            nc.sync.dma_start(out=planes[t][:], in_=k_rows[:, t, :])
+        k_rows = kT.rearrange("(p t) w -> p t w", t=PACK)
+        loads = [keep.tile([P, t1 - t0, T], F32, name="planes%d" % t0) for t0, t1 in LOADS]
+        last = keep.tile([P, T], F32, name="last_plane")
+        nc.sync.dma_start(offsets[:], offs)
+        nc.scalar.dma_start(out=bias_pages[:], in_=kb[0].rearrange("(g i) -> g i", i=SEG))
+        nc.scalar.dma_start(out=im_col[:], in_=im[0])
+        nc.scalar.dma_start(out=q_raw[:], in_=qT[0].rearrange("(p t) q -> p t q", t=PACK))
+        for n, (t0, t1) in enumerate(LOADS):
+            nc.sync.dma_start(out=loads[n][:], in_=k_rows[:, t0:t1, :])
+        nc.sync.dma_start(out=last[:], in_=k_rows[:, PACK - 1, :])
 
         ident = keep.tile([P, P], F32, name="ident")
         make_identity(nc, ident[:])
-        nc.gpsimd.memset(bias_paged[:, VECTOR_PAGES:, RUN:], 0.0)
-        nc.vector.memset(bias_paged[:, 0:VECTOR_PAGES, RUN:], 0.0)
-        turned_bias = [psum.tile([P, BANK], F32, name="turned_bias%d" % b, tag="bank%d" % (4 + b)) for b in range(2)]
-        banks = {b: psum.tile([P, BANK], F32, name="bank%d" % b, tag="bank%d" % b) for b in (0, 1, 2, 3, 6, 7)}
 
-        bias_dealt = keep.tile([P, P + SEG], F32, name="bias_dealt")
-        for c in range(0, P + SEG, SEG):
-            nc.vector.tensor_copy(out=bias_dealt[:, c:c + SEG].rearrange("p (r j) -> p r j", j=BLOCKS),
-                                  in_=bias_pages[:].rearrange("p (j r) -> p r j", j=BLOCKS))
-        for b in range(2):
-            for r in range(RUN // 2):
-                first = (b * RUN // 2 + r) * BLOCKS
-                nc.tensor.transpose(turned_bias[b][:, r * P:(r + 1) * P], bias_dealt[:, first:first + P], ident[:])
-            nc.scalar.activation(
-                out=bias_paged[:, :, b * RUN // 2:(b + 1) * RUN // 2],
-                in_=turned_bias[b][:].rearrange("p (r g) -> p g r", g=P), func=ACT.Copy)
-        bias_listed = keep.tile([P, N], F32, name="bias_listed", tag="listed")
+        bias_pool = keep.tile([P, T], F32, name="bias_pool", tag="listed")
+        bias_paged = bias_pool[:].rearrange("p (g i) -> p g i", i=SEG)
+        for b in range(SEG // 4):
+            spread = bank(b % 4, "spread%d" % b)
+            for r in range(4):
+                i = 4 * b + r
+                nc.tensor.transpose(spread[:, r * P:(r + 1) * P], bias_pages[:, i:i + 1].to_broadcast([P, P]), ident[:])
+            dst, src = bias_paged[:, :, 4 * b:4 * b + 4], spread[:].rearrange("p (r g) -> p g r", g=P)
+            if b // 2 % 2 == 0:
+                nc.scalar.activation(out=dst, in_=src, func=ACT.Copy)
+            else:
+                nc.vector.tensor_copy(out=dst, in_=src)
+        bias_listed = keep.tile([P, N], F32, name="bias_listed")
         nc.vector.tensor_copy(out=bias_listed[:], in_=bias_pool[:].indirect(offsets[:]))
-        bias_blocked = keep.tile([P, 2 * P], F32, name="bias_blocked")
-        nc.scalar.copy(out=bias_blocked[:].rearrange("p (s r) -> p s r", r=RUN),
-                       in_=bias_listed[:].rearrange("p (s i) -> p s i", i=SEG)[:, :, 0:RUN])
-        bias_cols = keep.tile([P, 2 * BLOCKS], F32, name="bias_cols")
-        for h in range(2):
-            nc.tensor.transpose(banks[6][:, h * P:(h + 1) * P], bias_blocked[:, h * P:(h + 1) * P], ident[:])
-        nc.scalar.copy(out=bias_cols[:].rearrange("p (h j) -> p h j", h=2),
-                       in_=banks[6][:, 0:2 * P].rearrange("p (h n) -> p h n", h=2)[:, :, 0:BLOCKS])
+        paired = slice(PIECES[PAIR_A][0], PIECES[PAIR_V][1])
+        bias_dealt = keep.tile([P, 6 * P], F32, name="bias_dealt")
+        nc.scalar.copy(out=bias_dealt[:].rearrange("p (g j s r) -> p g j s r", j=2, s=P // RUN, r=RUN),
+                       in_=bias_listed[:, paired].rearrange("p (g s j r) -> p g j s r", j=2, s=P // RUN, r=RUN))
+        slabs = [bias_listed[:, 0:P]] + [bias_dealt[:, j * P:(j + 1) * P] for j in range(6)]
+        bias_cols = keep.tile([P, 8], F32, name="bias_cols")
+        for b in range(2):
+            turned_bias = bank(4 + b, "turned_bias%d" % b)
+            some = slabs[4 * b:4 * b + 4]
+            for j, slab in enumerate(some):
+                nc.tensor.transpose(turned_bias[:, j * P:(j + 1) * P], slab, ident[:])
+            nc.scalar.copy(out=bias_cols[:, 4 * b:4 * b + len(some)],
+                           in_=turned_bias[:].rearrange("p (j n) -> p j n", n=P)[:, 0:len(some), 0])
+
+        im_spread = bank(4, "im_spread")
+        nc.tensor.transpose(im_spread[:, 0:P], im_col[:].to_broadcast([P, P]), ident[:])
+        im_rows = keep.tile([P, NQ], F32, name="im_rows")
+        nc.scalar.copy(out=im_rows[:], in_=im_spread[:, 0:P])
+        turned = [bank(6, "turned_early"), bank(7, "turned_late")]
+        for b in range(2):
+            for j in range(3):
+                nc.tensor.transpose(turned[b][:, j * P:(j + 1) * P], im_rows[:], ident[:])
+        wide, narrow = SEG + 2, RUN + 2
+        view_first = turned[0][:, 0:4 * wide].rearrange("p (s r) -> p s r", r=wide)
+        view_a = turned[0][:, 4 * wide:4 * wide + 8 * narrow].rearrange("p (s r) -> p s r", r=narrow)
+        view_bv = turned[1][:, 0:16 * narrow].rearrange("p (s r) -> p s r", r=narrow)
+        last_sum = keep.tile([P, 4, SEG + 4], F32, name="last_sum")
+        nc.vector.tensor_copy(out=last_sum[:, :, SEG:], in_=im_col[:].unsqueeze(2).to_broadcast([P, 4, 4]))
 
         q_bf = keep.tile([P, NQ, PACK], BF16, name="q_bf", align_bytes=64)
         nc.vector.tensor_copy(out=q_bf[:], in_=q_raw[:].rearrange("p t q -> p q t"))
@@ -84,61 +104,76 @@ def tile_attend_xtr_f_kernel(tc, qT, kT, kb, im, offs, out):
         nc.vector.quantize_mx(out=q_codes[:].bitcast(FP8X4), scales=q_scales[:],
                               in_=q_bf[:].rearrange("p q t -> p (q t)"))
 
-        im_wide = keep.tile([P, P], F32, name="im_wide")
-        nc.vector.tensor_copy(out=im_wide[:], in_=im_col[:].to_broadcast([P, P]))
-        nc.tensor.transpose(banks[2][:, 0:P], im_wide[:], ident[:])
-        im_rows = keep.tile([P, NQ], F32, name="im_rows")
-        nc.scalar.activation(out=im_rows[:], in_=banks[2][:, 0:P], func=ACT.Identity)
+        k_bf = [keep.tile([P, c1 - c0, PACK], BF16, name="k_bf%d" % c0, align_bytes=64) for c0, c1 in PIECES]
+        k_codes = [keep.tile([P, c1 - c0], U32, name="k_codes%d" % c0, align_bytes=64) for c0, c1 in PIECES]
+        k_scales = [keep.tile([P, c1 - c0], U8, name="k_scales%d" % c0, align_bytes=64) for c0, c1 in PIECES]
 
-        k_bf = [keep.tile([P, HALF, PACK], BF16, name="k_bf%d" % h, align_bytes=64) for h in range(2)]
-        quarters = [(h, u) for h in range(2) for u in range(2)]
-        k_codes = {q: keep.tile([P, 2 * P], U32, name="k_codes%d%d" % q, align_bytes=64) for q in quarters}
-        k_scales = {q: keep.tile([P, 2 * P], U8, name="k_scales%d%d" % q, align_bytes=64) for q in quarters}
-        half_list = [offsets[:, h * HALF // 16:(h + 1) * HALF // 16] for h in range(2)]
-        for t in range(PACK):
-            both = keep.tile([P, N], F32, name="listed%d" % t, tag="listed")
-            listed = [both[:, h * HALF:(h + 1) * HALF] for h in range(2)]
+        def weave(n, t0, t1, listed):
+            c0, c1 = PIECES[n]
+            copy = nc.vector.tensor_copy if n == PAIR_V else nc.scalar.copy
+            if n in PAIRS:
+                copy(out=k_bf[n][:, :, t0:t1].rearrange("p (j s r) t -> p j s r t", j=2, r=RUN),
+                     in_=listed[:, :, c0:c1].rearrange("p t (s j r) -> p j s r t", j=2, r=RUN))
+            else:
+                copy(out=k_bf[n][:, :, t0:t1], in_=listed[:, :, c0:c1].rearrange("p t c -> p c t"))
+
+        def quantise(n):
+            nc.vector.quantize_mx(out=k_codes[n][:].bitcast(FP8X4), scales=k_scales[n][:],
+                                  in_=k_bf[n][:].rearrange("p c t -> p (c t)"))
+
+        for n, (t0, t1) in enumerate(LOADS):
+            listed = keep.tile([P, t1 - t0, N], F32, name="listed%d" % n, tag="listed")
             for h in range(2):
-                nc.vector.tensor_copy(out=listed[h], in_=planes[t][:].indirect(half_list[h]))
-            for h, u in quarters:
-                copy = nc.scalar.copy if h == u else nc.vector.tensor_copy
-                copy(out=k_bf[h][:, u * 2 * P:(u + 1) * 2 * P, t].rearrange("p (j s r) -> p j s r", j=2, r=RUN),
-                     in_=listed[h].rearrange("p (s j r) -> p j s r", j=BLOCKS, r=RUN)[:, 2 * u:2 * u + 2])
-        for h, u in quarters:
-            nc.vector.quantize_mx(out=k_codes[h, u][:].bitcast(FP8X4), scales=k_scales[h, u][:],
-                                  in_=k_bf[h][:, u * 2 * P:(u + 1) * 2 * P].rearrange("p c t -> p (c t)"))
+                for t in range(t1 - t0):
+                    nc.vector.tensor_copy(out=listed[:, t, h * HALF:(h + 1) * HALF],
+                                          in_=loads[n][:, t, :].indirect(offsets[:, h * HALF // 16:(h + 1) * HALF // 16]))
+            for piece in range(len(PIECES)):
+                weave(piece, t0, t1, listed)
+        listed = keep.tile([P, 1, N], BF16, name="listed_last", tag="listed")
+        for c0, c1 in LAST_GATHERS:
+            nc.vector.tensor_copy(out=listed[:, 0, c0:c1], in_=last[:].indirect(offsets[:, c0 // 16:c1 // 16]))
+        for piece in (FIRST, PAIR_A, PAIR_B, LAST):
+            weave(piece, PACK - 1, PACK, listed)
+        quantise(FIRST)
+        weave(PAIR_V, PACK - 1, PACK, listed)
+        for piece in (PAIR_A, PAIR_V, PAIR_B, LAST):
+            quantise(piece)
 
-        for b in (4, 5):
-            banks[b] = psum.tile([P, BANK], F32, name="bank%d" % b, tag="bank%d" % b)
-        score = {(0, 0): banks[0][:, 0:P], (0, 1): banks[1][:, 0:P], (0, 2): banks[2][:, 0:P], (0, 3): banks[2][:, P:2 * P],
-                 (1, 0): banks[3][:, 0:P], (1, 1): banks[4][:, 0:P], (1, 2): banks[5][:, 0:P], (1, 3): banks[6][:, 0:P]}
-        turned = [banks[7], banks[1]]
-        for h in range(2):
-            for j in range(BLOCKS):
-                cols = slice(j % 2 * P, (j % 2 + 1) * P)
-                nc.tensor.matmul_mx(out=score[h, j], lhsT=k_codes[h, j // 2][:, cols].bitcast(FP8X4),
-                                    lhsT_scale=k_scales[h, j // 2][:, cols], rhs=q_codes[:].bitcast(FP8X4),
-                                    rhs_scale=q_scales[:], start=True, stop=True)
+        def scores(dst, piece, j):
+            cols = slice(j * P, (j + 1) * P)
+            nc.tensor.matmul_mx(out=dst, lhsT=k_codes[piece][:, cols].bitcast(FP8X4), lhsT_scale=k_scales[piece][:, cols],
+                                rhs=q_codes[:].bitcast(FP8X4), rhs_scale=q_scales[:], start=True, stop=True)
 
-        best = []
-        for h in range(2):
-            bias = lambda j: bias_cols[:, h * BLOCKS + j:h * BLOCKS + j + 1]
-            first0 = keep.tile([P, NQ], F32, name="first0_%d" % h)
-            first1 = keep.tile([P, NQ], F32, name="first1_%d" % h)
-            best0 = keep.tile([P, NQ], F32, name="best0_%d" % h)
-            best1 = keep.tile([P, NQ], F32, name="best1_%d" % h)
-            nc.scalar.activation(out=first0[:], in_=score[h, 0], func=ACT.Identity, bias=bias(0))
-            for dst, j, other in ((first1, 1, im_rows), (best0, 2, first0), (best1, 3, first1)):
-                nc.vector.scalar_tensor_tensor(out=dst[:], in0=score[h, j], scalar=bias(j), in1=other[:],
-                                               op0=ALU.add, op1=ALU.max)
-            best.append((best0, best1))
+        for_scalar = {piece: bank(piece, "for_scalar%d" % piece)[:, 0:P] for piece in (FIRST, PAIR_A, PAIR_V)}
+        for_scalar[PAIR_B] = turned[0][:, 3 * P:]
+        shared = bank(5, "for_vector_late")
+        for_vector = {PAIR_A: bank(2, "for_vector_a")[:, 0:P], PAIR_V: bank(4, "for_vector_v")[:, 0:P], PAIR_B: shared[:, 0:P]}
+        score_last = shared[:, P:2 * P]
+        scores(for_scalar[FIRST], FIRST, 0)
+        for piece in (PAIR_A, PAIR_V, PAIR_B):
+            scores(for_scalar[piece], piece, 0)
+            scores(for_vector[piece], piece, 1)
+        nc.tensor.matmul_mx(out=score_last, lhsT=q_codes[:].bitcast(FP8X4), lhsT_scale=q_scales[:],
+                            rhs=k_codes[LAST][:].bitcast(FP8X4), rhs_scale=k_scales[LAST][:], start=True, stop=True)
 
+        first = {piece: keep.tile([P, NQ], F32, name="first%d" % piece) for piece in (FIRST,) + PAIRS}
+        best = {piece: keep.tile([P, NQ], F32, name="best%d" % piece) for piece in PAIRS}
+        nc.scalar.activation(out=first[FIRST][:], in_=for_scalar[FIRST], func=ACT.Identity, bias=bias_cols[:, 0:1])
+        for piece in (PAIR_A, PAIR_V, PAIR_B):
+            nc.scalar.activation(out=first[piece][:], in_=for_scalar[piece], func=ACT.Identity,
+                                 bias=bias_cols[:, 2 * piece - 1:2 * piece])
+        for piece in (PAIR_A, PAIR_V, PAIR_B):
+            nc.vector.scalar_tensor_tensor(out=best[piece][:], in0=for_vector[piece],
+                                           scalar=bias_cols[:, 2 * piece:2 * piece + 1],
+                                           in1=first[piece][:], op0=ALU.add, op1=ALU.max)
+        nc.vector.tensor_tensor(out=last_sum[:, :, 0:SEG], in0=score_last.rearrange("p (s r) -> p s r", r=SEG),
+                                in1=bias_listed[:, PIECES[LAST][0]:].rearrange("p (s r) -> p s r", r=SEG), op=ALU.add)
+        nc.tensor.transpose(view_first[:, :, 0:SEG], first[FIRST][:], ident[:])
+        nc.tensor.transpose(view_a[:, :, 0:RUN], best[PAIR_A][:], ident[:])
+        nc.tensor.transpose(view_bv[:, 8:16, 0:RUN], best[PAIR_V][:], ident[:])
+        nc.tensor.transpose(view_bv[:, 0:8, 0:RUN], best[PAIR_B][:], ident[:])
         result = keep.tile([P, N // SEG], F32, name="result")
-        for h in range(2):
-            for u in range(2):
-                nc.tensor.transpose(turned[h][:, u * P:(u + 1) * P], best[h][u][:], ident[:])
-            nc.vector.tensor_reduce(
-                out=result[:, h * SEGS:(h + 1) * SEGS],
-                in_=turned[h][:, 0:2 * P].rearrange("p (u s r) -> p s u r", u=2, r=RUN),
-                axis=AXES.XY, op=ALU.max)
+        for cols, view in ((slice(28, 32), last_sum[:, :, 0:SEG + 1]), (slice(0, 4), view_first[:, :, 0:SEG + 1]),
+                           (slice(4, 12), view_a[:, :, 0:RUN + 1]), (slice(12, 28), view_bv[:, :, 0:RUN + 1])):
+            nc.vector.tensor_reduce(out=result[:, cols], in_=view, axis=AXES.X, op=ALU.max)
         nc.sync.dma_start(out=out[0], in_=result[:])

@@ -41,7 +41,7 @@ def tile_attend_xtr_f_kernel(tc, qT, kT, kb, im, offs, out):
         q_raw = keep.tile([P, PACK, NQ], F32, name="q_raw")
         im_col = keep.tile([P, 1], F32, name="im_col")
         k_rows = kT.rearrange("(p t) w -> p t w", t=PACK)
-        loads = [keep.tile([P, t1 - t0, T], F32, name="planes%d" % t0) for t0, t1 in LOADS]
+        loads = [keep.tile([P, t1 - t0, T], F32, name="planes%d" % t0, tag="planes%d" % t0, align_bytes=64) for t0, t1 in LOADS]
         last = keep.tile([P, T], F32, name="last_plane")
         nc.sync.dma_start(offsets[:], offs)
         nc.scalar.dma_start(out=bias_pages[:], in_=kb[0].rearrange("(g i) -> g i", i=SEG))
@@ -94,15 +94,8 @@ def tile_attend_xtr_f_kernel(tc, qT, kT, kb, im, offs, out):
         view_first = turned[0][:, 0:4 * wide].rearrange("p (s r) -> p s r", r=wide)
         view_a = turned[0][:, 4 * wide:4 * wide + 8 * narrow].rearrange("p (s r) -> p s r", r=narrow)
         view_bv = turned[1][:, 0:16 * narrow].rearrange("p (s r) -> p s r", r=narrow)
-        last_sum = keep.tile([P, 4, SEG + 4], F32, name="last_sum")
-        nc.vector.tensor_copy(out=last_sum[:, :, SEG:], in_=im_col[:].unsqueeze(2).to_broadcast([P, 4, 4]))
-
-        q_bf = keep.tile([P, NQ, PACK], BF16, name="q_bf", align_bytes=64)
-        nc.vector.tensor_copy(out=q_bf[:], in_=q_raw[:].rearrange("p t q -> p q t"))
-        q_codes = keep.tile([P, NQ], U32, name="q_codes", align_bytes=64)
-        q_scales = keep.tile([P, NQ], U8, name="q_scales", align_bytes=64)
-        nc.vector.quantize_mx(out=q_codes[:].bitcast(FP8X4), scales=q_scales[:],
-                              in_=q_bf[:].rearrange("p q t -> p (q t)"))
+        last_sum = keep.tile([P, 4, SEG + 8], F32, name="last_sum")
+        nc.gpsimd.tensor_copy(out=last_sum[:, :, SEG:], in_=im_col[:].unsqueeze(2).to_broadcast([P, 4, 8]))
 
         k_bf = [keep.tile([P, c1 - c0, PACK], BF16, name="k_bf%d" % c0, align_bytes=64) for c0, c1 in PIECES]
         k_codes = [keep.tile([P, c1 - c0], U32, name="k_codes%d" % c0, align_bytes=64) for c0, c1 in PIECES]
@@ -129,6 +122,13 @@ def tile_attend_xtr_f_kernel(tc, qT, kT, kb, im, offs, out):
                                           in_=loads[n][:, t, :].indirect(offsets[:, h * HALF // 16:(h + 1) * HALF // 16]))
             for piece in range(len(PIECES)):
                 weave(piece, t0, t1, listed)
+            if n == 0:
+                q_bf = keep.tile([P, NQ, PACK], BF16, name="q_bf", tag="planes0", align_bytes=64)
+                nc.vector.tensor_copy(out=q_bf[:], in_=q_raw[:].rearrange("p t q -> p q t"))
+                q_codes = keep.tile([P, NQ], U32, name="q_codes", align_bytes=64)
+                q_scales = keep.tile([P, NQ], U8, name="q_scales", align_bytes=64)
+                nc.vector.quantize_mx(out=q_codes[:].bitcast(FP8X4), scales=q_scales[:],
+                                      in_=q_bf[:].rearrange("p q t -> p (q t)"))
         listed = keep.tile([P, 1, N], BF16, name="listed_last", tag="listed")
         for c0, c1 in LAST_GATHERS:
             nc.vector.tensor_copy(out=listed[:, 0, c0:c1], in_=last[:].indirect(offsets[:, c0 // 16:c1 // 16]))

@@ -18,7 +18,6 @@ PACK = 4
 D, NQ, T, N, SEG = 512, 128, 4096, 1024, 32
 HALF = N // 2
 BANK = 512
-LOADS = ((0, 2), (2, 3))
 RUN = 16
 FIRST, PAIR_A, PAIR_B, PAIR_V, LAST = range(5)
 PIECES = ((0, 128), (128, 384), (384, 640), (640, 896), (896, 1024))
@@ -41,14 +40,15 @@ def tile_attend_xtr_f_kernel(tc, qT, kT, kb, im, offs, out):
         q_raw = keep.tile([P, PACK, NQ], F32, name="q_raw")
         im_col = keep.tile([P, 1], F32, name="im_col")
         k_rows = kT.rearrange("(p t) w -> p t w", t=PACK)
-        loads = [keep.tile([P, t1 - t0, T], F32, name="planes%d" % t0, tag="planes%d" % t0, align_bytes=64) for t0, t1 in LOADS]
+        early = keep.tile([P, 2, T], F32, name="early", tag="early", align_bytes=64)
+        third = keep.tile([P, T], F32, name="third", tag="third", align_bytes=64)
         last = keep.tile([P, T], F32, name="last_plane")
         nc.sync.dma_start(offsets[:], offs)
         nc.scalar.dma_start(out=bias_pages[:], in_=kb[0].rearrange("(g i) -> g i", i=SEG))
         nc.scalar.dma_start(out=im_col[:], in_=im[0])
         nc.scalar.dma_start(out=q_raw[:], in_=qT[0].rearrange("(p t) q -> p t q", t=PACK))
-        for n, (t0, t1) in enumerate(LOADS):
-            nc.sync.dma_start(out=loads[n][:], in_=k_rows[:, t0:t1, :])
+        nc.sync.dma_start(out=early[:], in_=k_rows[:, 0:2, :])
+        nc.sync.dma_start(out=third[:], in_=k_rows[:, 2, :])
         nc.sync.dma_start(out=last[:], in_=k_rows[:, PACK - 1, :])
 
         ident = keep.tile([P, P], F32, name="ident")
@@ -114,24 +114,30 @@ def tile_attend_xtr_f_kernel(tc, qT, kT, kb, im, offs, out):
             nc.vector.quantize_mx(out=k_codes[n][:].bitcast(FP8X4), scales=k_scales[n][:],
                                   in_=k_bf[n][:].rearrange("p c t -> p (c t)"))
 
-        for n, (t0, t1) in enumerate(LOADS):
-            listed = keep.tile([P, t1 - t0, N], F32, name="listed%d" % n, tag="listed")
-            for h in range(2):
-                for t in range(t1 - t0):
-                    nc.vector.tensor_copy(out=listed[:, t, h * HALF:(h + 1) * HALF],
-                                          in_=loads[n][:, t, :].indirect(offsets[:, h * HALF // 16:(h + 1) * HALF // 16]))
-            for piece in range(len(PIECES)):
-                weave(piece, t0, t1, listed)
-            if n == 0:
-                q_bf = keep.tile([P, NQ, PACK], BF16, name="q_bf", tag="planes0", align_bytes=64)
-                nc.vector.tensor_copy(out=q_bf[:], in_=q_raw[:].rearrange("p t q -> p q t"))
-                q_codes = keep.tile([P, NQ], U32, name="q_codes", align_bytes=64)
-                q_scales = keep.tile([P, NQ], U8, name="q_scales", align_bytes=64)
-                nc.vector.quantize_mx(out=q_codes[:].bitcast(FP8X4), scales=q_scales[:],
-                                      in_=q_bf[:].rearrange("p q t -> p (q t)"))
-        listed = keep.tile([P, 1, N], BF16, name="listed_last", tag="listed")
-        for c0, c1 in LAST_GATHERS:
-            nc.vector.tensor_copy(out=listed[:, 0, c0:c1], in_=last[:].indirect(offsets[:, c0 // 16:c1 // 16]))
+        listed = keep.tile([P, 2, N], F32, name="listed_early", tag="listed")
+        for h in range(2):
+            for t in range(2):
+                nc.vector.tensor_copy(out=listed[:, t, h * HALF:(h + 1) * HALF],
+                                      in_=early[:, t, :].indirect(offsets[:, h * HALF // 16:(h + 1) * HALF // 16]))
+        for piece in range(len(PIECES)):
+            weave(piece, 0, 2, listed)
+        q_bf = keep.tile([P, NQ, PACK], BF16, name="q_bf", tag="early", align_bytes=64)
+        nc.vector.tensor_copy(out=q_bf[:], in_=q_raw[:].rearrange("p t q -> p q t"))
+        q_codes = keep.tile([P, NQ], U32, name="q_codes", align_bytes=64)
+        q_scales = keep.tile([P, NQ], U8, name="q_scales", align_bytes=64)
+        nc.vector.quantize_mx(out=q_codes[:].bitcast(FP8X4), scales=q_scales[:],
+                              in_=q_bf[:].rearrange("p q t -> p (q t)"))
+
+        def gather(plane, tag):
+            listed = keep.tile([P, 1, N], BF16, name="listed_" + tag, tag=tag, align_bytes=64)
+            for c0, c1 in LAST_GATHERS:
+                nc.vector.tensor_copy(out=listed[:, 0, c0:c1], in_=plane[:].indirect(offsets[:, c0 // 16:c1 // 16]))
+            return listed
+
+        listed = gather(third, "early")
+        for piece in range(len(PIECES)):
+            weave(piece, 2, 3, listed)
+        listed = gather(last, "third")
         for piece in (FIRST, PAIR_A, PAIR_B, LAST):
             weave(piece, PACK - 1, PACK, listed)
         quantise(FIRST)

@@ -19,10 +19,11 @@ D, NQ, T, N, SEG = 512, 128, 4096, 1024, 32
 HALF = N // 2
 BANK = 512
 RUN = 16
-FIRST, PAIR_A, PAIR_B, PAIR_V, LAST = range(5)
+WIDE, NARROW = SEG + 8, RUN + 2
 PIECES = ((0, 128), (128, 384), (384, 640), (640, 896), (896, 1024))
-PAIRS = (PAIR_A, PAIR_B, PAIR_V)
-LAST_GATHERS = ((0, 128), (128, 384), (384, 640), (640, 1024))
+PAIRS = ()
+ON_VECTOR = (3,)
+GATHERS = ((0, 128), (128, 384), (384, 640), (640, 1024))
 
 FLOPS = 2 * D * NQ * N
 BYTES = 4 * (D * NQ + D * T + T + NQ + NQ * N // SEG) + 2 * P * N // 16
@@ -45,8 +46,8 @@ def tile_attend_xtr_f_kernel(tc, qT, kT, kb, im, offs, out):
         last = keep.tile([P, T], F32, name="last_plane")
         nc.sync.dma_start(offsets[:], offs)
         nc.scalar.dma_start(out=bias_pages[:], in_=kb[0].rearrange("(g i) -> g i", i=SEG))
-        nc.scalar.dma_start(out=im_col[:], in_=im[0])
         nc.scalar.dma_start(out=q_raw[:], in_=qT[0].rearrange("(p t) q -> p t q", t=PACK))
+        nc.scalar.dma_start(out=im_col[:], in_=im[0])
         nc.sync.dma_start(out=early[:], in_=k_rows[:, 0:2, :])
         nc.sync.dma_start(out=third[:], in_=k_rows[:, 2, :])
         nc.sync.dma_start(out=last[:], in_=k_rows[:, PACK - 1, :])
@@ -68,34 +69,9 @@ def tile_attend_xtr_f_kernel(tc, qT, kT, kb, im, offs, out):
                 nc.vector.tensor_copy(out=dst, in_=src)
         bias_listed = keep.tile([P, N], F32, name="bias_listed")
         nc.vector.tensor_copy(out=bias_listed[:], in_=bias_pool[:].indirect(offsets[:]))
-        paired = slice(PIECES[PAIR_A][0], PIECES[PAIR_V][1])
-        bias_dealt = keep.tile([P, 6 * P], F32, name="bias_dealt")
-        nc.scalar.copy(out=bias_dealt[:].rearrange("p (g j s r) -> p g j s r", j=2, s=P // RUN, r=RUN),
-                       in_=bias_listed[:, paired].rearrange("p (g s j r) -> p g j s r", j=2, s=P // RUN, r=RUN))
-        slabs = [bias_listed[:, 0:P]] + [bias_dealt[:, j * P:(j + 1) * P] for j in range(6)]
-        bias_cols = keep.tile([P, 8], F32, name="bias_cols")
-        for b in range(2):
-            turned_bias = bank(4 + b, "turned_bias%d" % b)
-            some = slabs[4 * b:4 * b + 4]
-            for j, slab in enumerate(some):
-                nc.tensor.transpose(turned_bias[:, j * P:(j + 1) * P], slab, ident[:])
-            nc.scalar.copy(out=bias_cols[:, 4 * b:4 * b + len(some)],
-                           in_=turned_bias[:].rearrange("p (j n) -> p j n", n=P)[:, 0:len(some), 0])
-
-        im_spread = bank(4, "im_spread")
-        nc.tensor.transpose(im_spread[:, 0:P], im_col[:].to_broadcast([P, P]), ident[:])
-        im_rows = keep.tile([P, NQ], F32, name="im_rows")
-        nc.scalar.copy(out=im_rows[:], in_=im_spread[:, 0:P])
-        turned = [bank(6, "turned_early"), bank(7, "turned_late")]
-        for b in range(2):
-            for j in range(3):
-                nc.tensor.transpose(turned[b][:, j * P:(j + 1) * P], im_rows[:], ident[:])
-        wide, narrow = SEG + 2, RUN + 2
-        view_first = turned[0][:, 0:4 * wide].rearrange("p (s r) -> p s r", r=wide)
-        view_a = turned[0][:, 4 * wide:4 * wide + 8 * narrow].rearrange("p (s r) -> p s r", r=narrow)
-        view_bv = turned[1][:, 0:16 * narrow].rearrange("p (s r) -> p s r", r=narrow)
-        last_sum = keep.tile([P, 4, SEG + 8], F32, name="last_sum")
-        nc.gpsimd.tensor_copy(out=last_sum[:, :, SEG:], in_=im_col[:].unsqueeze(2).to_broadcast([P, 4, 8]))
+        sums = keep.tile([P, N // SEG, WIDE], F32, name="sums")
+        nc.gpsimd.tensor_copy(out=sums[:, :, SEG:], in_=im_col[:].unsqueeze(2).to_broadcast([P, N // SEG, WIDE - SEG]))
+        turned, bias_cols = {}, {}
 
         k_bf = [keep.tile([P, c1 - c0, PACK], BF16, name="k_bf%d" % c0, align_bytes=64) for c0, c1 in PIECES]
         k_codes = [keep.tile([P, c1 - c0], U32, name="k_codes%d" % c0, align_bytes=64) for c0, c1 in PIECES]
@@ -103,7 +79,7 @@ def tile_attend_xtr_f_kernel(tc, qT, kT, kb, im, offs, out):
 
         def weave(n, t0, t1, listed):
             c0, c1 = PIECES[n]
-            copy = nc.vector.tensor_copy if n == PAIR_V else nc.scalar.copy
+            copy = nc.vector.tensor_copy if n in ON_VECTOR else nc.scalar.copy
             if n in PAIRS:
                 copy(out=k_bf[n][:, :, t0:t1].rearrange("p (j s r) t -> p j s r t", j=2, r=RUN),
                      in_=listed[:, :, c0:c1].rearrange("p t (s j r) -> p j s r t", j=2, r=RUN))
@@ -128,58 +104,85 @@ def tile_attend_xtr_f_kernel(tc, qT, kT, kb, im, offs, out):
         nc.vector.quantize_mx(out=q_codes[:].bitcast(FP8X4), scales=q_scales[:],
                               in_=q_bf[:].rearrange("p q t -> p (q t)"))
 
-        def gather(plane, tag):
+        def gather(plane, tag, order):
             listed = keep.tile([P, 1, N], BF16, name="listed_" + tag, tag=tag, align_bytes=64)
-            for c0, c1 in LAST_GATHERS:
+            for c0, c1 in [GATHERS[n] for n in order]:
                 nc.vector.tensor_copy(out=listed[:, 0, c0:c1], in_=plane[:].indirect(offsets[:, c0 // 16:c1 // 16]))
             return listed
 
-        listed = gather(third, "early")
+        listed = gather(third, "early", (0, 1, 3, 2))
         for piece in range(len(PIECES)):
             weave(piece, 2, 3, listed)
-        listed = gather(last, "third")
-        for piece in (FIRST, PAIR_A, PAIR_B, LAST):
-            weave(piece, PACK - 1, PACK, listed)
-        quantise(FIRST)
-        weave(PAIR_V, PACK - 1, PACK, listed)
-        for piece in (PAIR_A, PAIR_V, PAIR_B, LAST):
-            quantise(piece)
+        listed = gather(last, "third", range(len(GATHERS)))
 
-        def scores(dst, piece, j):
-            cols = slice(j * P, (j + 1) * P)
-            nc.tensor.matmul_mx(out=dst, lhsT=k_codes[piece][:, cols].bitcast(FP8X4), lhsT_scale=k_scales[piece][:, cols],
-                                rhs=q_codes[:].bitcast(FP8X4), rhs_scale=q_scales[:], start=True, stop=True)
-
-        for_scalar = {piece: bank(piece, "for_scalar%d" % piece)[:, 0:P] for piece in (FIRST, PAIR_A, PAIR_V)}
-        for_scalar[PAIR_B] = turned[0][:, 3 * P:]
-        shared = bank(5, "for_vector_late")
-        for_vector = {PAIR_A: bank(2, "for_vector_a")[:, 0:P], PAIR_V: bank(4, "for_vector_v")[:, 0:P], PAIR_B: shared[:, 0:P]}
-        score_last = shared[:, P:2 * P]
-        scores(for_scalar[FIRST], FIRST, 0)
-        for piece in (PAIR_A, PAIR_V, PAIR_B):
-            scores(for_scalar[piece], piece, 0)
-            scores(for_vector[piece], piece, 1)
-        nc.tensor.matmul_mx(out=score_last, lhsT=q_codes[:].bitcast(FP8X4), lhsT_scale=q_scales[:],
-                            rhs=k_codes[LAST][:].bitcast(FP8X4), rhs_scale=k_scales[LAST][:], start=True, stop=True)
-
-        first = {piece: keep.tile([P, NQ], F32, name="first%d" % piece) for piece in (FIRST,) + PAIRS}
-        best = {piece: keep.tile([P, NQ], F32, name="best%d" % piece) for piece in PAIRS}
-        nc.scalar.activation(out=first[FIRST][:], in_=for_scalar[FIRST], func=ACT.Identity, bias=bias_cols[:, 0:1])
-        for piece in (PAIR_A, PAIR_V, PAIR_B):
-            nc.scalar.activation(out=first[piece][:], in_=for_scalar[piece], func=ACT.Identity,
-                                 bias=bias_cols[:, 2 * piece - 1:2 * piece])
-        for piece in (PAIR_A, PAIR_V, PAIR_B):
-            nc.vector.scalar_tensor_tensor(out=best[piece][:], in0=for_vector[piece],
-                                           scalar=bias_cols[:, 2 * piece:2 * piece + 1],
-                                           in1=first[piece][:], op0=ALU.add, op1=ALU.max)
-        nc.vector.tensor_tensor(out=last_sum[:, :, 0:SEG], in0=score_last.rearrange("p (s r) -> p s r", r=SEG),
-                                in1=bias_listed[:, PIECES[LAST][0]:].rearrange("p (s r) -> p s r", r=SEG), op=ALU.add)
-        nc.tensor.transpose(view_first[:, :, 0:SEG], first[FIRST][:], ident[:])
-        nc.tensor.transpose(view_a[:, :, 0:RUN], best[PAIR_A][:], ident[:])
-        nc.tensor.transpose(view_bv[:, 8:16, 0:RUN], best[PAIR_V][:], ident[:])
-        nc.tensor.transpose(view_bv[:, 0:8, 0:RUN], best[PAIR_B][:], ident[:])
+        score, second, first, best = {}, {}, {}, {}
+        free = 0
+        for piece, (c0, c1) in enumerate(PIECES):
+            if piece in PAIRS:
+                score[piece] = turned[piece][:, 3 * P:]
+                second[piece] = bank(free, "second%d" % piece)[:, 0:P]
+                first[piece] = keep.tile([P, NQ], F32, name="first%d" % piece)
+                best[piece] = keep.tile([P, NQ], F32, name="best%d" % piece)
+            else:
+                score[piece] = bank(free, "score%d" % piece)[:, 0:c1 - c0]
+            free = free + 1
         result = keep.tile([P, N // SEG], F32, name="result")
-        for cols, view in ((slice(28, 32), last_sum[:, :, 0:SEG + 1]), (slice(0, 4), view_first[:, :, 0:SEG + 1]),
-                           (slice(4, 12), view_a[:, :, 0:RUN + 1]), (slice(12, 28), view_bv[:, :, 0:RUN + 1])):
-            nc.vector.tensor_reduce(out=result[:, cols], in_=view, axis=AXES.X, op=ALU.max)
+
+        def multiply(n):
+            if n in PAIRS:
+                for j, dst in enumerate((score[n], second[n])):
+                    cols = slice(j * P, (j + 1) * P)
+                    nc.tensor.matmul_mx(out=dst, lhsT=k_codes[n][:, cols].bitcast(FP8X4), lhsT_scale=k_scales[n][:, cols],
+                                        rhs=q_codes[:].bitcast(FP8X4), rhs_scale=q_scales[:], start=True, stop=True)
+            else:
+                nc.tensor.matmul_mx(out=score[n], lhsT=q_codes[:].bitcast(FP8X4), lhsT_scale=q_scales[:],
+                                    rhs=k_codes[n][:].bitcast(FP8X4), rhs_scale=k_scales[n][:], start=True, stop=True)
+
+        def add(n):
+            c0, c1 = PIECES[n]
+            if n in PAIRS:
+                j = 2 * PAIRS.index(n)
+                nc.scalar.activation(out=first[n][:], in_=score[n], func=ACT.Identity, bias=bias_cols[:, j:j + 1])
+                nc.vector.scalar_tensor_tensor(out=best[n][:], in0=second[n], scalar=bias_cols[:, j + 1:j + 2],
+                                               in1=first[n][:], op0=ALU.add, op1=ALU.max)
+                view = turned[n][:, 0:8 * NARROW].rearrange("p (s r) -> p s r", r=NARROW)
+                nc.tensor.transpose(view[:, :, 0:RUN], best[n][:], ident[:])
+            else:
+                nc.vector.tensor_tensor(out=sums[:, c0 // SEG:c1 // SEG, 0:SEG],
+                                        in0=score[n].rearrange("p (s r) -> p s r", r=SEG),
+                                        in1=bias_listed[:, c0:c1].rearrange("p (s r) -> p s r", r=SEG), op=ALU.add)
+
+        def reduce(n):
+            c0, c1 = PIECES[n]
+            if n in PAIRS:
+                view = turned[n][:, 0:8 * NARROW].rearrange("p (s r) -> p s r", r=NARROW)[:, :, 0:RUN + 1]
+            else:
+                view = sums[:, c0 // SEG:c1 // SEG, 0:SEG + 1]
+            nc.vector.tensor_reduce(out=result[:, c0 // SEG:c1 // SEG], in_=view, axis=AXES.X, op=ALU.max)
+
+        weave(0, PACK - 1, PACK, listed)
+        weave(1, PACK - 1, PACK, listed)
+        weave(2, PACK - 1, PACK, listed)
+        weave(4, PACK - 1, PACK, listed)
+        quantise(0)
+        multiply(0)
+        weave(3, PACK - 1, PACK, listed)
+        quantise(1)
+        multiply(1)
+        quantise(3)
+        multiply(3)
+        add(0)
+        quantise(2)
+        multiply(2)
+        add(1)
+        quantise(4)
+        multiply(4)
+        reduce(0)
+        add(3)
+        reduce(1)
+        add(2)
+        reduce(3)
+        add(4)
+        reduce(2)
+        reduce(4)
         nc.sync.dma_start(out=out[0], in_=result[:])

@@ -19,6 +19,8 @@ D, NQ, T, N, SEG = 512, 128, 4096, 1024, 32
 HALF = N // 2
 BANK = 512
 RUN = 16
+EIGHT = 8
+VECTOR_PAGES = 80
 WIDE, NARROW = SEG + 8, RUN + 2
 PIECES = ((0, 128), (128, 384), (384, 640), (640, 896), (896, 1024))
 PAIRS = ()
@@ -57,23 +59,42 @@ def tile_attend_xtr_f_kernel(tc, qT, kT, kb, im, offs, out):
 
         bias_pool = keep.tile([P, T], F32, name="bias_pool", tag="listed")
         bias_paged = bias_pool[:].rearrange("p (g i) -> p g i", i=SEG)
-        for b in range(SEG // 4):
-            spread = bank(b % 4, "spread%d" % b)
+        nc.gpsimd.memset(bias_paged[:, VECTOR_PAGES:, EIGHT:], 0.0)
+        nc.vector.memset(bias_paged[:, 0:VECTOR_PAGES, EIGHT:], 0.0)
+        bias_wide = keep.tile([P, P + SEG], F32, name="bias_wide")
+        for c in range(0, P + SEG, SEG):
+            nc.vector.tensor_copy(out=bias_wide[:, c:c + SEG].rearrange("p (r j) -> p r j", j=4),
+                                  in_=bias_pages[:].rearrange("p (j r) -> p r j", j=4))
+        for b in range(2):
+            spread = bank(b, "spread%d" % b)
             for r in range(4):
-                i = 4 * b + r
-                nc.tensor.transpose(spread[:, r * P:(r + 1) * P], bias_pages[:, i:i + 1].to_broadcast([P, P]), ident[:])
-            dst, src = bias_paged[:, :, 4 * b:4 * b + 4], spread[:].rearrange("p (r g) -> p g r", g=P)
-            if b // 2 % 2 == 0:
-                nc.scalar.activation(out=dst, in_=src, func=ACT.Copy)
-            else:
-                nc.vector.tensor_copy(out=dst, in_=src)
+                c0 = (4 * b + r) * 4
+                nc.tensor.transpose(spread[:, r * P:(r + 1) * P], bias_wide[:, c0:c0 + P], ident[:])
+            nc.scalar.activation(out=bias_paged[:, :, 4 * b:4 * b + 4],
+                                 in_=spread[:].rearrange("p (r g) -> p g r", g=P), func=ACT.Copy)
+        bias_gathered = keep.tile([P, N], F32, name="bias_gathered")
+        nc.vector.tensor_copy(out=bias_gathered[:], in_=bias_pool[:].indirect(offsets[:]))
+        bias_blocked = keep.tile([P, 2 * P], F32, name="bias_blocked")
+        nc.scalar.copy(out=bias_blocked[:].rearrange("p (s r) -> p s r", r=EIGHT),
+                       in_=bias_gathered[:].rearrange("p (s i) -> p s i", i=SEG)[:, :, 0:EIGHT])
+        down = bank(2, "down")
+        for h in range(2):
+            nc.tensor.transpose(down[:, h * P:(h + 1) * P], bias_blocked[:, h * P:(h + 1) * P], ident[:])
+        bias_down = keep.tile([P, 2, 4], F32, name="bias_down", tag="k_bf0", align_bytes=64)
+        nc.scalar.copy(out=bias_down[:], in_=down[:, 0:2 * P].rearrange("p (h n) -> p h n", h=2)[:, :, 0:4])
         bias_listed = keep.tile([P, N], F32, name="bias_listed")
-        nc.vector.tensor_copy(out=bias_listed[:], in_=bias_pool[:].indirect(offsets[:]))
+        for h in range(2):
+            along = bank(3 + h, "along%d" % h)
+            for j in range(4):
+                nc.tensor.transpose(along[:, j * P:(j + 1) * P], bias_down[:, h, j:j + 1].to_broadcast([P, P]), ident[:])
+            nc.scalar.copy(out=bias_listed[:, h * HALF:(h + 1) * HALF].rearrange("p (s j r) -> p j s r", j=4, r=EIGHT),
+                           in_=along[:].rearrange("p (j s r) -> p j s r", j=4, r=EIGHT))
         sums = keep.tile([P, N // SEG, WIDE], F32, name="sums")
         nc.gpsimd.tensor_copy(out=sums[:, :, SEG:], in_=im_col[:].unsqueeze(2).to_broadcast([P, N // SEG, WIDE - SEG]))
         turned, bias_cols = {}, {}
 
-        k_bf = [keep.tile([P, c1 - c0, PACK], BF16, name="k_bf%d" % c0, align_bytes=64) for c0, c1 in PIECES]
+        k_all = keep.tile([P, N, PACK], BF16, name="k_all", tag="k_bf0", align_bytes=64)
+        k_bf = [k_all[:, c0:c1, :] for c0, c1 in PIECES]
         k_codes = [keep.tile([P, c1 - c0], U32, name="k_codes%d" % c0, align_bytes=64) for c0, c1 in PIECES]
         k_scales = [keep.tile([P, c1 - c0], U8, name="k_scales%d" % c0, align_bytes=64) for c0, c1 in PIECES]
 
@@ -88,7 +109,7 @@ def tile_attend_xtr_f_kernel(tc, qT, kT, kb, im, offs, out):
 
         def quantise(n):
             nc.vector.quantize_mx(out=k_codes[n][:].bitcast(FP8X4), scales=k_scales[n][:],
-                                  in_=k_bf[n][:].rearrange("p c t -> p (c t)"))
+                                  in_=k_bf[n].rearrange("p c t -> p (c t)"))
 
         listed = keep.tile([P, 2, N], F32, name="listed_early", tag="listed")
         for h in range(2):

@@ -48,11 +48,11 @@ def tile_attend_xtr_f_kernel(tc, qT, kT, kb, im, offs, out):
         last = keep.tile([P, T], F32, name="last_plane")
         nc.sync.dma_start(offsets[:], offs)
         nc.scalar.dma_start(out=bias_pages[:], in_=kb[0].rearrange("(g i) -> g i", i=SEG))
-        nc.scalar.dma_start(out=q_raw[:], in_=qT[0].rearrange("(p t) q -> p t q", t=PACK))
         nc.scalar.dma_start(out=im_col[:], in_=im[0])
         nc.sync.dma_start(out=early[:], in_=k_rows[:, 0:2, :])
         nc.sync.dma_start(out=third[:], in_=k_rows[:, 2, :])
         nc.sync.dma_start(out=last[:], in_=k_rows[:, PACK - 1, :])
+        nc.sync.dma_start(out=q_raw[:], in_=qT[0].rearrange("(p t) q -> p t q", t=PACK))
 
         ident = keep.tile([P, P], F32, name="ident")
         make_identity(nc, ident[:])
@@ -118,12 +118,6 @@ def tile_attend_xtr_f_kernel(tc, qT, kT, kb, im, offs, out):
                                       in_=early[:, t, :].indirect(offsets[:, h * HALF // 16:(h + 1) * HALF // 16]))
         for piece in range(len(PIECES)):
             weave(piece, 0, 2, listed)
-        q_bf = keep.tile([P, NQ, PACK], BF16, name="q_bf", tag="early", align_bytes=64)
-        nc.vector.tensor_copy(out=q_bf[:], in_=q_raw[:].rearrange("p t q -> p q t"))
-        q_codes = keep.tile([P, NQ], U32, name="q_codes", align_bytes=64)
-        q_scales = keep.tile([P, NQ], U8, name="q_scales", align_bytes=64)
-        nc.vector.quantize_mx(out=q_codes[:].bitcast(FP8X4), scales=q_scales[:],
-                              in_=q_bf[:].rearrange("p q t -> p (q t)"))
 
         def gather(plane, tag, order):
             listed = keep.tile([P, 1, N], BF16, name="listed_" + tag, tag=tag, align_bytes=64)
@@ -136,6 +130,9 @@ def tile_attend_xtr_f_kernel(tc, qT, kT, kb, im, offs, out):
             weave(piece, 2, 3, listed)
         listed = gather(last, "third", range(len(GATHERS)))
 
+        q_bf = keep.tile([P, NQ, PACK], BF16, name="q_bf", align_bytes=64)
+        q_codes = keep.tile([P, NQ], U32, name="q_codes", align_bytes=64)
+        q_scales = keep.tile([P, NQ], U8, name="q_scales", align_bytes=64)
         score, second, first, best = {}, {}, {}, {}
         free = 0
         for piece, (c0, c1) in enumerate(PIECES):
@@ -182,22 +179,26 @@ def tile_attend_xtr_f_kernel(tc, qT, kT, kb, im, offs, out):
             nc.vector.tensor_reduce(out=result[:, c0 // SEG:c1 // SEG], in_=view, axis=AXES.X, op=ALU.max)
 
         weave(0, PACK - 1, PACK, listed)
+        nc.gpsimd.tensor_scalar(out=q_bf[:], in0=q_raw[:].rearrange("p t q -> p q t"), scalar1=1.0, scalar2=0.0,
+                                op0=ALU.mult, op1=ALU.add)
         weave(1, PACK - 1, PACK, listed)
         weave(2, PACK - 1, PACK, listed)
         weave(4, PACK - 1, PACK, listed)
         quantise(0)
+        nc.vector.quantize_mx(out=q_codes[:].bitcast(FP8X4), scales=q_scales[:],
+                              in_=q_bf[:].rearrange("p q t -> p (q t)"))
         multiply(0)
         weave(3, PACK - 1, PACK, listed)
         quantise(1)
         multiply(1)
         quantise(3)
         multiply(3)
-        add(0)
         quantise(2)
         multiply(2)
-        add(1)
         quantise(4)
         multiply(4)
+        add(0)
+        add(1)
         reduce(0)
         add(3)
         reduce(1)

@@ -24,7 +24,7 @@ VECTOR_PAGES = 80
 WIDE, NARROW = SEG + 8, RUN + 2
 PIECES = ((0, 128), (128, 384), (384, 640), (640, 896), (896, 1024))
 PAIRS = ()
-ON_VECTOR = (3,)
+ON_VECTOR = (3, 4)
 GATHERS = ((0, 128), (128, 384), (384, 640), (640, 1024))
 
 FLOPS = 2 * D * NQ * N
@@ -183,7 +183,6 @@ def tile_attend_xtr_f_kernel(tc, qT, kT, kb, im, offs, out):
                                 op0=ALU.mult, op1=ALU.add)
         weave(1, PACK - 1, PACK, listed)
         weave(2, PACK - 1, PACK, listed)
-        weave(4, PACK - 1, PACK, listed)
         quantise(0)
         nc.vector.quantize_mx(out=q_codes[:].bitcast(FP8X4), scales=q_scales[:],
                               in_=q_bf[:].rearrange("p q t -> p (q t)"))
@@ -191,6 +190,7 @@ def tile_attend_xtr_f_kernel(tc, qT, kT, kb, im, offs, out):
         weave(3, PACK - 1, PACK, listed)
         quantise(1)
         multiply(1)
+        weave(4, PACK - 1, PACK, listed)
         quantise(3)
         multiply(3)
         quantise(2)

@@ -40,12 +40,12 @@ def tile_attend_xtr_f_kernel(tc, qT, kT, kb, im, offs, out):
 
         offsets = keep.tile([P, N // 16], U16, name="offsets")
         bias_pages = keep.tile([P, SEG], F32, name="bias_pages")
-        q_raw = keep.tile([P, PACK, NQ], F32, name="q_raw")
+        q_raw = keep.tile([P, PACK, NQ], F32, name="q_raw", align_bytes=256)
         im_col = keep.tile([P, 1], F32, name="im_col")
         k_rows = kT.rearrange("(p t) w -> p t w", t=PACK)
-        early = keep.tile([P, 2, T], F32, name="early", tag="early", align_bytes=64)
-        third = keep.tile([P, T], F32, name="third", tag="third", align_bytes=64)
-        last = keep.tile([P, T], F32, name="last_plane")
+        early = keep.tile([P, 2, T], F32, name="early", tag="early", align_bytes=256)
+        third = keep.tile([P, T], F32, name="third", tag="third", align_bytes=256)
+        last = keep.tile([P, T], F32, name="last_plane", align_bytes=256)
         nc.sync.dma_start(offsets[:], offs)
         nc.scalar.dma_start(out=bias_pages[:], in_=kb[0].rearrange("(g i) -> g i", i=SEG))
         nc.scalar.dma_start(out=im_col[:], in_=im[0])
@@ -120,7 +120,7 @@ def tile_attend_xtr_f_kernel(tc, qT, kT, kb, im, offs, out):
             weave(piece, 0, 2, listed)
 
         def gather(plane, tag, order):
-            listed = keep.tile([P, 1, N], BF16, name="listed_" + tag, tag=tag, align_bytes=64)
+            listed = keep.tile([P, 1, N], BF16, name="listed_" + tag, tag=tag, align_bytes=256)
             for c0, c1 in [GATHERS[n] for n in order]:
                 nc.vector.tensor_copy(out=listed[:, 0, c0:c1], in_=plane[:].indirect(offsets[:, c0 // 16:c1 // 16]))
             return listed

@@ -16,16 +16,20 @@ AXES = mybir.AxisListType
 P = 128
 PACK = 4
 D, NQ, T, N, SEG = 512, 128, 4096, 1024, 32
+PER_COLUMN = 16
 HALF = N // 2
 BANK = 512
-RUN = 16
-EIGHT = 8
+MX_ALIGN = 64
+DMA_ALIGN = 256
+QUARTERS, QUARTER = 4, 8
 VECTOR_PAGES = 80
-WIDE, NARROW = SEG + 8, RUN + 2
+ROW = SEG + 8
+
 PIECES = ((0, 128), (128, 384), (384, 640), (640, 896), (896, 1024))
-PAIRS = ()
 ON_VECTOR = (3, 4)
+ON_SCALAR = (0, 1, 2)
 GATHERS = ((0, 128), (128, 384), (384, 640), (640, 1024))
+FINISH = (0, 1, 3, 2, 4)
 
 FLOPS = 2 * D * NQ * N
 BYTES = 4 * (D * NQ + D * T + T + NQ + NQ * N // SEG) + 2 * P * N // 16
@@ -36,175 +40,135 @@ def tile_attend_xtr_f_kernel(tc, qT, kT, kb, im, offs, out):
     with ExitStack() as ctx:
         keep = ctx.enter_context(tc.tile_pool(name="keep", bufs=1))
         psum = ctx.enter_context(tc.psum_pool(name="psum", bufs=1))
-        bank = lambda b, name: psum.tile([P, BANK], F32, name=name, tag="bank%d" % b)
 
-        offsets = keep.tile([P, N // 16], U16, name="offsets")
+        def bank(b, name):
+            return psum.tile([P, BANK], F32, name=name, tag="bank%d" % b)
+
+        def listed(window, c0, c1):
+            return window.indirect(offsets[:, c0 // PER_COLUMN:c1 // PER_COLUMN])
+
+        offsets = keep.tile([P, N // PER_COLUMN], U16, name="offsets")
         bias_pages = keep.tile([P, SEG], F32, name="bias_pages")
-        q_raw = keep.tile([P, PACK, NQ], F32, name="q_raw", align_bytes=256)
+        q_raw = keep.tile([P, PACK, NQ], F32, name="q_raw", align_bytes=DMA_ALIGN)
         im_col = keep.tile([P, 1], F32, name="im_col")
         k_rows = kT.rearrange("(p t) w -> p t w", t=PACK)
-        early = keep.tile([P, 2, T], F32, name="early", tag="early", align_bytes=256)
-        third = keep.tile([P, T], F32, name="third", tag="third", align_bytes=256)
-        last = keep.tile([P, T], F32, name="last_plane", align_bytes=256)
+        planes01 = keep.tile([P, 2, T], F32, name="planes01", tag="planes01", align_bytes=DMA_ALIGN)
+        plane2 = keep.tile([P, T], F32, name="plane2", tag="plane2", align_bytes=DMA_ALIGN)
+        plane3 = keep.tile([P, T], F32, name="plane3", align_bytes=DMA_ALIGN)
         nc.sync.dma_start(offsets[:], offs)
         nc.scalar.dma_start(out=bias_pages[:], in_=kb[0].rearrange("(g i) -> g i", i=SEG))
         nc.scalar.dma_start(out=im_col[:], in_=im[0])
-        nc.sync.dma_start(out=early[:], in_=k_rows[:, 0:2, :])
-        nc.sync.dma_start(out=third[:], in_=k_rows[:, 2, :])
-        nc.sync.dma_start(out=last[:], in_=k_rows[:, PACK - 1, :])
+        nc.sync.dma_start(out=planes01[:], in_=k_rows[:, 0:2, :])
+        nc.sync.dma_start(out=plane2[:], in_=k_rows[:, 2, :])
+        nc.sync.dma_start(out=plane3[:], in_=k_rows[:, 3, :])
         nc.sync.dma_start(out=q_raw[:], in_=qT[0].rearrange("(p t) q -> p t q", t=PACK))
 
         ident = keep.tile([P, P], F32, name="ident")
         make_identity(nc, ident[:])
 
-        bias_pool = keep.tile([P, T], F32, name="bias_pool", tag="listed")
-        bias_paged = bias_pool[:].rearrange("p (g i) -> p g i", i=SEG)
-        nc.gpsimd.memset(bias_paged[:, VECTOR_PAGES:, EIGHT:], 0.0)
-        nc.vector.memset(bias_paged[:, 0:VECTOR_PAGES, EIGHT:], 0.0)
+        bias_window = keep.tile([P, T], F32, name="bias_window", tag="staging")
+        bias_paged = bias_window[:].rearrange("p (g i) -> p g i", i=SEG)
+        nc.gpsimd.memset(bias_paged[:, VECTOR_PAGES:, QUARTER:], 0.0)
+        nc.vector.memset(bias_paged[:, 0:VECTOR_PAGES, QUARTER:], 0.0)
         bias_wide = keep.tile([P, P + SEG], F32, name="bias_wide")
-        for c in range(0, P + SEG, SEG):
-            nc.vector.tensor_copy(out=bias_wide[:, c:c + SEG].rearrange("p (r j) -> p r j", j=4),
-                                  in_=bias_pages[:].rearrange("p (j r) -> p r j", j=4))
-        for b in range(2):
-            spread = bank(b, "spread%d" % b)
-            for r in range(4):
-                c0 = (4 * b + r) * 4
-                nc.tensor.transpose(spread[:, r * P:(r + 1) * P], bias_wide[:, c0:c0 + P], ident[:])
-            nc.scalar.activation(out=bias_paged[:, :, 4 * b:4 * b + 4],
-                                 in_=spread[:].rearrange("p (r g) -> p g r", g=P), func=ACT.Copy)
+        for c0 in range(0, P + SEG, SEG):
+            nc.vector.tensor_copy(out=bias_wide[:, c0:c0 + SEG].rearrange("p (r j) -> p r j", j=QUARTERS),
+                                  in_=bias_pages[:].rearrange("p (j r) -> p r j", j=QUARTERS))
+        per_bank = BANK // P
+        for b in range(QUARTER // per_bank):
+            by_quarter = bank(b, "by_quarter%d" % b)
+            for n in range(per_bank):
+                c0 = (per_bank * b + n) * QUARTERS
+                nc.tensor.transpose(by_quarter[:, n * P:(n + 1) * P], bias_wide[:, c0:c0 + P], ident[:])
+            nc.scalar.activation(out=bias_paged[:, :, per_bank * b:per_bank * (b + 1)],
+                                 in_=by_quarter[:].rearrange("p (r g) -> p g r", g=P), func=ACT.Copy)
         bias_gathered = keep.tile([P, N], F32, name="bias_gathered")
-        nc.vector.tensor_copy(out=bias_gathered[:], in_=bias_pool[:].indirect(offsets[:]))
-        bias_blocked = keep.tile([P, 2 * P], F32, name="bias_blocked")
-        nc.scalar.copy(out=bias_blocked[:].rearrange("p (s r) -> p s r", r=EIGHT),
-                       in_=bias_gathered[:].rearrange("p (s i) -> p s i", i=SEG)[:, :, 0:EIGHT])
+        nc.vector.tensor_copy(out=bias_gathered[:], in_=listed(bias_window[:], 0, N))
+
+        bias_used = keep.tile([P, 2 * P], F32, name="bias_used")
+        nc.scalar.copy(out=bias_used[:].rearrange("p (s r) -> p s r", r=QUARTER),
+                       in_=bias_gathered[:].rearrange("p (s i) -> p s i", i=SEG)[:, :, 0:QUARTER])
         down = bank(2, "down")
         for h in range(2):
-            nc.tensor.transpose(down[:, h * P:(h + 1) * P], bias_blocked[:, h * P:(h + 1) * P], ident[:])
-        bias_down = keep.tile([P, 2, 4], F32, name="bias_down", tag="k_bf0", align_bytes=64)
-        nc.scalar.copy(out=bias_down[:], in_=down[:, 0:2 * P].rearrange("p (h n) -> p h n", h=2)[:, :, 0:4])
-        bias_listed = keep.tile([P, N], F32, name="bias_listed")
+            nc.tensor.transpose(down[:, h * P:(h + 1) * P], bias_used[:, h * P:(h + 1) * P], ident[:])
+        bias_down = keep.tile([P, 2, QUARTERS], F32, name="bias_down", tag="words", align_bytes=DMA_ALIGN)
+        nc.scalar.copy(out=bias_down[:], in_=down[:, 0:2 * P].rearrange("p (h n) -> p h n", h=2)[:, :, 0:QUARTERS])
+        bias_rows = keep.tile([P, N], F32, name="bias_rows", align_bytes=DMA_ALIGN)
         for h in range(2):
             along = bank(3 + h, "along%d" % h)
-            for j in range(4):
+            for j in range(QUARTERS):
                 nc.tensor.transpose(along[:, j * P:(j + 1) * P], bias_down[:, h, j:j + 1].to_broadcast([P, P]), ident[:])
-            nc.scalar.copy(out=bias_listed[:, h * HALF:(h + 1) * HALF].rearrange("p (s j r) -> p j s r", j=4, r=EIGHT),
-                           in_=along[:].rearrange("p (j s r) -> p j s r", j=4, r=EIGHT))
-        sums = keep.tile([P, N // SEG, WIDE], F32, name="sums")
-        nc.gpsimd.tensor_copy(out=sums[:, :, SEG:], in_=im_col[:].unsqueeze(2).to_broadcast([P, N // SEG, WIDE - SEG]))
-        turned, bias_cols = {}, {}
+            nc.scalar.copy(
+                out=bias_rows[:, h * HALF:(h + 1) * HALF].rearrange("p (s j r) -> p j s r", j=QUARTERS, r=QUARTER),
+                in_=along[:].rearrange("p (j s r) -> p j s r", j=QUARTERS, r=QUARTER))
 
-        k_all = keep.tile([P, N, PACK], BF16, name="k_all", tag="k_bf0", align_bytes=64)
-        k_bf = [k_all[:, c0:c1, :] for c0, c1 in PIECES]
-        k_codes = [keep.tile([P, c1 - c0], U32, name="k_codes%d" % c0, align_bytes=64) for c0, c1 in PIECES]
-        k_scales = [keep.tile([P, c1 - c0], U8, name="k_scales%d" % c0, align_bytes=64) for c0, c1 in PIECES]
+        sums = keep.tile([P, N // SEG, ROW], F32, name="sums", align_bytes=DMA_ALIGN)
+        nc.gpsimd.tensor_copy(out=sums[:, :, SEG:SEG + 1], in_=im_col[:].unsqueeze(2).to_broadcast([P, N // SEG, 1]))
 
-        def weave(n, t0, t1, listed):
-            c0, c1 = PIECES[n]
-            copy = nc.vector.tensor_copy if n in ON_VECTOR else nc.scalar.copy
-            if n in PAIRS:
-                copy(out=k_bf[n][:, :, t0:t1].rearrange("p (j s r) t -> p j s r t", j=2, r=RUN),
-                     in_=listed[:, :, c0:c1].rearrange("p t (s j r) -> p j s r t", j=2, r=RUN))
-            else:
-                copy(out=k_bf[n][:, :, t0:t1], in_=listed[:, :, c0:c1].rearrange("p t c -> p c t"))
+        words = keep.tile([P, N, PACK], BF16, name="words", tag="words", align_bytes=DMA_ALIGN)
+        k_codes = [keep.tile([P, c1 - c0], U32, name="k_codes%d" % c0, align_bytes=DMA_ALIGN) for c0, c1 in PIECES]
+        k_scales = [keep.tile([P, c1 - c0], U8, name="k_scales%d" % c0, align_bytes=MX_ALIGN) for c0, c1 in PIECES]
 
-        def quantise(n):
-            nc.vector.quantize_mx(out=k_codes[n][:].bitcast(FP8X4), scales=k_scales[n][:],
-                                  in_=k_bf[n].rearrange("p c t -> p (c t)"))
+        def interleave(piece, t0, t1, gathered):
+            c0, c1 = PIECES[piece]
+            copy = nc.vector.tensor_copy if piece in ON_VECTOR else nc.scalar.copy
+            copy(out=words[:, c0:c1, t0:t1], in_=gathered[:, :, c0:c1].rearrange("p t c -> p c t"))
 
-        listed = keep.tile([P, 2, N], F32, name="listed_early", tag="listed")
-        for h in range(2):
+        gathered = keep.tile([P, 2, N], F32, name="gathered01", tag="staging")
+        for c0 in (0, HALF):
             for t in range(2):
-                nc.vector.tensor_copy(out=listed[:, t, h * HALF:(h + 1) * HALF],
-                                      in_=early[:, t, :].indirect(offsets[:, h * HALF // 16:(h + 1) * HALF // 16]))
+                nc.vector.tensor_copy(out=gathered[:, t, c0:c0 + HALF], in_=listed(planes01[:, t, :], c0, c0 + HALF))
         for piece in range(len(PIECES)):
-            weave(piece, 0, 2, listed)
+            interleave(piece, 0, 2, gathered)
 
-        def gather(plane, tag, order):
-            listed = keep.tile([P, 1, N], BF16, name="listed_" + tag, tag=tag, align_bytes=256)
-            for c0, c1 in [GATHERS[n] for n in order]:
-                nc.vector.tensor_copy(out=listed[:, 0, c0:c1], in_=plane[:].indirect(offsets[:, c0 // 16:c1 // 16]))
-            return listed
+        def gather(plane, behind, order):
+            staged = keep.tile([P, 1, N], BF16, name="gathered_behind_" + behind, tag=behind, align_bytes=DMA_ALIGN)
+            for n in order:
+                c0, c1 = GATHERS[n]
+                nc.vector.tensor_copy(out=staged[:, 0, c0:c1], in_=listed(plane[:], c0, c1))
+            return staged
 
-        listed = gather(third, "early", (0, 1, 3, 2))
+        gathered = gather(plane2, "planes01", (0, 1, 3, 2))
         for piece in range(len(PIECES)):
-            weave(piece, 2, 3, listed)
-        listed = gather(last, "third", range(len(GATHERS)))
+            interleave(piece, 2, 3, gathered)
+        gathered = gather(plane3, "plane2", range(len(GATHERS)))
 
-        q_bf = keep.tile([P, NQ, PACK], BF16, name="q_bf", align_bytes=64)
-        q_codes = keep.tile([P, NQ], U32, name="q_codes", align_bytes=64)
-        q_scales = keep.tile([P, NQ], U8, name="q_scales", align_bytes=64)
-        score, second, first, best = {}, {}, {}, {}
-        free = 0
-        for piece, (c0, c1) in enumerate(PIECES):
-            if piece in PAIRS:
-                score[piece] = turned[piece][:, 3 * P:]
-                second[piece] = bank(free, "second%d" % piece)[:, 0:P]
-                first[piece] = keep.tile([P, NQ], F32, name="first%d" % piece)
-                best[piece] = keep.tile([P, NQ], F32, name="best%d" % piece)
-            else:
-                score[piece] = bank(free, "score%d" % piece)[:, 0:c1 - c0]
-            free = free + 1
-        result = keep.tile([P, N // SEG], F32, name="result")
+        q_words = keep.tile([P, NQ, PACK], BF16, name="q_words", align_bytes=DMA_ALIGN)
+        q_codes = keep.tile([P, NQ], U32, name="q_codes", align_bytes=DMA_ALIGN)
+        q_scales = keep.tile([P, NQ], U8, name="q_scales", align_bytes=MX_ALIGN)
+        scores = [bank(piece, "scores%d" % piece)[:, 0:c1 - c0] for piece, (c0, c1) in enumerate(PIECES)]
+        result = keep.tile([P, N // SEG], F32, name="result", align_bytes=DMA_ALIGN)
 
-        def multiply(n):
-            if n in PAIRS:
-                for j, dst in enumerate((score[n], second[n])):
-                    cols = slice(j * P, (j + 1) * P)
-                    nc.tensor.matmul_mx(out=dst, lhsT=k_codes[n][:, cols].bitcast(FP8X4), lhsT_scale=k_scales[n][:, cols],
-                                        rhs=q_codes[:].bitcast(FP8X4), rhs_scale=q_scales[:], start=True, stop=True)
-            else:
-                nc.tensor.matmul_mx(out=score[n], lhsT=q_codes[:].bitcast(FP8X4), lhsT_scale=q_scales[:],
-                                    rhs=k_codes[n][:].bitcast(FP8X4), rhs_scale=k_scales[n][:], start=True, stop=True)
+        for piece in ON_SCALAR:
+            interleave(piece, 3, 4, gathered)
+            if piece == ON_SCALAR[0]:
+                nc.gpsimd.tensor_scalar(out=q_words[:], in0=q_raw[:].rearrange("p t q -> p q t"),
+                                        scalar1=1.0, scalar2=0.0, op0=ALU.mult, op1=ALU.add)
 
-        def add(n):
-            c0, c1 = PIECES[n]
-            if n in PAIRS:
-                j = 2 * PAIRS.index(n)
-                nc.scalar.activation(out=first[n][:], in_=score[n], func=ACT.Identity, bias=bias_cols[:, j:j + 1])
-                nc.vector.scalar_tensor_tensor(out=best[n][:], in0=second[n], scalar=bias_cols[:, j + 1:j + 2],
-                                               in1=first[n][:], op0=ALU.add, op1=ALU.max)
-                view = turned[n][:, 0:8 * NARROW].rearrange("p (s r) -> p s r", r=NARROW)
-                nc.tensor.transpose(view[:, :, 0:RUN], best[n][:], ident[:])
-            else:
-                nc.vector.tensor_tensor(out=sums[:, c0 // SEG:c1 // SEG, 0:SEG],
-                                        in0=score[n].rearrange("p (s r) -> p s r", r=SEG),
-                                        in1=bias_listed[:, c0:c1].rearrange("p (s r) -> p s r", r=SEG), op=ALU.add)
+        for n, piece in enumerate(FINISH):
+            c0, c1 = PIECES[piece]
+            nc.vector.quantize_mx(out=k_codes[piece][:].bitcast(FP8X4), scales=k_scales[piece][:],
+                                  in_=words[:, c0:c1, :].rearrange("p c t -> p (c t)"))
+            if n == 0:
+                nc.vector.quantize_mx(out=q_codes[:].bitcast(FP8X4), scales=q_scales[:],
+                                      in_=q_words[:].rearrange("p q t -> p (q t)"))
+            nc.tensor.matmul_mx(out=scores[piece], lhsT=q_codes[:].bitcast(FP8X4), lhsT_scale=q_scales[:],
+                                rhs=k_codes[piece][:].bitcast(FP8X4), rhs_scale=k_scales[piece][:],
+                                start=True, stop=True)
+            if n < len(ON_VECTOR):
+                interleave(ON_VECTOR[n], 3, 4, gathered)
 
-        def reduce(n):
-            c0, c1 = PIECES[n]
-            if n in PAIRS:
-                view = turned[n][:, 0:8 * NARROW].rearrange("p (s r) -> p s r", r=NARROW)[:, :, 0:RUN + 1]
-            else:
-                view = sums[:, c0 // SEG:c1 // SEG, 0:SEG + 1]
-            nc.vector.tensor_reduce(out=result[:, c0 // SEG:c1 // SEG], in_=view, axis=AXES.X, op=ALU.max)
+        def add_bias(piece):
+            c0, c1 = PIECES[piece]
+            nc.vector.tensor_tensor(out=sums[:, c0 // SEG:c1 // SEG, 0:SEG],
+                                    in0=scores[piece].rearrange("p (s i) -> p s i", i=SEG),
+                                    in1=bias_rows[:, c0:c1].rearrange("p (s i) -> p s i", i=SEG), op=ALU.add)
 
-        weave(0, PACK - 1, PACK, listed)
-        nc.gpsimd.tensor_scalar(out=q_bf[:], in0=q_raw[:].rearrange("p t q -> p q t"), scalar1=1.0, scalar2=0.0,
-                                op0=ALU.mult, op1=ALU.add)
-        weave(1, PACK - 1, PACK, listed)
-        weave(2, PACK - 1, PACK, listed)
-        quantise(0)
-        nc.vector.quantize_mx(out=q_codes[:].bitcast(FP8X4), scales=q_scales[:],
-                              in_=q_bf[:].rearrange("p q t -> p (q t)"))
-        multiply(0)
-        weave(3, PACK - 1, PACK, listed)
-        quantise(1)
-        multiply(1)
-        weave(4, PACK - 1, PACK, listed)
-        quantise(3)
-        multiply(3)
-        quantise(2)
-        multiply(2)
-        quantise(4)
-        multiply(4)
-        add(0)
-        add(1)
-        reduce(0)
-        add(3)
-        reduce(1)
-        add(2)
-        reduce(3)
-        add(4)
-        reduce(2)
-        reduce(4)
+        add_bias(FINISH[0])
+        for n, piece in enumerate(FINISH):
+            if n + 1 < len(FINISH):
+                add_bias(FINISH[n + 1])
+            c0, c1 = PIECES[piece]
+            nc.vector.tensor_reduce(out=result[:, c0 // SEG:c1 // SEG], in_=sums[:, c0 // SEG:c1 // SEG, 0:SEG + 1],
+                                    axis=AXES.X, op=ALU.max)
         nc.sync.dma_start(out=out[0], in_=result[:])

@@ -25,11 +25,11 @@ QUARTERS, QUARTER = 4, 8
 VECTOR_PAGES = 80
 ROW = SEG + 8
 
-PIECES = ((0, 128), (128, 384), (384, 640), (640, 896), (896, 1024))
-ON_VECTOR = (3, 4)
-ON_SCALAR = (0, 1, 2)
-GATHERS = ((0, 128), (128, 384), (384, 640), (640, 1024))
-FINISH = (0, 1, 3, 2, 4)
+PIECES = ((0, 128), (128, 384), (384, 640), (768, 1024), (640, 768))
+ON_VECTOR = (3,)
+ON_SCALAR = (0, 1, 2, 4)
+GATHERS = ((0, 128), (128, 384), (768, 1024), (384, 768))
+BY_GPSIMD = 1
 
 FLOPS = 2 * D * NQ * N
 BYTES = 4 * (D * NQ + D * T + T + NQ + NQ * N // SEG) + 2 * P * N // 16
@@ -49,7 +49,7 @@ def tile_attend_xtr_f_kernel(tc, qT, kT, kb, im, offs, out):
 
         offsets = keep.tile([P, N // PER_COLUMN], U16, name="offsets")
         bias_pages = keep.tile([P, SEG], F32, name="bias_pages")
-        q_raw = keep.tile([P, PACK, NQ], F32, name="q_raw", align_bytes=DMA_ALIGN)
+        q_raw = keep.tile([P, PACK, NQ], F32, name="q_raw", tag="q_raw", align_bytes=DMA_ALIGN)
         im_col = keep.tile([P, 1], F32, name="im_col")
         k_rows = kT.rearrange("(p t) w -> p t w", t=PACK)
         planes01 = keep.tile([P, 2, T], F32, name="planes01", tag="planes01", align_bytes=DMA_ALIGN)
@@ -57,11 +57,11 @@ def tile_attend_xtr_f_kernel(tc, qT, kT, kb, im, offs, out):
         plane3 = keep.tile([P, T], F32, name="plane3", align_bytes=DMA_ALIGN)
         nc.sync.dma_start(offsets[:], offs)
         nc.scalar.dma_start(out=bias_pages[:], in_=kb[0].rearrange("(g i) -> g i", i=SEG))
-        nc.scalar.dma_start(out=im_col[:], in_=im[0])
         nc.sync.dma_start(out=planes01[:], in_=k_rows[:, 0:2, :])
         nc.sync.dma_start(out=plane2[:], in_=k_rows[:, 2, :])
         nc.sync.dma_start(out=plane3[:], in_=k_rows[:, 3, :])
         nc.sync.dma_start(out=q_raw[:], in_=qT[0].rearrange("(p t) q -> p t q", t=PACK))
+        nc.sync.dma_start(out=im_col[:], in_=im[0])
 
         ident = keep.tile([P, P], F32, name="ident")
         make_identity(nc, ident[:])
@@ -93,21 +93,17 @@ def tile_attend_xtr_f_kernel(tc, qT, kT, kb, im, offs, out):
             nc.tensor.transpose(down[:, h * P:(h + 1) * P], bias_used[:, h * P:(h + 1) * P], ident[:])
         bias_down = keep.tile([P, 2, QUARTERS], F32, name="bias_down", tag="words", align_bytes=DMA_ALIGN)
         nc.scalar.copy(out=bias_down[:], in_=down[:, 0:2 * P].rearrange("p (h n) -> p h n", h=2)[:, :, 0:QUARTERS])
-        bias_rows = keep.tile([P, N], F32, name="bias_rows", align_bytes=DMA_ALIGN)
+        rows = keep.tile([P, N // SEG, ROW], F32, name="rows", align_bytes=DMA_ALIGN)
         for h in range(2):
             along = bank(3 + h, "along%d" % h)
             for j in range(QUARTERS):
                 nc.tensor.transpose(along[:, j * P:(j + 1) * P], bias_down[:, h, j:j + 1].to_broadcast([P, P]), ident[:])
             nc.scalar.copy(
-                out=bias_rows[:, h * HALF:(h + 1) * HALF].rearrange("p (s j r) -> p j s r", j=QUARTERS, r=QUARTER),
+                out=rows[:, h * (HALF // SEG):(h + 1) * (HALF // SEG), 0:SEG].rearrange("p s (j r) -> p j s r", r=QUARTER),
                 in_=along[:].rearrange("p (j s r) -> p j s r", j=QUARTERS, r=QUARTER))
-
-        sums = keep.tile([P, N // SEG, ROW], F32, name="sums", align_bytes=DMA_ALIGN)
-        nc.gpsimd.tensor_copy(out=sums[:, :, SEG:SEG + 1], in_=im_col[:].unsqueeze(2).to_broadcast([P, N // SEG, 1]))
 
         words = keep.tile([P, N, PACK], BF16, name="words", tag="words", align_bytes=DMA_ALIGN)
         k_codes = [keep.tile([P, c1 - c0], U32, name="k_codes%d" % c0, align_bytes=DMA_ALIGN) for c0, c1 in PIECES]
-        k_scales = [keep.tile([P, c1 - c0], U8, name="k_scales%d" % c0, align_bytes=MX_ALIGN) for c0, c1 in PIECES]
 
         def interleave(piece, t0, t1, gathered):
             c0, c1 = PIECES[piece]
@@ -128,47 +124,79 @@ def tile_attend_xtr_f_kernel(tc, qT, kT, kb, im, offs, out):
                 nc.vector.tensor_copy(out=staged[:, 0, c0:c1], in_=listed(plane[:], c0, c1))
             return staged
 
-        gathered = gather(plane2, "planes01", (0, 1, 3, 2))
+        gathered = gather(plane2, "planes01", (0, 1, 2, 3))
         for piece in range(len(PIECES)):
             interleave(piece, 2, 3, gathered)
-        gathered = gather(plane3, "plane2", range(len(GATHERS)))
+        gathered = gather(plane3, "plane2", (0, 1, 3, 2))
 
-        q_words = keep.tile([P, NQ, PACK], BF16, name="q_words", align_bytes=DMA_ALIGN)
+        q_words = keep.tile([P, NQ, PACK], BF16, name="q_words", tag="q_words", align_bytes=DMA_ALIGN)
         q_codes = keep.tile([P, NQ], U32, name="q_codes", align_bytes=DMA_ALIGN)
         q_scales = keep.tile([P, NQ], U8, name="q_scales", align_bytes=MX_ALIGN)
         scores = [bank(piece, "scores%d" % piece)[:, 0:c1 - c0] for piece, (c0, c1) in enumerate(PIECES)]
         result = keep.tile([P, N // SEG], F32, name="result", align_bytes=DMA_ALIGN)
+        g0, g1 = PIECES[BY_GPSIMD]
+        copied = keep.tile([P, (g1 - g0) // SEG, ROW], F32, name="copied", align_bytes=DMA_ALIGN)
+        nc.gpsimd.memset(copied[:, :, SEG:SEG + 1], 0.0)
 
         for piece in ON_SCALAR:
             interleave(piece, 3, 4, gathered)
             if piece == ON_SCALAR[0]:
                 nc.gpsimd.tensor_scalar(out=q_words[:], in0=q_raw[:].rearrange("p t q -> p q t"),
                                         scalar1=1.0, scalar2=0.0, op0=ALU.mult, op1=ALU.add)
+        nc.scalar.copy(out=rows[:, :, SEG:SEG + 1], in_=im_col[:].unsqueeze(2).to_broadcast([P, N // SEG, 1]))
 
-        for n, piece in enumerate(FINISH):
+        first_scales = keep.tile([P, PIECES[0][1]], U8, name="first_scales", tag="first_scales", align_bytes=MX_ALIGN)
+
+        def quantise(piece, scales):
             c0, c1 = PIECES[piece]
-            nc.vector.quantize_mx(out=k_codes[piece][:].bitcast(FP8X4), scales=k_scales[piece][:],
+            nc.vector.quantize_mx(out=k_codes[piece][:].bitcast(FP8X4), scales=scales,
                                   in_=words[:, c0:c1, :].rearrange("p c t -> p (c t)"))
-            if n == 0:
-                nc.vector.quantize_mx(out=q_codes[:].bitcast(FP8X4), scales=q_scales[:],
-                                      in_=q_words[:].rearrange("p q t -> p (q t)"))
+
+        def multiply(piece, scales):
+            c0, c1 = PIECES[piece]
             nc.tensor.matmul_mx(out=scores[piece], lhsT=q_codes[:].bitcast(FP8X4), lhsT_scale=q_scales[:],
-                                rhs=k_codes[piece][:].bitcast(FP8X4), rhs_scale=k_scales[piece][:],
+                                rhs=k_codes[piece][:].bitcast(FP8X4), rhs_scale=scales,
                                 start=True, stop=True)
-            if n < len(ON_VECTOR):
-                interleave(ON_VECTOR[n], 3, 4, gathered)
+
+        def passages(tile, piece, width):
+            c0, c1 = PIECES[piece]
+            return tile[:, c0 // SEG:c1 // SEG, 0:width]
 
         def add_bias(piece):
-            c0, c1 = PIECES[piece]
-            nc.vector.tensor_tensor(out=sums[:, c0 // SEG:c1 // SEG, 0:SEG],
-                                    in0=scores[piece].rearrange("p (s i) -> p s i", i=SEG),
-                                    in1=bias_rows[:, c0:c1].rearrange("p (s i) -> p s i", i=SEG), op=ALU.add)
+            nc.vector.tensor_tensor(out=passages(rows, piece, SEG), in0=scores[piece].rearrange("p (s i) -> p s i", i=SEG),
+                                    in1=passages(rows, piece, SEG), op=ALU.add)
 
-        add_bias(FINISH[0])
-        for n, piece in enumerate(FINISH):
-            if n + 1 < len(FINISH):
-                add_bias(FINISH[n + 1])
+        def largest(piece, sums):
             c0, c1 = PIECES[piece]
-            nc.vector.tensor_reduce(out=result[:, c0 // SEG:c1 // SEG], in_=sums[:, c0 // SEG:c1 // SEG, 0:SEG + 1],
-                                    axis=AXES.X, op=ALU.max)
+            nc.vector.tensor_reduce(out=result[:, c0 // SEG:c1 // SEG], in_=sums, axis=AXES.X, op=ALU.max)
+
+        quantise(0, first_scales[:])
+        nc.vector.quantize_mx(out=q_codes[:].bitcast(FP8X4), scales=q_scales[:],
+                              in_=q_words[:].rearrange("p q t -> p (q t)"))
+        multiply(0, first_scales[:])
+        later_scales = keep.tile([P, N], U8, name="later_scales", tag="q_raw", align_bytes=DMA_ALIGN)
+
+        interleave(3, 3, 4, gathered)
+        quantise(1, later_scales[:, PIECES[1][0]:PIECES[1][1]])
+        multiply(1, later_scales[:, PIECES[1][0]:PIECES[1][1]])
+        nc.scalar.copy(out=copied[:, :, 0:SEG], in_=scores[BY_GPSIMD].rearrange("p (s i) -> p s i", i=SEG))
+        quantise(3, later_scales[:, PIECES[3][0]:PIECES[3][1]])
+        multiply(3, later_scales[:, PIECES[3][0]:PIECES[3][1]])
+        quantise(2, later_scales[:, PIECES[2][0]:PIECES[2][1]])
+        multiply(2, later_scales[:, PIECES[2][0]:PIECES[2][1]])
+        add_bias(0)
+        last_scales = keep.tile([P, PIECES[4][1] - PIECES[4][0]], U8, name="last_scales", tag="first_scales", align_bytes=MX_ALIGN)
+        quantise(4, last_scales[:])
+        multiply(4, last_scales[:])
+        g_sums = keep.tile([P, (g1 - g0) // SEG, ROW], F32, name="g_sums", tag="words", align_bytes=DMA_ALIGN)
+        nc.gpsimd.tensor_tensor(out=g_sums[:, :, 0:SEG + 1], in0=copied[:, :, 0:SEG + 1],
+                                in1=passages(rows, BY_GPSIMD, SEG + 1), op=ALU.add)
+        largest(0, passages(rows, 0, SEG + 1))
+        add_bias(3)
+        add_bias(2)
+        largest(3, passages(rows, 3, SEG + 1))
+        add_bias(4)
+        largest(2, passages(rows, 2, SEG + 1))
+        largest(BY_GPSIMD, g_sums[:, :, 0:SEG + 1])
+        largest(4, passages(rows, 4, SEG + 1))
         nc.sync.dma_start(out=out[0], in_=result[:])

@@ -57,11 +57,11 @@ def tile_attend_xtr_f_kernel(tc, qT, kT, kb, im, offs, out):
         plane3 = keep.tile([P, T], F32, name="plane3", align_bytes=DMA_ALIGN)
         nc.sync.dma_start(offsets[:], offs)
         nc.scalar.dma_start(out=bias_pages[:], in_=kb[0].rearrange("(g i) -> g i", i=SEG))
+        nc.scalar.dma_start(out=im_col[:], in_=im[0])
         nc.sync.dma_start(out=planes01[:], in_=k_rows[:, 0:2, :])
         nc.sync.dma_start(out=plane2[:], in_=k_rows[:, 2, :])
         nc.sync.dma_start(out=plane3[:], in_=k_rows[:, 3, :])
         nc.sync.dma_start(out=q_raw[:], in_=qT[0].rearrange("(p t) q -> p t q", t=PACK))
-        nc.sync.dma_start(out=im_col[:], in_=im[0])
 
         ident = keep.tile([P, P], F32, name="ident")
         make_identity(nc, ident[:])
@@ -101,6 +101,8 @@ def tile_attend_xtr_f_kernel(tc, qT, kT, kb, im, offs, out):
             nc.scalar.copy(
                 out=rows[:, h * (HALF // SEG):(h + 1) * (HALF // SEG), 0:SEG].rearrange("p s (j r) -> p j s r", r=QUARTER),
                 in_=along[:].rearrange("p (j s r) -> p j s r", j=QUARTERS, r=QUARTER))
+
+        nc.gpsimd.tensor_copy(out=rows[:, :, SEG:SEG + 1], in_=im_col[:].unsqueeze(2).to_broadcast([P, N // SEG, 1]))
 
         words = keep.tile([P, N, PACK], BF16, name="words", tag="words", align_bytes=DMA_ALIGN)
         k_codes = [keep.tile([P, c1 - c0], U32, name="k_codes%d" % c0, align_bytes=DMA_ALIGN) for c0, c1 in PIECES]
@@ -143,7 +145,6 @@ def tile_attend_xtr_f_kernel(tc, qT, kT, kb, im, offs, out):
             if piece == ON_SCALAR[0]:
                 nc.gpsimd.tensor_scalar(out=q_words[:], in0=q_raw[:].rearrange("p t q -> p q t"),
                                         scalar1=1.0, scalar2=0.0, op0=ALU.mult, op1=ALU.add)
-        nc.scalar.copy(out=rows[:, :, SEG:SEG + 1], in_=im_col[:].unsqueeze(2).to_broadcast([P, N // SEG, 1]))
 
         first_scales = keep.tile([P, PIECES[0][1]], U8, name="first_scales", tag="first_scales", align_bytes=MX_ALIGN)
 

@@ -29,7 +29,6 @@ PIECES = ((0, 128), (128, 384), (384, 640), (768, 1024), (640, 768))
 ON_VECTOR = (3,)
 ON_SCALAR = (0, 1, 2, 4)
 GATHERS = ((0, 128), (128, 384), (768, 1024), (384, 768))
-BY_GPSIMD = 1
 
 FLOPS = 2 * D * NQ * N
 BYTES = 4 * (D * NQ + D * T + T + NQ + NQ * N // SEG) + 2 * P * N // 16
@@ -134,11 +133,9 @@ def tile_attend_xtr_f_kernel(tc, qT, kT, kb, im, offs, out):
         q_words = keep.tile([P, NQ, PACK], BF16, name="q_words", tag="q_words", align_bytes=DMA_ALIGN)
         q_codes = keep.tile([P, NQ], U32, name="q_codes", align_bytes=DMA_ALIGN)
         q_scales = keep.tile([P, NQ], U8, name="q_scales", align_bytes=MX_ALIGN)
-        scores = [bank(piece, "scores%d" % piece)[:, 0:c1 - c0] for piece, (c0, c1) in enumerate(PIECES)]
+        banks = [bank(b, "scores%d" % b) for b in range(4)]
+        scores = [banks[b][:, at:at + c1 - c0] for (b, at), (c0, c1) in zip(((0, 0), (1, 0), (2, 0), (3, 0), (2, 256)), PIECES)]
         result = keep.tile([P, N // SEG], F32, name="result", align_bytes=DMA_ALIGN)
-        g0, g1 = PIECES[BY_GPSIMD]
-        copied = keep.tile([P, (g1 - g0) // SEG, ROW], F32, name="copied", align_bytes=DMA_ALIGN)
-        nc.gpsimd.memset(copied[:, :, SEG:SEG + 1], 0.0)
 
         for piece in ON_SCALAR:
             interleave(piece, 3, 4, gathered)
@@ -159,45 +156,35 @@ def tile_attend_xtr_f_kernel(tc, qT, kT, kb, im, offs, out):
                                 rhs=k_codes[piece][:].bitcast(FP8X4), rhs_scale=scales,
                                 start=True, stop=True)
 
-        def passages(tile, piece, width):
-            c0, c1 = PIECES[piece]
-            return tile[:, c0 // SEG:c1 // SEG, 0:width]
+        def add_bias(b, c0, c1):
+            sums = rows[:, c0 // SEG:c1 // SEG, 0:SEG]
+            nc.vector.tensor_tensor(out=sums, in0=banks[b][:, 0:c1 - c0].rearrange("p (s i) -> p s i", i=SEG),
+                                    in1=sums, op=ALU.add)
 
-        def add_bias(piece):
-            nc.vector.tensor_tensor(out=passages(rows, piece, SEG), in0=scores[piece].rearrange("p (s i) -> p s i", i=SEG),
-                                    in1=passages(rows, piece, SEG), op=ALU.add)
-
-        def largest(piece, sums):
-            c0, c1 = PIECES[piece]
-            nc.vector.tensor_reduce(out=result[:, c0 // SEG:c1 // SEG], in_=sums, axis=AXES.X, op=ALU.max)
+        def largest(c0, c1):
+            nc.vector.tensor_reduce(out=result[:, c0 // SEG:c1 // SEG], in_=rows[:, c0 // SEG:c1 // SEG, 0:SEG + 1],
+                                    axis=AXES.X, op=ALU.max)
 
         quantise(0, first_scales[:])
         nc.vector.quantize_mx(out=q_codes[:].bitcast(FP8X4), scales=q_scales[:],
                               in_=q_words[:].rearrange("p q t -> p (q t)"))
         multiply(0, first_scales[:])
         later_scales = keep.tile([P, N], U8, name="later_scales", tag="q_raw", align_bytes=DMA_ALIGN)
-
         interleave(3, 3, 4, gathered)
         quantise(1, later_scales[:, PIECES[1][0]:PIECES[1][1]])
         multiply(1, later_scales[:, PIECES[1][0]:PIECES[1][1]])
-        nc.scalar.copy(out=copied[:, :, 0:SEG], in_=scores[BY_GPSIMD].rearrange("p (s i) -> p s i", i=SEG))
         quantise(3, later_scales[:, PIECES[3][0]:PIECES[3][1]])
         multiply(3, later_scales[:, PIECES[3][0]:PIECES[3][1]])
         quantise(2, later_scales[:, PIECES[2][0]:PIECES[2][1]])
         multiply(2, later_scales[:, PIECES[2][0]:PIECES[2][1]])
-        add_bias(0)
+        add_bias(0, 0, 128)
         last_scales = keep.tile([P, PIECES[4][1] - PIECES[4][0]], U8, name="last_scales", tag="first_scales", align_bytes=MX_ALIGN)
         quantise(4, last_scales[:])
         multiply(4, last_scales[:])
-        g_sums = keep.tile([P, (g1 - g0) // SEG, ROW], F32, name="g_sums", tag="words", align_bytes=DMA_ALIGN)
-        nc.gpsimd.tensor_tensor(out=g_sums[:, :, 0:SEG + 1], in0=copied[:, :, 0:SEG + 1],
-                                in1=passages(rows, BY_GPSIMD, SEG + 1), op=ALU.add)
-        largest(0, passages(rows, 0, SEG + 1))
-        add_bias(3)
-        add_bias(2)
-        largest(3, passages(rows, 3, SEG + 1))
-        add_bias(4)
-        largest(2, passages(rows, 2, SEG + 1))
-        largest(BY_GPSIMD, g_sums[:, :, 0:SEG + 1])
-        largest(4, passages(rows, 4, SEG + 1))
+        add_bias(1, 128, 384)
+        add_bias(3, 768, 1024)
+        largest(0, 384)
+        add_bias(2, 384, 768)
+        largest(768, 1024)
+        largest(384, 768)
         nc.sync.dma_start(out=out[0], in_=result[:])

@@ -111,24 +111,19 @@ def tile_attend_xtr_f_kernel(tc, qT, kT, kb, im, offs, out):
             copy = nc.vector.tensor_copy if piece in ON_VECTOR else nc.scalar.copy
             copy(out=words[:, c0:c1, t0:t1], in_=gathered[:, :, c0:c1].rearrange("p t c -> p c t"))
 
-        gathered = keep.tile([P, 2, N], F32, name="gathered01", tag="staging")
+        gathered = keep.tile([P, 3, N], F32, name="gathered012", tag="staging")
         for c0 in (0, HALF):
             for t in range(2):
                 nc.vector.tensor_copy(out=gathered[:, t, c0:c0 + HALF], in_=listed(planes01[:, t, :], c0, c0 + HALF))
+        for c0 in (0, HALF):
+            nc.vector.tensor_copy(out=gathered[:, 2, c0:c0 + HALF], in_=listed(plane2[:], c0, c0 + HALF))
         for piece in range(len(PIECES)):
-            interleave(piece, 0, 2, gathered)
+            interleave(piece, 0, 3, gathered)
 
-        def gather(plane, behind, order):
-            staged = keep.tile([P, 1, N], BF16, name="gathered_behind_" + behind, tag=behind, align_bytes=DMA_ALIGN)
-            for n in order:
-                c0, c1 = GATHERS[n]
-                nc.vector.tensor_copy(out=staged[:, 0, c0:c1], in_=listed(plane[:], c0, c1))
-            return staged
-
-        gathered = gather(plane2, "planes01", (0, 1, 2, 3))
-        for piece in range(len(PIECES)):
-            interleave(piece, 2, 3, gathered)
-        gathered = gather(plane3, "plane2", (0, 1, 3, 2))
+        gathered = keep.tile([P, 1, N], BF16, name="gathered3", tag="plane2", align_bytes=DMA_ALIGN)
+        for n in (0, 1, 3, 2):
+            c0, c1 = GATHERS[n]
+            nc.vector.tensor_copy(out=gathered[:, 0, c0:c1], in_=listed(plane3[:], c0, c1))
 
         q_words = keep.tile([P, NQ, PACK], BF16, name="q_words", tag="q_words", align_bytes=DMA_ALIGN)
         q_codes = keep.tile([P, NQ], U32, name="q_codes", align_bytes=DMA_ALIGN)

@@ -26,8 +26,8 @@ VECTOR_PAGES = 80
 ROW = SEG + 8
 
 PIECES = ((0, 128), (128, 384), (384, 640), (768, 1024), (640, 768))
-ON_VECTOR = (3,)
-ON_SCALAR = (0, 1, 2, 4)
+SCALAR_COPIES = ((0, 128), (128, 384), (384, 640), (640, 768))
+VECTOR_COPY = (768, 1024)
 GATHERS = ((0, 128), (128, 384), (768, 1024), (384, 768))
 
 FLOPS = 2 * D * NQ * N
@@ -106,9 +106,8 @@ def tile_attend_xtr_f_kernel(tc, qT, kT, kb, im, offs, out):
         words = keep.tile([P, N, PACK], BF16, name="words", tag="words", align_bytes=DMA_ALIGN)
         k_codes = [keep.tile([P, c1 - c0], U32, name="k_codes%d" % c0, align_bytes=DMA_ALIGN) for c0, c1 in PIECES]
 
-        def interleave(piece, t0, t1, gathered):
-            c0, c1 = PIECES[piece]
-            copy = nc.vector.tensor_copy if piece in ON_VECTOR else nc.scalar.copy
+        def interleave(copy, span, t0, t1, gathered):
+            c0, c1 = span
             copy(out=words[:, c0:c1, t0:t1], in_=gathered[:, :, c0:c1].rearrange("p t c -> p c t"))
 
         gathered = keep.tile([P, 3, N], F32, name="gathered012", tag="staging")
@@ -117,12 +116,12 @@ def tile_attend_xtr_f_kernel(tc, qT, kT, kb, im, offs, out):
                 nc.vector.tensor_copy(out=gathered[:, t, c0:c0 + HALF], in_=listed(planes01[:, t, :], c0, c0 + HALF))
         for c0 in (0, HALF):
             nc.vector.tensor_copy(out=gathered[:, 2, c0:c0 + HALF], in_=listed(plane2[:], c0, c0 + HALF))
-        for piece in range(len(PIECES)):
-            interleave(piece, 0, 3, gathered)
+        for span in SCALAR_COPIES:
+            interleave(nc.scalar.copy, span, 0, 3, gathered)
+        interleave(nc.vector.tensor_copy, VECTOR_COPY, 0, 3, gathered)
 
         gathered = keep.tile([P, 1, N], BF16, name="gathered3", tag="plane2", align_bytes=DMA_ALIGN)
-        for n in (0, 1, 3, 2):
-            c0, c1 = GATHERS[n]
+        for c0, c1 in GATHERS:
             nc.vector.tensor_copy(out=gathered[:, 0, c0:c1], in_=listed(plane3[:], c0, c1))
 
         q_words = keep.tile([P, NQ, PACK], BF16, name="q_words", tag="q_words", align_bytes=DMA_ALIGN)
@@ -132,9 +131,9 @@ def tile_attend_xtr_f_kernel(tc, qT, kT, kb, im, offs, out):
         scores = [banks[b][:, at:at + c1 - c0] for (b, at), (c0, c1) in zip(((0, 0), (1, 0), (2, 0), (3, 0), (2, 256)), PIECES)]
         result = keep.tile([P, N // SEG], F32, name="result", align_bytes=DMA_ALIGN)
 
-        for piece in ON_SCALAR:
-            interleave(piece, 3, 4, gathered)
-            if piece == ON_SCALAR[0]:
+        for span in SCALAR_COPIES:
+            interleave(nc.scalar.copy, span, 3, 4, gathered)
+            if span == SCALAR_COPIES[0]:
                 nc.gpsimd.tensor_scalar(out=q_words[:], in0=q_raw[:].rearrange("p t q -> p q t"),
                                         scalar1=1.0, scalar2=0.0, op0=ALU.mult, op1=ALU.add)
 
@@ -165,7 +164,7 @@ def tile_attend_xtr_f_kernel(tc, qT, kT, kb, im, offs, out):
                               in_=q_words[:].rearrange("p q t -> p (q t)"))
         multiply(0, first_scales[:])
         later_scales = keep.tile([P, N], U8, name="later_scales", tag="q_raw", align_bytes=DMA_ALIGN)
-        interleave(3, 3, 4, gathered)
+        interleave(nc.vector.tensor_copy, VECTOR_COPY, 3, 4, gathered)
         quantise(1, later_scales[:, PIECES[1][0]:PIECES[1][1]])
         multiply(1, later_scales[:, PIECES[1][0]:PIECES[1][1]])
         quantise(3, later_scales[:, PIECES[3][0]:PIECES[3][1]])

@@ -25,10 +25,10 @@ QUARTERS, QUARTER = 4, 8
 VECTOR_PAGES = 80
 ROW = SEG + 8
 
-PIECES = ((0, 128), (128, 384), (384, 640), (768, 1024), (640, 768))
-SCALAR_COPIES = ((0, 128), (128, 384), (384, 640), (640, 768))
-VECTOR_COPY = (768, 1024)
-GATHERS = ((0, 128), (128, 384), (768, 1024), (384, 768))
+FIRST, SECOND, THIRD, LAST = (0, 128), (128, 384), (384, 640), (640, 768)
+OWN = (768, 1024)
+ON_SCALAR = (FIRST, SECOND, THIRD, LAST)
+GATHERS = (FIRST, SECOND, OWN, (THIRD[0], LAST[1]))
 
 FLOPS = 2 * D * NQ * N
 BYTES = 4 * (D * NQ + D * T + T + NQ + NQ * N // SEG) + 2 * P * N // 16
@@ -51,13 +51,13 @@ def tile_attend_xtr_f_kernel(tc, qT, kT, kb, im, offs, out):
         q_raw = keep.tile([P, PACK, NQ], F32, name="q_raw", tag="q_raw", align_bytes=DMA_ALIGN)
         im_col = keep.tile([P, 1], F32, name="im_col")
         k_rows = kT.rearrange("(p t) w -> p t w", t=PACK)
-        planes01 = keep.tile([P, 2, T], F32, name="planes01", tag="planes01", align_bytes=DMA_ALIGN)
-        plane2 = keep.tile([P, T], F32, name="plane2", tag="plane2", align_bytes=DMA_ALIGN)
+        planes01 = keep.tile([P, 2, T], F32, name="planes01", align_bytes=DMA_ALIGN)
+        plane2 = keep.tile([P, T], F32, name="plane2", align_bytes=DMA_ALIGN)
         plane3 = keep.tile([P, T], F32, name="plane3", align_bytes=DMA_ALIGN)
-        nc.sync.dma_start(offsets[:], offs)
         nc.scalar.dma_start(out=bias_pages[:], in_=kb[0].rearrange("(g i) -> g i", i=SEG))
         nc.scalar.dma_start(out=im_col[:], in_=im[0])
         nc.sync.dma_start(out=planes01[:], in_=k_rows[:, 0:2, :])
+        nc.sync.dma_start(offsets[:], offs)
         nc.sync.dma_start(out=plane2[:], in_=k_rows[:, 2, :])
         nc.sync.dma_start(out=plane3[:], in_=k_rows[:, 3, :])
         nc.sync.dma_start(out=q_raw[:], in_=qT[0].rearrange("(p t) q -> p t q", t=PACK))
@@ -90,95 +90,95 @@ def tile_attend_xtr_f_kernel(tc, qT, kT, kb, im, offs, out):
         down = bank(2, "down")
         for h in range(2):
             nc.tensor.transpose(down[:, h * P:(h + 1) * P], bias_used[:, h * P:(h + 1) * P], ident[:])
-        bias_down = keep.tile([P, 2, QUARTERS], F32, name="bias_down", tag="words", align_bytes=DMA_ALIGN)
+        bias_down = keep.tile([P, 2, QUARTERS], F32, name="bias_down")
         nc.scalar.copy(out=bias_down[:], in_=down[:, 0:2 * P].rearrange("p (h n) -> p h n", h=2)[:, :, 0:QUARTERS])
         rows = keep.tile([P, N // SEG, ROW], F32, name="rows", align_bytes=DMA_ALIGN)
+
+        def passages(c0, c1, width):
+            return rows[:, c0 // SEG:c1 // SEG, 0:width]
+
         for h in range(2):
             along = bank(3 + h, "along%d" % h)
             for j in range(QUARTERS):
                 nc.tensor.transpose(along[:, j * P:(j + 1) * P], bias_down[:, h, j:j + 1].to_broadcast([P, P]), ident[:])
-            nc.scalar.copy(
-                out=rows[:, h * (HALF // SEG):(h + 1) * (HALF // SEG), 0:SEG].rearrange("p s (j r) -> p j s r", r=QUARTER),
-                in_=along[:].rearrange("p (j s r) -> p j s r", j=QUARTERS, r=QUARTER))
-
+            nc.scalar.copy(out=passages(h * HALF, (h + 1) * HALF, SEG).rearrange("p s (j r) -> p j s r", r=QUARTER),
+                           in_=along[:].rearrange("p (j s r) -> p j s r", j=QUARTERS, r=QUARTER))
         nc.gpsimd.tensor_copy(out=rows[:, :, SEG:SEG + 1], in_=im_col[:].unsqueeze(2).to_broadcast([P, N // SEG, 1]))
 
-        words = keep.tile([P, N, PACK], BF16, name="words", tag="words", align_bytes=DMA_ALIGN)
-        k_codes = [keep.tile([P, c1 - c0], U32, name="k_codes%d" % c0, align_bytes=DMA_ALIGN) for c0, c1 in PIECES]
+        words = keep.tile([P, N, PACK], BF16, name="words", align_bytes=DMA_ALIGN)
+        k_codes = {piece: keep.tile([P, piece[1] - piece[0]], U32, name="k_codes%d" % piece[0], align_bytes=DMA_ALIGN)
+                   for piece in (FIRST, SECOND, THIRD, OWN, LAST)}
 
-        def interleave(copy, span, t0, t1, gathered):
-            c0, c1 = span
+        def interleave(copy, piece, t0, t1, gathered):
+            c0, c1 = piece
             copy(out=words[:, c0:c1, t0:t1], in_=gathered[:, :, c0:c1].rearrange("p t c -> p c t"))
 
-        gathered = keep.tile([P, 3, N], F32, name="gathered012", tag="staging")
+        early = keep.tile([P, PACK - 1, N], F32, name="early", tag="staging")
         for c0 in (0, HALF):
             for t in range(2):
-                nc.vector.tensor_copy(out=gathered[:, t, c0:c0 + HALF], in_=listed(planes01[:, t, :], c0, c0 + HALF))
-        for c0 in (0, HALF):
-            nc.vector.tensor_copy(out=gathered[:, 2, c0:c0 + HALF], in_=listed(plane2[:], c0, c0 + HALF))
-        for span in SCALAR_COPIES:
-            interleave(nc.scalar.copy, span, 0, 3, gathered)
-        interleave(nc.vector.tensor_copy, VECTOR_COPY, 0, 3, gathered)
+                nc.vector.tensor_copy(out=early[:, t, c0:c0 + HALF], in_=listed(planes01[:, t, :], c0, c0 + HALF))
+        for c0 in (HALF, 0):
+            nc.vector.tensor_copy(out=early[:, 2, c0:c0 + HALF], in_=listed(plane2[:], c0, c0 + HALF))
+        interleave(nc.vector.tensor_copy, (HALF, N), 0, PACK - 1, early)
+        interleave(nc.scalar.copy, (0, HALF), 0, PACK - 1, early)
 
-        gathered = keep.tile([P, 1, N], BF16, name="gathered3", tag="plane2", align_bytes=DMA_ALIGN)
+        late = keep.tile([P, 1, N], BF16, name="late", align_bytes=DMA_ALIGN)
         for c0, c1 in GATHERS:
-            nc.vector.tensor_copy(out=gathered[:, 0, c0:c1], in_=listed(plane3[:], c0, c1))
+            nc.vector.tensor_copy(out=late[:, 0, c0:c1], in_=listed(plane3[:], c0, c1))
 
-        q_words = keep.tile([P, NQ, PACK], BF16, name="q_words", tag="q_words", align_bytes=DMA_ALIGN)
+        q_words = keep.tile([P, NQ, PACK], BF16, name="q_words", align_bytes=DMA_ALIGN)
         q_codes = keep.tile([P, NQ], U32, name="q_codes", align_bytes=DMA_ALIGN)
         q_scales = keep.tile([P, NQ], U8, name="q_scales", align_bytes=MX_ALIGN)
-        banks = [bank(b, "scores%d" % b) for b in range(4)]
-        scores = [banks[b][:, at:at + c1 - c0] for (b, at), (c0, c1) in zip(((0, 0), (1, 0), (2, 0), (3, 0), (2, 256)), PIECES)]
+        both = (THIRD[0], LAST[1])
+        runs = {run: bank(b, "scores%d" % b)[:, 0:run[1] - run[0]] for b, run in enumerate((FIRST, SECOND, both, OWN))}
+        scores = {FIRST: runs[FIRST], SECOND: runs[SECOND], OWN: runs[OWN],
+                  THIRD: runs[both][:, 0:THIRD[1] - THIRD[0]], LAST: runs[both][:, THIRD[1] - THIRD[0]:]}
         result = keep.tile([P, N // SEG], F32, name="result", align_bytes=DMA_ALIGN)
 
-        for span in SCALAR_COPIES:
-            interleave(nc.scalar.copy, span, 3, 4, gathered)
-            if span == SCALAR_COPIES[0]:
-                nc.gpsimd.tensor_scalar(out=q_words[:], in0=q_raw[:].rearrange("p t q -> p q t"),
-                                        scalar1=1.0, scalar2=0.0, op0=ALU.mult, op1=ALU.add)
-
-        first_scales = keep.tile([P, PIECES[0][1]], U8, name="first_scales", tag="first_scales", align_bytes=MX_ALIGN)
+        interleave(nc.scalar.copy, FIRST, PACK - 1, PACK, late)
+        nc.gpsimd.tensor_scalar(out=q_words[:], in0=q_raw[:].rearrange("p t q -> p q t"),
+                                scalar1=1.0, scalar2=0.0, op0=ALU.mult, op1=ALU.add)
+        for piece in ON_SCALAR[1:]:
+            interleave(nc.scalar.copy, piece, PACK - 1, PACK, late)
 
         def quantise(piece, scales):
-            c0, c1 = PIECES[piece]
+            c0, c1 = piece
             nc.vector.quantize_mx(out=k_codes[piece][:].bitcast(FP8X4), scales=scales,
                                   in_=words[:, c0:c1, :].rearrange("p c t -> p (c t)"))
 
         def multiply(piece, scales):
-            c0, c1 = PIECES[piece]
             nc.tensor.matmul_mx(out=scores[piece], lhsT=q_codes[:].bitcast(FP8X4), lhsT_scale=q_scales[:],
-                                rhs=k_codes[piece][:].bitcast(FP8X4), rhs_scale=scales,
-                                start=True, stop=True)
+                                rhs=k_codes[piece][:].bitcast(FP8X4), rhs_scale=scales, start=True, stop=True)
 
-        def add_bias(b, c0, c1):
-            sums = rows[:, c0 // SEG:c1 // SEG, 0:SEG]
-            nc.vector.tensor_tensor(out=sums, in0=banks[b][:, 0:c1 - c0].rearrange("p (s i) -> p s i", i=SEG),
-                                    in1=sums, op=ALU.add)
+        def add_scores(run):
+            sums = passages(run[0], run[1], SEG)
+            nc.vector.tensor_tensor(out=sums, in0=runs[run].rearrange("p (s i) -> p s i", i=SEG), in1=sums, op=ALU.add)
 
         def largest(c0, c1):
-            nc.vector.tensor_reduce(out=result[:, c0 // SEG:c1 // SEG], in_=rows[:, c0 // SEG:c1 // SEG, 0:SEG + 1],
+            nc.vector.tensor_reduce(out=result[:, c0 // SEG:c1 // SEG], in_=passages(c0, c1, SEG + 1),
                                     axis=AXES.X, op=ALU.max)
 
-        quantise(0, first_scales[:])
+        first_scales = keep.tile([P, FIRST[1]], U8, name="first_scales", tag="first_scales", align_bytes=MX_ALIGN)
+        quantise(FIRST, first_scales[:])
         nc.vector.quantize_mx(out=q_codes[:].bitcast(FP8X4), scales=q_scales[:],
                               in_=q_words[:].rearrange("p q t -> p (q t)"))
-        multiply(0, first_scales[:])
+        multiply(FIRST, first_scales[:])
+
         later_scales = keep.tile([P, N], U8, name="later_scales", tag="q_raw", align_bytes=DMA_ALIGN)
-        interleave(nc.vector.tensor_copy, VECTOR_COPY, 3, 4, gathered)
-        quantise(1, later_scales[:, PIECES[1][0]:PIECES[1][1]])
-        multiply(1, later_scales[:, PIECES[1][0]:PIECES[1][1]])
-        quantise(3, later_scales[:, PIECES[3][0]:PIECES[3][1]])
-        multiply(3, later_scales[:, PIECES[3][0]:PIECES[3][1]])
-        quantise(2, later_scales[:, PIECES[2][0]:PIECES[2][1]])
-        multiply(2, later_scales[:, PIECES[2][0]:PIECES[2][1]])
-        add_bias(0, 0, 128)
-        last_scales = keep.tile([P, PIECES[4][1] - PIECES[4][0]], U8, name="last_scales", tag="first_scales", align_bytes=MX_ALIGN)
-        quantise(4, last_scales[:])
-        multiply(4, last_scales[:])
-        add_bias(1, 128, 384)
-        add_bias(3, 768, 1024)
-        largest(0, 384)
-        add_bias(2, 384, 768)
-        largest(768, 1024)
-        largest(384, 768)
+        interleave(nc.vector.tensor_copy, OWN, PACK - 1, PACK, late)
+        for piece in (SECOND, OWN, THIRD):
+            quantise(piece, later_scales[:, piece[0]:piece[1]])
+            multiply(piece, later_scales[:, piece[0]:piece[1]])
+
+        add_scores(FIRST)
+        last_scales = keep.tile([P, LAST[1] - LAST[0]], U8, name="last_scales", tag="first_scales", align_bytes=MX_ALIGN)
+        quantise(LAST, last_scales[:])
+        multiply(LAST, last_scales[:])
+
+        add_scores(SECOND)
+        add_scores(OWN)
+        largest(FIRST[0], SECOND[1])
+        add_scores(both)
+        largest(*OWN)
+        largest(*both)
         nc.sync.dma_start(out=out[0], in_=result[:])

@@ -25,10 +25,11 @@ QUARTERS, QUARTER = 4, 8
 VECTOR_PAGES = 80
 ROW = SEG + 8
 
-FIRST, SECOND, THIRD, LAST = (0, 128), (128, 384), (384, 640), (640, 768)
+FRONT = (0, 256)
 OWN = (768, 1024)
-ON_SCALAR = (FIRST, SECOND, THIRD, LAST)
-GATHERS = (FIRST, SECOND, OWN, (THIRD[0], LAST[1]))
+PLAIN = (256, 768)
+GATHERS = ((0, 128), (128, 512), OWN, (512, 768))
+PLAIN_PIECES = ((256, 512), (512, 640), (640, 768))
 
 FLOPS = 2 * D * NQ * N
 BYTES = 4 * (D * NQ + D * T + T + NQ + NQ * N // SEG) + 2 * P * N // 16
@@ -56,8 +57,8 @@ def tile_attend_xtr_f_kernel(tc, qT, kT, kb, im, offs, out):
         plane3 = keep.tile([P, T], F32, name="plane3", align_bytes=DMA_ALIGN)
         nc.scalar.dma_start(out=bias_pages[:], in_=kb[0].rearrange("(g i) -> g i", i=SEG))
         nc.scalar.dma_start(out=im_col[:], in_=im[0])
-        nc.sync.dma_start(out=planes01[:], in_=k_rows[:, 0:2, :])
         nc.sync.dma_start(offsets[:], offs)
+        nc.sync.dma_start(out=planes01[:], in_=k_rows[:, 0:2, :])
         nc.sync.dma_start(out=plane2[:], in_=k_rows[:, 2, :])
         nc.sync.dma_start(out=plane3[:], in_=k_rows[:, 3, :])
         nc.sync.dma_start(out=q_raw[:], in_=qT[0].rearrange("(p t) q -> p t q", t=PACK))
@@ -85,33 +86,44 @@ def tile_attend_xtr_f_kernel(tc, qT, kT, kb, im, offs, out):
         nc.vector.tensor_copy(out=bias_gathered[:], in_=listed(bias_window[:], 0, N))
 
         bias_used = keep.tile([P, 2 * P], F32, name="bias_used")
-        nc.scalar.copy(out=bias_used[:].rearrange("p (s r) -> p s r", r=QUARTER),
-                       in_=bias_gathered[:].rearrange("p (s i) -> p s i", i=SEG)[:, :, 0:QUARTER])
+        by_passage = bias_gathered[:].rearrange("p (a s i) -> p a s i", a=4, i=SEG)
+        used = bias_used[:].rearrange("p (a s r) -> p a s r", a=4, r=QUARTER)
+        nc.scalar.copy(out=used[:, 0:2], in_=by_passage[:, 0:4:3, :, 0:QUARTER])
+        nc.scalar.copy(out=used[:, 2:4], in_=by_passage[:, 1:3, :, 0:QUARTER])
         down = bank(2, "down")
         for h in range(2):
             nc.tensor.transpose(down[:, h * P:(h + 1) * P], bias_used[:, h * P:(h + 1) * P], ident[:])
+        nc.tensor.transpose(down[:, 2 * P:3 * P], im_col[:].to_broadcast([P, P]), ident[:])
         bias_down = keep.tile([P, 2, QUARTERS], F32, name="bias_down")
         nc.scalar.copy(out=bias_down[:], in_=down[:, 0:2 * P].rearrange("p (h n) -> p h n", h=2)[:, :, 0:QUARTERS])
-        rows = keep.tile([P, N // SEG, ROW], F32, name="rows", align_bytes=DMA_ALIGN)
+        rows = keep.tile([P, HALF // SEG, ROW], F32, name="rows", align_bytes=DMA_ALIGN)
+        im_row = rows[:, 0:4, 0:SEG]
+        nc.scalar.copy(out=im_row, in_=down[:, 2 * P:3 * P].rearrange("p (s i) -> p s i", i=SEG))
+        bias_rows = keep.tile([P, HALF // SEG, SEG], F32, name="bias_rows", align_bytes=DMA_ALIGN)
+        kept = [keep.tile([P, NQ], F32, name="kept%d" % j, align_bytes=DMA_ALIGN) for j in range(QUARTERS)]
+        by_rows = [tile[:].rearrange("p (s i) -> p s i", i=SEG) for tile in kept]
 
-        def passages(c0, c1, width):
-            return rows[:, c0 // SEG:c1 // SEG, 0:width]
+        def passages(c0, c1, width, tile=rows):
+            return tile[:, (c0 - PLAIN[0]) // SEG:(c1 - PLAIN[0]) // SEG, 0:width]
 
-        for h in range(2):
-            along = bank(3 + h, "along%d" % h)
-            for j in range(QUARTERS):
-                nc.tensor.transpose(along[:, j * P:(j + 1) * P], bias_down[:, h, j:j + 1].to_broadcast([P, P]), ident[:])
-            nc.scalar.copy(out=passages(h * HALF, (h + 1) * HALF, SEG).rearrange("p s (j r) -> p j s r", r=QUARTER),
-                           in_=along[:].rearrange("p (j s r) -> p j s r", j=QUARTERS, r=QUARTER))
-        nc.gpsimd.tensor_copy(out=rows[:, :, SEG:SEG + 1], in_=im_col[:].unsqueeze(2).to_broadcast([P, N // SEG, 1]))
+        along = bank(3, "along")
+        for j in range(QUARTERS):
+            nc.tensor.transpose(along[:, j * P:(j + 1) * P], bias_down[:, 1, j:j + 1].to_broadcast([P, P]), ident[:])
+        nc.scalar.copy(out=bias_rows[:].rearrange("p s (j r) -> p j s r", r=QUARTER),
+                       in_=along[:].rearrange("p (j s r) -> p j s r", j=QUARTERS, r=QUARTER))
+        nc.gpsimd.tensor_copy(out=rows[:, :, SEG:SEG + 1], in_=im_col[:].unsqueeze(2).to_broadcast([P, HALF // SEG, 1]))
 
-        words = keep.tile([P, N, PACK], BF16, name="words", align_bytes=DMA_ALIGN)
-        k_codes = {piece: keep.tile([P, piece[1] - piece[0]], U32, name="k_codes%d" % piece[0], align_bytes=DMA_ALIGN)
-                   for piece in (FIRST, SECOND, THIRD, OWN, LAST)}
+        slab_words = keep.tile([P, HALF, PACK], BF16, name="slab_words", align_bytes=DMA_ALIGN)
+        plain_words = keep.tile([P, HALF, PACK], BF16, name="plain_words", align_bytes=DMA_ALIGN)
+        dealt = slab_words[:].rearrange("p (j s r) t -> p s j r t", j=QUARTERS, r=QUARTER)
 
-        def interleave(copy, piece, t0, t1, gathered):
-            c0, c1 = piece
-            copy(out=words[:, c0:c1, t0:t1], in_=gathered[:, :, c0:c1].rearrange("p t c -> p c t"))
+        def deal(copy, c0, c1, t0, t1, gathered):
+            s0 = (c0 if c0 < PLAIN[0] else c0 - HALF) // SEG
+            copy(out=dealt[:, s0:s0 + (c1 - c0) // SEG, :, :, t0:t1],
+                 in_=gathered[:, :, c0:c1].rearrange("p t (s j r) -> p s j r t", j=QUARTERS, r=QUARTER))
+
+        def interleave(copy, c0, c1, t0, t1, gathered):
+            copy(out=plain_words[:, c0 - PLAIN[0]:c1 - PLAIN[0], t0:t1], in_=gathered[:, :, c0:c1].rearrange("p t c -> p c t"))
 
         early = keep.tile([P, PACK - 1, N], F32, name="early", tag="staging")
         for c0 in (0, HALF):
@@ -119,8 +131,10 @@ def tile_attend_xtr_f_kernel(tc, qT, kT, kb, im, offs, out):
                 nc.vector.tensor_copy(out=early[:, t, c0:c0 + HALF], in_=listed(planes01[:, t, :], c0, c0 + HALF))
         for c0 in (HALF, 0):
             nc.vector.tensor_copy(out=early[:, 2, c0:c0 + HALF], in_=listed(plane2[:], c0, c0 + HALF))
-        interleave(nc.vector.tensor_copy, (HALF, N), 0, PACK - 1, early)
-        interleave(nc.scalar.copy, (0, HALF), 0, PACK - 1, early)
+        interleave(nc.vector.tensor_copy, HALF, PLAIN[1], 0, PACK - 1, early)
+        deal(nc.vector.tensor_copy, OWN[0], OWN[1], 0, PACK - 1, early)
+        deal(nc.scalar.copy, FRONT[0], FRONT[1], 0, PACK - 1, early)
+        interleave(nc.scalar.copy, PLAIN[0], HALF, 0, PACK - 1, early)
 
         late = keep.tile([P, 1, N], BF16, name="late", align_bytes=DMA_ALIGN)
         for c0, c1 in GATHERS:
@@ -129,56 +143,75 @@ def tile_attend_xtr_f_kernel(tc, qT, kT, kb, im, offs, out):
         q_words = keep.tile([P, NQ, PACK], BF16, name="q_words", align_bytes=DMA_ALIGN)
         q_codes = keep.tile([P, NQ], U32, name="q_codes", align_bytes=DMA_ALIGN)
         q_scales = keep.tile([P, NQ], U8, name="q_scales", align_bytes=MX_ALIGN)
-        both = (THIRD[0], LAST[1])
-        runs = {run: bank(b, "scores%d" % b)[:, 0:run[1] - run[0]] for b, run in enumerate((FIRST, SECOND, both, OWN))}
-        scores = {FIRST: runs[FIRST], SECOND: runs[SECOND], OWN: runs[OWN],
-                  THIRD: runs[both][:, 0:THIRD[1] - THIRD[0]], LAST: runs[both][:, THIRD[1] - THIRD[0]:]}
         result = keep.tile([P, N // SEG], F32, name="result", align_bytes=DMA_ALIGN)
 
-        interleave(nc.scalar.copy, FIRST, PACK - 1, PACK, late)
+        deal(nc.scalar.copy, 0, 128, PACK - 1, PACK, late)
         nc.gpsimd.tensor_scalar(out=q_words[:], in0=q_raw[:].rearrange("p t q -> p q t"),
                                 scalar1=1.0, scalar2=0.0, op0=ALU.mult, op1=ALU.add)
-        for piece in ON_SCALAR[1:]:
-            interleave(nc.scalar.copy, piece, PACK - 1, PACK, late)
+        deal(nc.scalar.copy, 128, 256, PACK - 1, PACK, late)
+        for c0, c1 in PLAIN_PIECES:
+            interleave(nc.scalar.copy, c0, c1, PACK - 1, PACK, late)
+        deal(nc.vector.tensor_copy, OWN[0], OWN[1], PACK - 1, PACK, late)
 
-        def quantise(piece, scales):
-            c0, c1 = piece
-            nc.vector.quantize_mx(out=k_codes[piece][:].bitcast(FP8X4), scales=scales,
-                                  in_=words[:, c0:c1, :].rearrange("p c t -> p (c t)"))
+        nc.vector.quantize_mx(out=q_codes[:].bitcast(FP8X4), scales=q_scales[:],
+                              in_=q_words[:].rearrange("p q t -> p (q t)"))
+        k_scales = keep.tile([P, N], U8, name="k_scales", tag="q_raw", align_bytes=DMA_ALIGN)
+        slab_codes = [keep.tile([P, 2 * P], U32, name="slab_codes%d" % h, tag="slab_codes%d" % h, align_bytes=DMA_ALIGN) for h in range(2)]
+        slab_scores = [bank(4 + h, "slab_scores%d" % h) for h in range(2)]
+        first_bank, second_bank = bank(6, "plain_scores0"), bank(7, "plain_scores1")
+        plain_scores = {256: first_bank[:, 0:256], 512: second_bank[:, 0:128], 640: second_bank[:, 128:256]}
+        runs = {256: first_bank[:, 0:256], 512: second_bank[:, 0:256]}
 
-        def multiply(piece, scales):
-            nc.tensor.matmul_mx(out=scores[piece], lhsT=q_codes[:].bitcast(FP8X4), lhsT_scale=q_scales[:],
-                                rhs=k_codes[piece][:].bitcast(FP8X4), rhs_scale=scales, start=True, stop=True)
+        def slab_pair(h):
+            scales = k_scales[:, 2 * P * h:2 * P * (h + 1)]
+            nc.vector.quantize_mx(out=slab_codes[h][:].bitcast(FP8X4), scales=scales,
+                                  in_=slab_words[:, 2 * P * h:2 * P * (h + 1), :].rearrange("p c t -> p (c t)"))
+            for n in range(2):
+                nc.tensor.matmul_mx(out=slab_scores[h][:, n * NQ:(n + 1) * NQ],
+                                    lhsT=slab_codes[h][:, n * P:(n + 1) * P].bitcast(FP8X4),
+                                    lhsT_scale=scales[:, n * P:(n + 1) * P],
+                                    rhs=q_codes[:].bitcast(FP8X4), rhs_scale=q_scales[:], start=True, stop=True)
 
-        def add_scores(run):
-            sums = passages(run[0], run[1], SEG)
-            nc.vector.tensor_tensor(out=sums, in0=runs[run].rearrange("p (s i) -> p s i", i=SEG), in1=sums, op=ALU.add)
+        plain_codes = {}
+
+        def plain_piece(c0, c1):
+            plain_codes[c0] = keep.tile([P, c1 - c0], U32, name="plain_codes%d" % c0, align_bytes=DMA_ALIGN,
+                                        tag={256: "plain_codes0", 512: "plain_codes1", 640: "slab_codes0"}[c0])
+            scales = k_scales[:, c0 + 256:c1 + 256]
+            nc.vector.quantize_mx(out=plain_codes[c0][:].bitcast(FP8X4), scales=scales,
+                                  in_=plain_words[:, c0 - PLAIN[0]:c1 - PLAIN[0], :].rearrange("p c t -> p (c t)"))
+            nc.tensor.matmul_mx(out=plain_scores[c0], lhsT=q_codes[:].bitcast(FP8X4), lhsT_scale=q_scales[:],
+                                rhs=plain_codes[c0][:].bitcast(FP8X4), rhs_scale=scales, start=True, stop=True)
+
+        def keep_larger(j):
+            nc.vector.scalar_tensor_tensor(out=by_rows[j], in0=slab_scores[j // 2][:, (j % 2) * NQ:(j % 2 + 1) * NQ].rearrange("p (s i) -> p s i", i=SEG),
+                                           scalar=bias_down[:, 0, j:j + 1], in1=im_row if j < 2 else by_rows[j - 2], op0=ALU.add, op1=ALU.max)
+
+        def add_scores(c0, c1):
+            sums = passages(c0, c1, SEG)
+            nc.vector.tensor_tensor(out=sums, in0=runs[c0].rearrange("p (s i) -> p s i", i=SEG), in1=passages(c0, c1, SEG, bias_rows), op=ALU.add)
 
         def largest(c0, c1):
             nc.vector.tensor_reduce(out=result[:, c0 // SEG:c1 // SEG], in_=passages(c0, c1, SEG + 1),
                                     axis=AXES.X, op=ALU.max)
 
-        first_scales = keep.tile([P, FIRST[1]], U8, name="first_scales", tag="first_scales", align_bytes=MX_ALIGN)
-        quantise(FIRST, first_scales[:])
-        nc.vector.quantize_mx(out=q_codes[:].bitcast(FP8X4), scales=q_scales[:],
-                              in_=q_words[:].rearrange("p q t -> p (q t)"))
-        multiply(FIRST, first_scales[:])
-
-        later_scales = keep.tile([P, N], U8, name="later_scales", tag="q_raw", align_bytes=DMA_ALIGN)
-        interleave(nc.vector.tensor_copy, OWN, PACK - 1, PACK, late)
-        for piece in (SECOND, OWN, THIRD):
-            quantise(piece, later_scales[:, piece[0]:piece[1]])
-            multiply(piece, later_scales[:, piece[0]:piece[1]])
-
-        add_scores(FIRST)
-        last_scales = keep.tile([P, LAST[1] - LAST[0]], U8, name="last_scales", tag="first_scales", align_bytes=MX_ALIGN)
-        quantise(LAST, last_scales[:])
-        multiply(LAST, last_scales[:])
-
-        add_scores(SECOND)
-        add_scores(OWN)
-        largest(FIRST[0], SECOND[1])
-        add_scores(both)
-        largest(*OWN)
-        largest(*both)
+        slab_pair(0)
+        slab_pair(1)
+        plain_piece(*PLAIN_PIECES[0])
+        plain_piece(*PLAIN_PIECES[1])
+        keep_larger(0)
+        keep_larger(1)
+        plain_piece(*PLAIN_PIECES[2])
+        keep_larger(2)
+        keep_larger(3)
+        turned = bank(0, "turned")
+        for h in range(2):
+            nc.tensor.transpose(turned[:, h * P:(h + 1) * P], kept[2 + h][:], ident[:])
+        add_scores(256, 512)
+        add_scores(512, 768)
+        largest(256, 512)
+        largest(512, 768)
+        nc.vector.tensor_reduce(out=result[:].rearrange("p (a s) -> p a s", a=4)[:, 0:4:3, :],
+                                in_=turned[:, 0:2 * P].rearrange("p (h a s r) -> p a s h r", h=2, a=2, r=QUARTER),
+                                axis=AXES.XY, op=ALU.max)
         nc.sync.dma_start(out=out[0], in_=result[:])

@@ -25,11 +25,9 @@ QUARTERS, QUARTER = 4, 8
 VECTOR_PAGES = 80
 ROW = SEG + 8
 
-FRONT = (0, 256)
-OWN = (768, 1024)
-PLAIN = (256, 768)
+PAIR = 256
+THIRD, LAST, OWN = (512, 640), (640, 768), (768, 1024)
 GATHERS = ((0, 128), (128, 512), OWN, (512, 768))
-PLAIN_PIECES = ((256, 512), (512, 640), (640, 768))
 
 FLOPS = 2 * D * NQ * N
 BYTES = 4 * (D * NQ + D * T + T + NQ + NQ * N // SEG) + 2 * P * N // 16
@@ -85,56 +83,60 @@ def tile_attend_xtr_f_kernel(tc, qT, kT, kb, im, offs, out):
         bias_gathered = keep.tile([P, N], F32, name="bias_gathered")
         nc.vector.tensor_copy(out=bias_gathered[:], in_=listed(bias_window[:], 0, N))
 
-        bias_used = keep.tile([P, 2 * P], F32, name="bias_used")
-        by_passage = bias_gathered[:].rearrange("p (a s i) -> p a s i", a=4, i=SEG)
-        used = bias_used[:].rearrange("p (a s r) -> p a s r", a=4, r=QUARTER)
-        nc.scalar.copy(out=used[:, 0:2], in_=by_passage[:, 0:4:3, :, 0:QUARTER])
-        nc.scalar.copy(out=used[:, 2:4], in_=by_passage[:, 1:3, :, 0:QUARTER])
+        bias_used = keep.tile([P, 3 * P], F32, name="bias_used")
+        by_passage = bias_gathered[:].rearrange("p (a s i) -> p a s i", a=4, i=SEG)[:, :, :, 0:QUARTER]
+        nc.scalar.copy(out=bias_used[:, 0:2 * P].rearrange("p (a h s r) -> p a h s r", a=2, h=2, r=QUARTER),
+                       in_=by_passage[:, 0:2].unsqueeze(2).to_broadcast([P, 2, 2, 8, QUARTER]))
+        nc.scalar.copy(out=bias_used[:, 2 * P:].rearrange("p (a s r) -> p a s r", a=2, r=QUARTER), in_=by_passage[:, 2:4])
         down = bank(2, "down")
-        for h in range(2):
+        for h in range(3):
             nc.tensor.transpose(down[:, h * P:(h + 1) * P], bias_used[:, h * P:(h + 1) * P], ident[:])
-        nc.tensor.transpose(down[:, 2 * P:3 * P], im_col[:].to_broadcast([P, P]), ident[:])
-        bias_down = keep.tile([P, 2, QUARTERS], F32, name="bias_down")
-        nc.scalar.copy(out=bias_down[:], in_=down[:, 0:2 * P].rearrange("p (h n) -> p h n", h=2)[:, :, 0:QUARTERS])
+        nc.tensor.transpose(down[:, 3 * P:], im_col[:].to_broadcast([P, P]), ident[:])
+        by_block = down[:].rearrange("p (a n) -> p a n", a=4)
+        slab_bias = keep.tile([P, 2, 2], F32, name="slab_bias")
+        for h in range(2):
+            part = slice(h * P // 2, (h + 1) * P // 2)
+            nc.scalar.copy(out=slab_bias[part], in_=by_block[part, 0:2, h:QUARTERS:2])
+        bias_down = keep.tile([P, QUARTERS], F32, name="bias_down")
+        nc.scalar.copy(out=bias_down[:], in_=by_block[:, 2, 0:QUARTERS])
+        im_row = keep.tile([P, NQ], F32, name="im_row", align_bytes=DMA_ALIGN)
+        nc.scalar.copy(out=im_row[:], in_=by_block[:, 3, :])
         rows = keep.tile([P, HALF // SEG, ROW], F32, name="rows", align_bytes=DMA_ALIGN)
-        im_row = rows[:, 0:4, 0:SEG]
-        nc.scalar.copy(out=im_row, in_=down[:, 2 * P:3 * P].rearrange("p (s i) -> p s i", i=SEG))
-        bias_rows = keep.tile([P, HALF // SEG, SEG], F32, name="bias_rows", align_bytes=DMA_ALIGN)
-        kept = [keep.tile([P, NQ], F32, name="kept%d" % j, align_bytes=DMA_ALIGN) for j in range(QUARTERS)]
-        by_rows = [tile[:].rearrange("p (s i) -> p s i", i=SEG) for tile in kept]
 
-        def passages(c0, c1, width, tile=rows):
-            return tile[:, (c0 - PLAIN[0]) // SEG:(c1 - PLAIN[0]) // SEG, 0:width]
+        def passages(c0, c1, width):
+            return rows[:, (c0 - HALF) // SEG:(c1 - HALF) // SEG, 0:width]
 
         along = bank(3, "along")
         for j in range(QUARTERS):
-            nc.tensor.transpose(along[:, j * P:(j + 1) * P], bias_down[:, 1, j:j + 1].to_broadcast([P, P]), ident[:])
-        nc.scalar.copy(out=bias_rows[:].rearrange("p s (j r) -> p j s r", r=QUARTER),
+            nc.tensor.transpose(along[:, j * P:(j + 1) * P], bias_down[:, j:j + 1].to_broadcast([P, P]), ident[:])
+        nc.scalar.copy(out=passages(HALF, N, SEG).rearrange("p s (j r) -> p j s r", r=QUARTER),
                        in_=along[:].rearrange("p (j s r) -> p j s r", j=QUARTERS, r=QUARTER))
         nc.gpsimd.tensor_copy(out=rows[:, :, SEG:SEG + 1], in_=im_col[:].unsqueeze(2).to_broadcast([P, HALF // SEG, 1]))
 
-        slab_words = keep.tile([P, HALF, PACK], BF16, name="slab_words", align_bytes=DMA_ALIGN)
+        slab_words = [keep.tile([P, PAIR, PACK], BF16, name="slab_words%d" % a, align_bytes=DMA_ALIGN) for a in range(2)]
         plain_words = keep.tile([P, HALF, PACK], BF16, name="plain_words", align_bytes=DMA_ALIGN)
-        dealt = slab_words[:].rearrange("p (j s r) t -> p s j r t", j=QUARTERS, r=QUARTER)
 
-        def deal(copy, c0, c1, t0, t1, gathered):
-            s0 = (c0 if c0 < PLAIN[0] else c0 - HALF) // SEG
-            copy(out=dealt[:, s0:s0 + (c1 - c0) // SEG, :, :, t0:t1],
-                 in_=gathered[:, :, c0:c1].rearrange("p t (s j r) -> p s j r t", j=QUARTERS, r=QUARTER))
+        def deal(c0, c1, t0, t1, gathered):
+            dealt = slab_words[c0 // PAIR][:].rearrange("p (j s r) t -> p s j r t", j=QUARTERS, r=QUARTER)
+            s0 = c0 % PAIR // SEG
+            nc.scalar.copy(out=dealt[:, s0:s0 + (c1 - c0) // SEG, :, :, t0:t1],
+                           in_=gathered[:, :, c0:c1].rearrange("p t (s j r) -> p s j r t", j=QUARTERS, r=QUARTER))
 
-        def interleave(copy, c0, c1, t0, t1, gathered):
-            copy(out=plain_words[:, c0 - PLAIN[0]:c1 - PLAIN[0], t0:t1], in_=gathered[:, :, c0:c1].rearrange("p t c -> p c t"))
+        def interleave(copy, piece, t0, t1, gathered):
+            c0, c1 = piece
+            copy(out=plain_words[:, c0 - HALF:c1 - HALF, t0:t1], in_=gathered[:, :, c0:c1].rearrange("p t c -> p c t"))
 
+        zero = plain_words[:, OWN[0] - HALF, PACK - 1:PACK]
+        nc.vector.memset(zero, 0.0)
         early = keep.tile([P, PACK - 1, N], F32, name="early", tag="staging")
         for c0 in (0, HALF):
             for t in range(2):
                 nc.vector.tensor_copy(out=early[:, t, c0:c0 + HALF], in_=listed(planes01[:, t, :], c0, c0 + HALF))
         for c0 in (HALF, 0):
             nc.vector.tensor_copy(out=early[:, 2, c0:c0 + HALF], in_=listed(plane2[:], c0, c0 + HALF))
-        interleave(nc.vector.tensor_copy, HALF, PLAIN[1], 0, PACK - 1, early)
-        deal(nc.vector.tensor_copy, OWN[0], OWN[1], 0, PACK - 1, early)
-        deal(nc.scalar.copy, FRONT[0], FRONT[1], 0, PACK - 1, early)
-        interleave(nc.scalar.copy, PLAIN[0], HALF, 0, PACK - 1, early)
+        interleave(nc.vector.tensor_copy, (HALF, N), 0, PACK - 1, early)
+        for c0 in (0, PAIR):
+            deal(c0, c0 + PAIR, 0, PACK - 1, early)
 
         late = keep.tile([P, 1, N], BF16, name="late", align_bytes=DMA_ALIGN)
         for c0, c1 in GATHERS:
@@ -145,73 +147,75 @@ def tile_attend_xtr_f_kernel(tc, qT, kT, kb, im, offs, out):
         q_scales = keep.tile([P, NQ], U8, name="q_scales", align_bytes=MX_ALIGN)
         result = keep.tile([P, N // SEG], F32, name="result", align_bytes=DMA_ALIGN)
 
-        deal(nc.scalar.copy, 0, 128, PACK - 1, PACK, late)
+        deal(0, 128, PACK - 1, PACK, late)
         nc.gpsimd.tensor_scalar(out=q_words[:], in0=q_raw[:].rearrange("p t q -> p q t"),
-                                scalar1=1.0, scalar2=0.0, op0=ALU.mult, op1=ALU.add)
-        deal(nc.scalar.copy, 128, 256, PACK - 1, PACK, late)
-        for c0, c1 in PLAIN_PIECES:
-            interleave(nc.scalar.copy, c0, c1, PACK - 1, PACK, late)
-        deal(nc.vector.tensor_copy, OWN[0], OWN[1], PACK - 1, PACK, late)
+                                scalar1=1.0, scalar2=zero, op0=ALU.mult, op1=ALU.add)
+        deal(128, 256, PACK - 1, PACK, late)
+        deal(256, 512, PACK - 1, PACK, late)
+        for piece in (THIRD, LAST):
+            interleave(nc.scalar.copy, piece, PACK - 1, PACK, late)
 
-        nc.vector.quantize_mx(out=q_codes[:].bitcast(FP8X4), scales=q_scales[:],
-                              in_=q_words[:].rearrange("p q t -> p (q t)"))
-        k_scales = keep.tile([P, N], U8, name="k_scales", tag="q_raw", align_bytes=DMA_ALIGN)
-        slab_codes = [keep.tile([P, 2 * P], U32, name="slab_codes%d" % h, tag="slab_codes%d" % h, align_bytes=DMA_ALIGN) for h in range(2)]
-        slab_scores = [bank(4 + h, "slab_scores%d" % h) for h in range(2)]
-        first_bank, second_bank = bank(6, "plain_scores0"), bank(7, "plain_scores1")
-        plain_scores = {256: first_bank[:, 0:256], 512: second_bank[:, 0:128], 640: second_bank[:, 128:256]}
-        runs = {256: first_bank[:, 0:256], 512: second_bank[:, 0:256]}
+        slab_codes = [keep.tile([P, PAIR], U32, name="slab_codes%d" % a, tag="slab_codes%d" % a, align_bytes=DMA_ALIGN)
+                      for a in range(2)]
+        slab_scores = [bank(4 + a, "slab_scores%d" % a) for a in range(2)]
+        both = (THIRD[0], LAST[1])
+        runs = {both: bank(6, "scores_both")[:, 0:PAIR], OWN: bank(7, "scores_own")[:, 0:PAIR]}
+        scores = {THIRD: runs[both][:, 0:P], LAST: runs[both][:, P:], OWN: runs[OWN]}
+        kept = [[keep.tile([P, NQ], F32, name="kept%d%d" % (a, j), align_bytes=DMA_ALIGN) for j in range(2)] for a in range(2)]
 
-        def slab_pair(h):
-            scales = k_scales[:, 2 * P * h:2 * P * (h + 1)]
-            nc.vector.quantize_mx(out=slab_codes[h][:].bitcast(FP8X4), scales=scales,
-                                  in_=slab_words[:, 2 * P * h:2 * P * (h + 1), :].rearrange("p c t -> p (c t)"))
-            for n in range(2):
-                nc.tensor.matmul_mx(out=slab_scores[h][:, n * NQ:(n + 1) * NQ],
-                                    lhsT=slab_codes[h][:, n * P:(n + 1) * P].bitcast(FP8X4),
-                                    lhsT_scale=scales[:, n * P:(n + 1) * P],
+        def quantise(codes, scales, words):
+            nc.vector.quantize_mx(out=codes.bitcast(FP8X4), scales=scales, in_=words.rearrange("p c t -> p (c t)"))
+
+        def slabs(a, scales):
+            for j in range(2):
+                nc.tensor.matmul_mx(out=slab_scores[a][:, j * NQ:(j + 1) * NQ],
+                                    lhsT=slab_codes[a][:, j * P:(j + 1) * P].bitcast(FP8X4),
+                                    lhsT_scale=scales[:, j * P:(j + 1) * P],
                                     rhs=q_codes[:].bitcast(FP8X4), rhs_scale=q_scales[:], start=True, stop=True)
 
-        plain_codes = {}
+        def plain(piece, codes, scales):
+            quantise(codes, scales, plain_words[:, piece[0] - HALF:piece[1] - HALF, :])
+            nc.tensor.matmul_mx(out=scores[piece], lhsT=q_codes[:].bitcast(FP8X4), lhsT_scale=q_scales[:],
+                                rhs=codes.bitcast(FP8X4), rhs_scale=scales, start=True, stop=True)
 
-        def plain_piece(c0, c1):
-            plain_codes[c0] = keep.tile([P, c1 - c0], U32, name="plain_codes%d" % c0, align_bytes=DMA_ALIGN,
-                                        tag={256: "plain_codes0", 512: "plain_codes1", 640: "slab_codes0"}[c0])
-            scales = k_scales[:, c0 + 256:c1 + 256]
-            nc.vector.quantize_mx(out=plain_codes[c0][:].bitcast(FP8X4), scales=scales,
-                                  in_=plain_words[:, c0 - PLAIN[0]:c1 - PLAIN[0], :].rearrange("p c t -> p (c t)"))
-            nc.tensor.matmul_mx(out=plain_scores[c0], lhsT=q_codes[:].bitcast(FP8X4), lhsT_scale=q_scales[:],
-                                rhs=plain_codes[c0][:].bitcast(FP8X4), rhs_scale=scales, start=True, stop=True)
+        def keep_larger(a, j):
+            nc.vector.scalar_tensor_tensor(out=kept[a][j][:], in0=slab_scores[a][:, j * NQ:(j + 1) * NQ],
+                                           scalar=slab_bias[:, a, j:j + 1], in1=kept[a][0][:] if j else im_row[:],
+                                           op0=ALU.add, op1=ALU.max)
 
-        def keep_larger(j):
-            nc.vector.scalar_tensor_tensor(out=by_rows[j], in0=slab_scores[j // 2][:, (j % 2) * NQ:(j % 2 + 1) * NQ].rearrange("p (s i) -> p s i", i=SEG),
-                                           scalar=bias_down[:, 0, j:j + 1], in1=im_row if j < 2 else by_rows[j - 2], op0=ALU.add, op1=ALU.max)
-
-        def add_scores(c0, c1):
-            sums = passages(c0, c1, SEG)
-            nc.vector.tensor_tensor(out=sums, in0=runs[c0].rearrange("p (s i) -> p s i", i=SEG), in1=passages(c0, c1, SEG, bias_rows), op=ALU.add)
+        def add_scores(run):
+            sums = passages(run[0], run[1], SEG)
+            nc.vector.tensor_tensor(out=sums, in0=runs[run].rearrange("p (s i) -> p s i", i=SEG), in1=sums, op=ALU.add)
 
         def largest(c0, c1):
             nc.vector.tensor_reduce(out=result[:, c0 // SEG:c1 // SEG], in_=passages(c0, c1, SEG + 1),
                                     axis=AXES.X, op=ALU.max)
 
-        slab_pair(0)
-        slab_pair(1)
-        plain_piece(*PLAIN_PIECES[0])
-        plain_piece(*PLAIN_PIECES[1])
-        keep_larger(0)
-        keep_larger(1)
-        plain_piece(*PLAIN_PIECES[2])
-        keep_larger(2)
-        keep_larger(3)
+        first_scales = keep.tile([P, PAIR], U8, name="first_scales", align_bytes=MX_ALIGN)
+        quantise(slab_codes[0][:], first_scales[:], slab_words[0][:])
+        quantise(q_codes[:], q_scales[:], q_words[:])
+        slabs(0, first_scales[:])
+        later_scales = keep.tile([P, N], U8, name="later_scales", tag="q_raw", align_bytes=DMA_ALIGN)
+        interleave(nc.vector.tensor_copy, OWN, PACK - 1, PACK, late)
+        quantise(slab_codes[1][:], later_scales[:, PAIR:HALF], slab_words[1][:])
+        slabs(1, later_scales[:, PAIR:HALF])
+        own_codes = keep.tile([P, PAIR], U32, name="own_codes", align_bytes=DMA_ALIGN)
+        plain(OWN, own_codes[:], later_scales[:, OWN[0]:OWN[1]])
+        keep_larger(0, 0)
+        last_codes = keep.tile([P, PAIR], U32, name="last_codes", tag="slab_codes0", align_bytes=DMA_ALIGN)
+        plain(THIRD, last_codes[:, 0:P], later_scales[:, THIRD[0]:THIRD[1]])
+        plain(LAST, last_codes[:, P:], later_scales[:, LAST[0]:LAST[1]])
+        keep_larger(0, 1)
+        keep_larger(1, 0)
+        add_scores(OWN)
+        keep_larger(1, 1)
         turned = bank(0, "turned")
-        for h in range(2):
-            nc.tensor.transpose(turned[:, h * P:(h + 1) * P], kept[2 + h][:], ident[:])
-        add_scores(256, 512)
-        add_scores(512, 768)
-        largest(256, 512)
-        largest(512, 768)
-        nc.vector.tensor_reduce(out=result[:].rearrange("p (a s) -> p a s", a=4)[:, 0:4:3, :],
-                                in_=turned[:, 0:2 * P].rearrange("p (h a s r) -> p a s h r", h=2, a=2, r=QUARTER),
+        for a in range(2):
+            nc.tensor.transpose(turned[:, a * P:(a + 1) * P], kept[a][1][:], ident[:])
+        add_scores(both)
+        largest(*OWN)
+        largest(*both)
+        nc.vector.tensor_reduce(out=result[:, 0:HALF // SEG].rearrange("p (a s) -> p a s", a=2),
+                                in_=turned[:, 0:2 * P].rearrange("p (a h s r) -> p a s h r", a=2, h=2, r=QUARTER),
                                 axis=AXES.XY, op=ALU.max)
         nc.sync.dma_start(out=out[0], in_=result[:])

@@ -27,7 +27,7 @@ ROW = SEG + 8
 
 PAIR = 256
 THIRD, LAST, OWN = (512, 640), (640, 768), (768, 1024)
-GATHERS = ((0, 128), (128, 512), OWN, (512, 768))
+GATHERS = ((0, 128), (128, 384), (384, 768), OWN)
 
 FLOPS = 2 * D * NQ * N
 BYTES = 4 * (D * NQ + D * T + T + NQ + NQ * N // SEG) + 2 * P * N // 16

@@ -26,8 +26,8 @@ VECTOR_PAGES = 80
 ROW = SEG + 8
 
 PAIR = 256
-THIRD, LAST, OWN = (512, 640), (640, 768), (768, 1024)
-GATHERS = ((0, 128), (128, 384), (384, 768), OWN)
+SECOND, THIRD, LAST = (512, 768), (768, 896), (896, 1024)
+GATHERS = ((0, 128), (128, 256), (256, 768), (768, 1024))
 
 FLOPS = 2 * D * NQ * N
 BYTES = 4 * (D * NQ + D * T + T + NQ + NQ * N // SEG) + 2 * P * N // 16
@@ -116,27 +116,26 @@ def tile_attend_xtr_f_kernel(tc, qT, kT, kb, im, offs, out):
         slab_words = [keep.tile([P, PAIR, PACK], BF16, name="slab_words%d" % a, align_bytes=DMA_ALIGN) for a in range(2)]
         plain_words = keep.tile([P, HALF, PACK], BF16, name="plain_words", align_bytes=DMA_ALIGN)
 
-        def deal(c0, c1, t0, t1, gathered):
+        def deal(copy, c0, c1, t0, t1, gathered):
             dealt = slab_words[c0 // PAIR][:].rearrange("p (j s r) t -> p s j r t", j=QUARTERS, r=QUARTER)
             s0 = c0 % PAIR // SEG
-            nc.scalar.copy(out=dealt[:, s0:s0 + (c1 - c0) // SEG, :, :, t0:t1],
-                           in_=gathered[:, :, c0:c1].rearrange("p t (s j r) -> p s j r t", j=QUARTERS, r=QUARTER))
+            copy(out=dealt[:, s0:s0 + (c1 - c0) // SEG, :, :, t0:t1],
+                 in_=gathered[:, :, c0:c1].rearrange("p t (s j r) -> p s j r t", j=QUARTERS, r=QUARTER))
 
         def interleave(copy, piece, t0, t1, gathered):
             c0, c1 = piece
             copy(out=plain_words[:, c0 - HALF:c1 - HALF, t0:t1], in_=gathered[:, :, c0:c1].rearrange("p t c -> p c t"))
 
-        zero = plain_words[:, OWN[0] - HALF, PACK - 1:PACK]
-        nc.vector.memset(zero, 0.0)
         early = keep.tile([P, PACK - 1, N], F32, name="early", tag="staging")
         for c0 in (0, HALF):
             for t in range(2):
                 nc.vector.tensor_copy(out=early[:, t, c0:c0 + HALF], in_=listed(planes01[:, t, :], c0, c0 + HALF))
-        for c0 in (HALF, 0):
+        for c0 in (0, HALF):
             nc.vector.tensor_copy(out=early[:, 2, c0:c0 + HALF], in_=listed(plane2[:], c0, c0 + HALF))
-        interleave(nc.vector.tensor_copy, (HALF, N), 0, PACK - 1, early)
-        for c0 in (0, PAIR):
-            deal(c0, c0 + PAIR, 0, PACK - 1, early)
+        deal(nc.vector.tensor_copy, PAIR, HALF, 0, PACK - 1, early)
+        deal(nc.scalar.copy, 0, PAIR, 0, PACK - 1, early)
+        interleave(nc.vector.tensor_copy, SECOND, 0, PACK - 1, early)
+        interleave(nc.scalar.copy, (THIRD[0], N), 0, PACK - 1, early)
 
         late = keep.tile([P, 1, N], BF16, name="late", align_bytes=DMA_ALIGN)
         for c0, c1 in GATHERS:
@@ -147,20 +146,20 @@ def tile_attend_xtr_f_kernel(tc, qT, kT, kb, im, offs, out):
         q_scales = keep.tile([P, NQ], U8, name="q_scales", align_bytes=MX_ALIGN)
         result = keep.tile([P, N // SEG], F32, name="result", align_bytes=DMA_ALIGN)
 
-        deal(0, 128, PACK - 1, PACK, late)
+        deal(nc.vector.tensor_copy, PAIR, HALF, PACK - 1, PACK, late)
+        deal(nc.scalar.copy, 0, 128, PACK - 1, PACK, late)
         nc.gpsimd.tensor_scalar(out=q_words[:], in0=q_raw[:].rearrange("p t q -> p q t"),
-                                scalar1=1.0, scalar2=zero, op0=ALU.mult, op1=ALU.add)
-        deal(128, 256, PACK - 1, PACK, late)
-        deal(256, 512, PACK - 1, PACK, late)
-        for piece in (THIRD, LAST):
+                                scalar1=1.0, scalar2=0.0, op0=ALU.mult, op1=ALU.add)
+        deal(nc.scalar.copy, 128, 256, PACK - 1, PACK, late)
+        for piece in (SECOND, THIRD, LAST):
             interleave(nc.scalar.copy, piece, PACK - 1, PACK, late)
 
         slab_codes = [keep.tile([P, PAIR], U32, name="slab_codes%d" % a, tag="slab_codes%d" % a, align_bytes=DMA_ALIGN)
                       for a in range(2)]
         slab_scores = [bank(4 + a, "slab_scores%d" % a) for a in range(2)]
         both = (THIRD[0], LAST[1])
-        runs = {both: bank(6, "scores_both")[:, 0:PAIR], OWN: bank(7, "scores_own")[:, 0:PAIR]}
-        scores = {THIRD: runs[both][:, 0:P], LAST: runs[both][:, P:], OWN: runs[OWN]}
+        runs = {both: bank(6, "scores_both")[:, 0:PAIR], SECOND: bank(7, "scores_second")[:, 0:PAIR]}
+        scores = {THIRD: runs[both][:, 0:P], LAST: runs[both][:, P:], SECOND: runs[SECOND]}
         kept = [[keep.tile([P, NQ], F32, name="kept%d%d" % (a, j), align_bytes=DMA_ALIGN) for j in range(2)] for a in range(2)]
 
         def quantise(codes, scales, words):
@@ -196,24 +195,24 @@ def tile_attend_xtr_f_kernel(tc, qT, kT, kb, im, offs, out):
         quantise(q_codes[:], q_scales[:], q_words[:])
         slabs(0, first_scales[:])
         later_scales = keep.tile([P, N], U8, name="later_scales", tag="q_raw", align_bytes=DMA_ALIGN)
-        interleave(nc.vector.tensor_copy, OWN, PACK - 1, PACK, late)
         quantise(slab_codes[1][:], later_scales[:, PAIR:HALF], slab_words[1][:])
         slabs(1, later_scales[:, PAIR:HALF])
-        own_codes = keep.tile([P, PAIR], U32, name="own_codes", align_bytes=DMA_ALIGN)
-        plain(OWN, own_codes[:], later_scales[:, OWN[0]:OWN[1]])
+        second_codes = keep.tile([P, PAIR], U32, name="second_codes", align_bytes=DMA_ALIGN)
+        plain(SECOND, second_codes[:], later_scales[:, SECOND[0]:SECOND[1]])
+        third_codes = keep.tile([P, P], U32, name="third_codes", align_bytes=DMA_ALIGN)
+        plain(THIRD, third_codes[:], later_scales[:, THIRD[0]:THIRD[1]])
         keep_larger(0, 0)
-        last_codes = keep.tile([P, PAIR], U32, name="last_codes", tag="slab_codes0", align_bytes=DMA_ALIGN)
-        plain(THIRD, last_codes[:, 0:P], later_scales[:, THIRD[0]:THIRD[1]])
-        plain(LAST, last_codes[:, P:], later_scales[:, LAST[0]:LAST[1]])
-        keep_larger(0, 1)
+        last_codes = keep.tile([P, P], U32, name="last_codes", tag="slab_codes0", align_bytes=DMA_ALIGN)
+        plain(LAST, last_codes[:], later_scales[:, LAST[0]:LAST[1]])
         keep_larger(1, 0)
-        add_scores(OWN)
+        keep_larger(0, 1)
+        add_scores(SECOND)
         keep_larger(1, 1)
         turned = bank(0, "turned")
         for a in range(2):
             nc.tensor.transpose(turned[:, a * P:(a + 1) * P], kept[a][1][:], ident[:])
         add_scores(both)
-        largest(*OWN)
+        largest(*SECOND)
         largest(*both)
         nc.vector.tensor_reduce(out=result[:, 0:HALF // SEG].rearrange("p (a s) -> p a s", a=2),
                                 in_=turned[:, 0:2 * P].rearrange("p (a h s r) -> p a s h r", a=2, h=2, r=QUARTER),

@@ -26,8 +26,8 @@ VECTOR_PAGES = 80
 ROW = SEG + 8
 
 PAIR = 256
-SECOND, THIRD, LAST = (512, 768), (768, 896), (896, 1024)
-GATHERS = ((0, 128), (128, 256), (256, 768), (768, 1024))
+SECOND, OWN, THIRD, LAST = (256, 512), (512, 768), (768, 896), (896, 1024)
+GATHERS = ((0, 128), (128, 384), (384, 768), (768, 1024))
 
 FLOPS = 2 * D * NQ * N
 BYTES = 4 * (D * NQ + D * T + T + NQ + NQ * N // SEG) + 2 * P * N // 16
@@ -55,8 +55,8 @@ def tile_attend_xtr_f_kernel(tc, qT, kT, kb, im, offs, out):
         plane3 = keep.tile([P, T], F32, name="plane3", align_bytes=DMA_ALIGN)
         nc.scalar.dma_start(out=bias_pages[:], in_=kb[0].rearrange("(g i) -> g i", i=SEG))
         nc.scalar.dma_start(out=im_col[:], in_=im[0])
-        nc.sync.dma_start(offsets[:], offs)
         nc.sync.dma_start(out=planes01[:], in_=k_rows[:, 0:2, :])
+        nc.sync.dma_start(offsets[:], offs)
         nc.sync.dma_start(out=plane2[:], in_=k_rows[:, 2, :])
         nc.sync.dma_start(out=plane3[:], in_=k_rows[:, 3, :])
         nc.sync.dma_start(out=q_raw[:], in_=qT[0].rearrange("(p t) q -> p t q", t=PACK))
@@ -86,8 +86,8 @@ def tile_attend_xtr_f_kernel(tc, qT, kT, kb, im, offs, out):
         bias_used = keep.tile([P, 3 * P], F32, name="bias_used")
         by_passage = bias_gathered[:].rearrange("p (a s i) -> p a s i", a=4, i=SEG)[:, :, :, 0:QUARTER]
         nc.scalar.copy(out=bias_used[:, 0:2 * P].rearrange("p (a h s r) -> p a h s r", a=2, h=2, r=QUARTER),
-                       in_=by_passage[:, 0:2].unsqueeze(2).to_broadcast([P, 2, 2, 8, QUARTER]))
-        nc.scalar.copy(out=bias_used[:, 2 * P:].rearrange("p (a s r) -> p a s r", a=2, r=QUARTER), in_=by_passage[:, 2:4])
+                       in_=by_passage[:, 0:4:2].unsqueeze(2).to_broadcast([P, 2, 2, 8, QUARTER]))
+        nc.scalar.copy(out=bias_used[:, 2 * P:].rearrange("p (a s r) -> p a s r", a=2, r=QUARTER), in_=by_passage[:, 1:4:2])
         down = bank(2, "down")
         for h in range(3):
             nc.tensor.transpose(down[:, h * P:(h + 1) * P], bias_used[:, h * P:(h + 1) * P], ident[:])
@@ -103,13 +103,16 @@ def tile_attend_xtr_f_kernel(tc, qT, kT, kb, im, offs, out):
         nc.scalar.copy(out=im_row[:], in_=by_block[:, 3, :])
         rows = keep.tile([P, HALF // SEG, ROW], F32, name="rows", align_bytes=DMA_ALIGN)
 
+        def place(c):
+            return c - PAIR if c <= HALF else c - HALF
+
         def passages(c0, c1, width):
-            return rows[:, (c0 - HALF) // SEG:(c1 - HALF) // SEG, 0:width]
+            return rows[:, place(c0) // SEG:place(c1) // SEG, 0:width]
 
         along = bank(3, "along")
         for j in range(QUARTERS):
             nc.tensor.transpose(along[:, j * P:(j + 1) * P], bias_down[:, j:j + 1].to_broadcast([P, P]), ident[:])
-        nc.scalar.copy(out=passages(HALF, N, SEG).rearrange("p s (j r) -> p j s r", r=QUARTER),
+        nc.scalar.copy(out=rows[:, :, 0:SEG].rearrange("p s (j r) -> p j s r", r=QUARTER),
                        in_=along[:].rearrange("p (j s r) -> p j s r", j=QUARTERS, r=QUARTER))
         nc.gpsimd.tensor_copy(out=rows[:, :, SEG:SEG + 1], in_=im_col[:].unsqueeze(2).to_broadcast([P, HALF // SEG, 1]))
 
@@ -117,25 +120,25 @@ def tile_attend_xtr_f_kernel(tc, qT, kT, kb, im, offs, out):
         plain_words = keep.tile([P, HALF, PACK], BF16, name="plain_words", align_bytes=DMA_ALIGN)
 
         def deal(copy, c0, c1, t0, t1, gathered):
-            dealt = slab_words[c0 // PAIR][:].rearrange("p (j s r) t -> p s j r t", j=QUARTERS, r=QUARTER)
+            dealt = slab_words[c0 // HALF][:].rearrange("p (j s r) t -> p s j r t", j=QUARTERS, r=QUARTER)
             s0 = c0 % PAIR // SEG
             copy(out=dealt[:, s0:s0 + (c1 - c0) // SEG, :, :, t0:t1],
                  in_=gathered[:, :, c0:c1].rearrange("p t (s j r) -> p s j r t", j=QUARTERS, r=QUARTER))
 
         def interleave(copy, piece, t0, t1, gathered):
             c0, c1 = piece
-            copy(out=plain_words[:, c0 - HALF:c1 - HALF, t0:t1], in_=gathered[:, :, c0:c1].rearrange("p t c -> p c t"))
+            copy(out=plain_words[:, place(c0):place(c1), t0:t1], in_=gathered[:, :, c0:c1].rearrange("p t c -> p c t"))
 
         early = keep.tile([P, PACK - 1, N], F32, name="early", tag="staging")
         for c0 in (0, HALF):
             for t in range(2):
                 nc.vector.tensor_copy(out=early[:, t, c0:c0 + HALF], in_=listed(planes01[:, t, :], c0, c0 + HALF))
-        for c0 in (0, HALF):
+        for c0 in (HALF, 0):
             nc.vector.tensor_copy(out=early[:, 2, c0:c0 + HALF], in_=listed(plane2[:], c0, c0 + HALF))
-        deal(nc.vector.tensor_copy, PAIR, HALF, 0, PACK - 1, early)
+        deal(nc.vector.tensor_copy, OWN[0], OWN[1], 0, PACK - 1, early)
+        interleave(nc.vector.tensor_copy, (THIRD[0], N), 0, PACK - 1, early)
         deal(nc.scalar.copy, 0, PAIR, 0, PACK - 1, early)
-        interleave(nc.vector.tensor_copy, SECOND, 0, PACK - 1, early)
-        interleave(nc.scalar.copy, (THIRD[0], N), 0, PACK - 1, early)
+        interleave(nc.scalar.copy, SECOND, 0, PACK - 1, early)
 
         late = keep.tile([P, 1, N], BF16, name="late", align_bytes=DMA_ALIGN)
         for c0, c1 in GATHERS:
@@ -146,12 +149,12 @@ def tile_attend_xtr_f_kernel(tc, qT, kT, kb, im, offs, out):
         q_scales = keep.tile([P, NQ], U8, name="q_scales", align_bytes=MX_ALIGN)
         result = keep.tile([P, N // SEG], F32, name="result", align_bytes=DMA_ALIGN)
 
-        deal(nc.vector.tensor_copy, PAIR, HALF, PACK - 1, PACK, late)
+        deal(nc.vector.tensor_copy, OWN[0], OWN[1], PACK - 1, PACK, late)
         deal(nc.scalar.copy, 0, 128, PACK - 1, PACK, late)
         nc.gpsimd.tensor_scalar(out=q_words[:], in0=q_raw[:].rearrange("p t q -> p q t"),
                                 scalar1=1.0, scalar2=0.0, op0=ALU.mult, op1=ALU.add)
         deal(nc.scalar.copy, 128, 256, PACK - 1, PACK, late)
-        for piece in (SECOND, THIRD, LAST):
+        for piece in ((256, 384), (384, 512), THIRD, LAST):
             interleave(nc.scalar.copy, piece, PACK - 1, PACK, late)
 
         slab_codes = [keep.tile([P, PAIR], U32, name="slab_codes%d" % a, tag="slab_codes%d" % a, align_bytes=DMA_ALIGN)
@@ -173,7 +176,7 @@ def tile_attend_xtr_f_kernel(tc, qT, kT, kb, im, offs, out):
                                     rhs=q_codes[:].bitcast(FP8X4), rhs_scale=q_scales[:], start=True, stop=True)
 
         def plain(piece, codes, scales):
-            quantise(codes, scales, plain_words[:, piece[0] - HALF:piece[1] - HALF, :])
+            quantise(codes, scales, plain_words[:, place(piece[0]):place(piece[1]), :])
             nc.tensor.matmul_mx(out=scores[piece], lhsT=q_codes[:].bitcast(FP8X4), lhsT_scale=q_scales[:],
                                 rhs=codes.bitcast(FP8X4), rhs_scale=scales, start=True, stop=True)
 
@@ -195,8 +198,8 @@ def tile_attend_xtr_f_kernel(tc, qT, kT, kb, im, offs, out):
         quantise(q_codes[:], q_scales[:], q_words[:])
         slabs(0, first_scales[:])
         later_scales = keep.tile([P, N], U8, name="later_scales", tag="q_raw", align_bytes=DMA_ALIGN)
-        quantise(slab_codes[1][:], later_scales[:, PAIR:HALF], slab_words[1][:])
-        slabs(1, later_scales[:, PAIR:HALF])
+        quantise(slab_codes[1][:], later_scales[:, OWN[0]:OWN[1]], slab_words[1][:])
+        slabs(1, later_scales[:, OWN[0]:OWN[1]])
         second_codes = keep.tile([P, PAIR], U32, name="second_codes", align_bytes=DMA_ALIGN)
         plain(SECOND, second_codes[:], later_scales[:, SECOND[0]:SECOND[1]])
         third_codes = keep.tile([P, P], U32, name="third_codes", align_bytes=DMA_ALIGN)
@@ -214,7 +217,7 @@ def tile_attend_xtr_f_kernel(tc, qT, kT, kb, im, offs, out):
         add_scores(both)
         largest(*SECOND)
         largest(*both)
-        nc.vector.tensor_reduce(out=result[:, 0:HALF // SEG].rearrange("p (a s) -> p a s", a=2),
+        nc.vector.tensor_reduce(out=result[:].rearrange("p (a s) -> p a s", a=4)[:, 0:4:2],
                                 in_=turned[:, 0:2 * P].rearrange("p (a h s r) -> p a s h r", a=2, h=2, r=QUARTER),
                                 axis=AXES.XY, op=ALU.max)
         nc.sync.dma_start(out=out[0], in_=result[:])

@@ -159,7 +159,7 @@ def tile_attend_xtr_f_kernel(tc, qT, kT, kb, im, offs, out):
 
         slab_codes = [keep.tile([P, PAIR], U32, name="slab_codes%d" % a, tag="slab_codes%d" % a, align_bytes=DMA_ALIGN)
                       for a in range(2)]
-        slab_scores = [bank(4 + a, "slab_scores%d" % a) for a in range(2)]
+        slab_scores = [[bank(4 * (1 - j) + a, "slab_scores%d%d" % (a, j))[:, 0:NQ] for j in range(2)] for a in range(2)]
         both = (THIRD[0], LAST[1])
         runs = {both: bank(6, "scores_both")[:, 0:PAIR], SECOND: bank(7, "scores_second")[:, 0:PAIR]}
         scores = {THIRD: runs[both][:, 0:P], LAST: runs[both][:, P:], SECOND: runs[SECOND]}
@@ -170,7 +170,7 @@ def tile_attend_xtr_f_kernel(tc, qT, kT, kb, im, offs, out):
 
         def slabs(a, scales):
             for j in range(2):
-                nc.tensor.matmul_mx(out=slab_scores[a][:, j * NQ:(j + 1) * NQ],
+                nc.tensor.matmul_mx(out=slab_scores[a][j],
                                     lhsT=slab_codes[a][:, j * P:(j + 1) * P].bitcast(FP8X4),
                                     lhsT_scale=scales[:, j * P:(j + 1) * P],
                                     rhs=q_codes[:].bitcast(FP8X4), rhs_scale=q_scales[:], start=True, stop=True)
@@ -181,7 +181,7 @@ def tile_attend_xtr_f_kernel(tc, qT, kT, kb, im, offs, out):
                                 rhs=codes.bitcast(FP8X4), rhs_scale=scales, start=True, stop=True)
 
         def keep_larger(a, j):
-            nc.vector.scalar_tensor_tensor(out=kept[a][j][:], in0=slab_scores[a][:, j * NQ:(j + 1) * NQ],
+            nc.vector.scalar_tensor_tensor(out=kept[a][j][:], in0=slab_scores[a][j],
                                            scalar=slab_bias[:, a, j:j + 1], in1=kept[a][0][:] if j else im_row[:],
                                            op0=ALU.add, op1=ALU.max)
 
@@ -205,13 +205,12 @@ def tile_attend_xtr_f_kernel(tc, qT, kT, kb, im, offs, out):
         third_codes = keep.tile([P, P], U32, name="third_codes", align_bytes=DMA_ALIGN)
         plain(THIRD, third_codes[:], later_scales[:, THIRD[0]:THIRD[1]])
         keep_larger(0, 0)
-        last_codes = keep.tile([P, P], U32, name="last_codes", tag="slab_codes0", align_bytes=DMA_ALIGN)
-        plain(LAST, last_codes[:], later_scales[:, LAST[0]:LAST[1]])
+        plain(LAST, slab_codes[0][:, 0:P], later_scales[:, LAST[0]:LAST[1]])
         keep_larger(1, 0)
         keep_larger(0, 1)
         add_scores(SECOND)
         keep_larger(1, 1)
-        turned = bank(0, "turned")
+        turned = bank(4, "turned")
         for a in range(2):
             nc.tensor.transpose(turned[:, a * P:(a + 1) * P], kept[a][1][:], ident[:])
         add_scores(both)

from contextlib import ExitStack

import concourse.mybir as mybir
from concourse.masks import make_identity

F32 = mybir.dt.float32
BF16 = mybir.dt.bfloat16
U32 = mybir.dt.uint32
U16 = mybir.dt.uint16
U8 = mybir.dt.uint8
FP8X4 = mybir.dt.float8_e4m3fn_x4
ALU = mybir.AluOpType
ACT = mybir.ActivationFunctionType
AXES = mybir.AxisListType

P = 128
PACK = 4
D, NQ, T, N, SEG = 512, 128, 4096, 1024, 32
PER_COLUMN = 16
HALF = N // 2
BANK = 512
MX_ALIGN = 64
DMA_ALIGN = 256
QUARTERS, QUARTER = 4, 8
VECTOR_PAGES = 80
ROW = SEG + 8

PAIR = 256
SECOND, OWN, THIRD, LAST = (256, 512), (512, 768), (768, 896), (896, 1024)
GATHERS = ((0, 128), (128, 384), (384, 768), (768, 1024))

FLOPS = 2 * D * NQ * N
BYTES = 4 * (D * NQ + D * T + T + NQ + NQ * N // SEG) + 2 * P * N // 16


def tile_attend_xtr_f_kernel(tc, qT, kT, kb, im, offs, out):
    nc = tc.nc
    with ExitStack() as ctx:
        keep = ctx.enter_context(tc.tile_pool(name="keep", bufs=1))
        psum = ctx.enter_context(tc.psum_pool(name="psum", bufs=1))

        def bank(b, name):
            return psum.tile([P, BANK], F32, name=name, tag="bank%d" % b)

        def listed(window, c0, c1):
            return window.indirect(offsets[:, c0 // PER_COLUMN:c1 // PER_COLUMN])

        offsets = keep.tile([P, N // PER_COLUMN], U16, name="offsets")
        bias_pages = keep.tile([P, SEG], F32, name="bias_pages")
        q_raw = keep.tile([P, PACK, NQ], F32, name="q_raw", tag="q_raw", align_bytes=DMA_ALIGN)
        im_col = keep.tile([P, 1], F32, name="im_col")
        k_rows = kT.rearrange("(p t) w -> p t w", t=PACK)
        planes01 = keep.tile([P, 2, T], F32, name="planes01", align_bytes=DMA_ALIGN)
        plane2 = keep.tile([P, T], F32, name="plane2", align_bytes=DMA_ALIGN)
        plane3 = keep.tile([P, T], F32, name="plane3", align_bytes=DMA_ALIGN)
        nc.scalar.dma_start(out=bias_pages[:], in_=kb[0].rearrange("(g i) -> g i", i=SEG))
        nc.scalar.dma_start(out=im_col[:], in_=im[0])
        nc.sync.dma_start(out=planes01[:], in_=k_rows[:, 0:2, :])
        nc.sync.dma_start(offsets[:], offs)
        nc.sync.dma_start(out=plane2[:], in_=k_rows[:, 2, :])
        nc.sync.dma_start(out=plane3[:], in_=k_rows[:, 3, :])
        nc.sync.dma_start(out=q_raw[:], in_=qT[0].rearrange("(p t) q -> p t q", t=PACK))

        ident = keep.tile([P, P], F32, name="ident")
        make_identity(nc, ident[:])

        bias_window = keep.tile([P, T], F32, name="bias_window", tag="staging")
        bias_paged = bias_window[:].rearrange("p (g i) -> p g i", i=SEG)
        nc.gpsimd.memset(bias_paged[:, VECTOR_PAGES:, QUARTER:], 0.0)
        nc.vector.memset(bias_paged[:, 0:VECTOR_PAGES, QUARTER:], 0.0)
        bias_wide = keep.tile([P, P + SEG], F32, name="bias_wide")
        for c0 in range(0, P + SEG, SEG):
            nc.vector.tensor_copy(out=bias_wide[:, c0:c0 + SEG].rearrange("p (r j) -> p r j", j=QUARTERS),
                                  in_=bias_pages[:].rearrange("p (j r) -> p r j", j=QUARTERS))
        per_bank = BANK // P
        for b in range(QUARTER // per_bank):
            by_quarter = bank(b, "by_quarter%d" % b)
            for n in range(per_bank):
                c0 = (per_bank * b + n) * QUARTERS
                nc.tensor.transpose(by_quarter[:, n * P:(n + 1) * P], bias_wide[:, c0:c0 + P], ident[:])
            nc.scalar.activation(out=bias_paged[:, :, per_bank * b:per_bank * (b + 1)],
                                 in_=by_quarter[:].rearrange("p (r g) -> p g r", g=P), func=ACT.Copy)
        bias_gathered = keep.tile([P, N], F32, name="bias_gathered")
        nc.vector.tensor_copy(out=bias_gathered[:], in_=listed(bias_window[:], 0, N))

        bias_used = keep.tile([P, 3 * P], F32, name="bias_used")
        by_passage = bias_gathered[:].rearrange("p (a s i) -> p a s i", a=4, i=SEG)[:, :, :, 0:QUARTER]
        nc.scalar.copy(out=bias_used[:, 0:2 * P].rearrange("p (a h s r) -> p a h s r", a=2, h=2, r=QUARTER),
                       in_=by_passage[:, 0:4:2].unsqueeze(2).to_broadcast([P, 2, 2, 8, QUARTER]))
        nc.scalar.copy(out=bias_used[:, 2 * P:].rearrange("p (a s r) -> p a s r", a=2, r=QUARTER), in_=by_passage[:, 1:4:2])
        down = bank(2, "down")
        for h in range(3):
            nc.tensor.transpose(down[:, h * P:(h + 1) * P], bias_used[:, h * P:(h + 1) * P], ident[:])
        nc.tensor.transpose(down[:, 3 * P:], im_col[:].to_broadcast([P, P]), ident[:])
        by_block = down[:].rearrange("p (a n) -> p a n", a=4)
        slab_bias = keep.tile([P, 2, 2], F32, name="slab_bias")
        for h in range(2):
            part = slice(h * P // 2, (h + 1) * P // 2)
            nc.scalar.copy(out=slab_bias[part], in_=by_block[part, 0:2, h:QUARTERS:2])
        bias_down = keep.tile([P, QUARTERS], F32, name="bias_down")
        nc.scalar.copy(out=bias_down[:], in_=by_block[:, 2, 0:QUARTERS])
        im_row = keep.tile([P, NQ], F32, name="im_row", align_bytes=DMA_ALIGN)
        nc.scalar.copy(out=im_row[:], in_=by_block[:, 3, :])
        rows = keep.tile([P, HALF // SEG, ROW], F32, name="rows", align_bytes=DMA_ALIGN)

        def place(c):
            return c - PAIR if c <= HALF else c - HALF

        def passages(c0, c1, width):
            return rows[:, place(c0) // SEG:place(c1) // SEG, 0:width]

        along = bank(3, "along")
        for j in range(QUARTERS):
            nc.tensor.transpose(along[:, j * P:(j + 1) * P], bias_down[:, j:j + 1].to_broadcast([P, P]), ident[:])
        nc.scalar.copy(out=rows[:, :, 0:SEG].rearrange("p s (j r) -> p j s r", r=QUARTER),
                       in_=along[:].rearrange("p (j s r) -> p j s r", j=QUARTERS, r=QUARTER))
        nc.gpsimd.tensor_copy(out=rows[:, :, SEG:SEG + 1], in_=im_col[:].unsqueeze(2).to_broadcast([P, HALF // SEG, 1]))

        slab_words = [keep.tile([P, PAIR, PACK], BF16, name="slab_words%d" % a, align_bytes=DMA_ALIGN) for a in range(2)]
        plain_words = keep.tile([P, HALF, PACK], BF16, name="plain_words", align_bytes=DMA_ALIGN)

        def deal(copy, c0, c1, t0, t1, gathered):
            dealt = slab_words[c0 // HALF][:].rearrange("p (j s r) t -> p s j r t", j=QUARTERS, r=QUARTER)
            s0 = c0 % PAIR // SEG
            copy(out=dealt[:, s0:s0 + (c1 - c0) // SEG, :, :, t0:t1],
                 in_=gathered[:, :, c0:c1].rearrange("p t (s j r) -> p s j r t", j=QUARTERS, r=QUARTER))

        def interleave(copy, piece, t0, t1, gathered):
            c0, c1 = piece
            copy(out=plain_words[:, place(c0):place(c1), t0:t1], in_=gathered[:, :, c0:c1].rearrange("p t c -> p c t"))

        early = keep.tile([P, PACK - 1, N], F32, name="early", tag="staging")
        for c0 in (0, HALF):
            for t in range(2):
                nc.vector.tensor_copy(out=early[:, t, c0:c0 + HALF], in_=listed(planes01[:, t, :], c0, c0 + HALF))
        for c0 in (HALF, 0):
            nc.vector.tensor_copy(out=early[:, 2, c0:c0 + HALF], in_=listed(plane2[:], c0, c0 + HALF))
        deal(nc.vector.tensor_copy, OWN[0], OWN[1], 0, PACK - 1, early)
        interleave(nc.vector.tensor_copy, (THIRD[0], N), 0, PACK - 1, early)
        deal(nc.scalar.copy, 0, PAIR, 0, PACK - 1, early)
        interleave(nc.scalar.copy, SECOND, 0, PACK - 1, early)

        late = keep.tile([P, 1, N], BF16, name="late", align_bytes=DMA_ALIGN)
        for c0, c1 in GATHERS:
            nc.vector.tensor_copy(out=late[:, 0, c0:c1], in_=listed(plane3[:], c0, c1))

        q_words = keep.tile([P, NQ, PACK], BF16, name="q_words", align_bytes=DMA_ALIGN)
        q_codes = keep.tile([P, NQ], U32, name="q_codes", align_bytes=DMA_ALIGN)
        q_scales = keep.tile([P, NQ], U8, name="q_scales", align_bytes=MX_ALIGN)
        result = keep.tile([P, N // SEG], F32, name="result", align_bytes=DMA_ALIGN)

        deal(nc.vector.tensor_copy, OWN[0], OWN[1], PACK - 1, PACK, late)
        deal(nc.scalar.copy, 0, 128, PACK - 1, PACK, late)
        nc.gpsimd.tensor_scalar(out=q_words[:], in0=q_raw[:].rearrange("p t q -> p q t"),
                                scalar1=1.0, scalar2=0.0, op0=ALU.mult, op1=ALU.add)
        deal(nc.scalar.copy, 128, 256, PACK - 1, PACK, late)
        for piece in ((256, 384), (384, 512), THIRD, LAST):
            interleave(nc.scalar.copy, piece, PACK - 1, PACK, late)

        slab_codes = [keep.tile([P, PAIR], U32, name="slab_codes%d" % a, tag="slab_codes%d" % a, align_bytes=DMA_ALIGN)
                      for a in range(2)]
        slab_scores = [[bank(4 * (1 - j) + a, "slab_scores%d%d" % (a, j))[:, 0:NQ] for j in range(2)] for a in range(2)]
        both = (THIRD[0], LAST[1])
        runs = {both: bank(6, "scores_both")[:, 0:PAIR], SECOND: bank(7, "scores_second")[:, 0:PAIR]}
        scores = {THIRD: runs[both][:, 0:P], LAST: runs[both][:, P:], SECOND: runs[SECOND]}
        kept = [[keep.tile([P, NQ], F32, name="kept%d%d" % (a, j), align_bytes=DMA_ALIGN) for j in range(2)] for a in range(2)]

        def quantise(codes, scales, words):
            nc.vector.quantize_mx(out=codes.bitcast(FP8X4), scales=scales, in_=words.rearrange("p c t -> p (c t)"))

        def slabs(a, scales):
            for j in range(2):
                nc.tensor.matmul_mx(out=slab_scores[a][j],
                                    lhsT=slab_codes[a][:, j * P:(j + 1) * P].bitcast(FP8X4),
                                    lhsT_scale=scales[:, j * P:(j + 1) * P],
                                    rhs=q_codes[:].bitcast(FP8X4), rhs_scale=q_scales[:], start=True, stop=True)

        def plain(piece, codes, scales):
            quantise(codes, scales, plain_words[:, place(piece[0]):place(piece[1]), :])
            nc.tensor.matmul_mx(out=scores[piece], lhsT=q_codes[:].bitcast(FP8X4), lhsT_scale=q_scales[:],
                                rhs=codes.bitcast(FP8X4), rhs_scale=scales, start=True, stop=True)

        def keep_larger(a, j):
            nc.vector.scalar_tensor_tensor(out=kept[a][j][:], in0=slab_scores[a][j],
                                           scalar=slab_bias[:, a, j:j + 1], in1=kept[a][0][:] if j else im_row[:],
                                           op0=ALU.add, op1=ALU.max)

        def add_scores(run):
            sums = passages(run[0], run[1], SEG)
            nc.vector.tensor_tensor(out=sums, in0=runs[run].rearrange("p (s i) -> p s i", i=SEG), in1=sums, op=ALU.add)

        def largest(c0, c1):
            nc.vector.tensor_reduce(out=result[:, c0 // SEG:c1 // SEG], in_=passages(c0, c1, SEG + 1),
                                    axis=AXES.X, op=ALU.max)

        first_scales = keep.tile([P, PAIR], U8, name="first_scales", align_bytes=MX_ALIGN)
        quantise(slab_codes[0][:], first_scales[:], slab_words[0][:])
        quantise(q_codes[:], q_scales[:], q_words[:])
        slabs(0, first_scales[:])
        later_scales = keep.tile([P, N], U8, name="later_scales", tag="q_raw", align_bytes=DMA_ALIGN)
        quantise(slab_codes[1][:], later_scales[:, OWN[0]:OWN[1]], slab_words[1][:])
        slabs(1, later_scales[:, OWN[0]:OWN[1]])
        second_codes = keep.tile([P, PAIR], U32, name="second_codes", align_bytes=DMA_ALIGN)
        plain(SECOND, second_codes[:], later_scales[:, SECOND[0]:SECOND[1]])
        third_codes = keep.tile([P, P], U32, name="third_codes", align_bytes=DMA_ALIGN)
        plain(THIRD, third_codes[:], later_scales[:, THIRD[0]:THIRD[1]])
        keep_larger(0, 0)
        plain(LAST, slab_codes[0][:, 0:P], later_scales[:, LAST[0]:LAST[1]])
        keep_larger(1, 0)
        keep_larger(0, 1)
        add_scores(SECOND)
        keep_larger(1, 1)
        turned = bank(4, "turned")
        for a in range(2):
            nc.tensor.transpose(turned[:, a * P:(a + 1) * P], kept[a][1][:], ident[:])
        add_scores(both)
        largest(*SECOND)
        largest(*both)
        nc.vector.tensor_reduce(out=result[:].rearrange("p (a s) -> p a s", a=4)[:, 0:4:2],
                                in_=turned[:, 0:2 * P].rearrange("p (a h s r) -> p a s h r", a=2, h=2, r=QUARTER),
                                axis=AXES.XY, op=ALU.max)
        nc.sync.dma_start(out=out[0], in_=result[:])
